import numpy as np
import ml_dtypes


def mxq(x, axis, fmt="e4m3"):
    dtype, down = {"e4m3": (ml_dtypes.float8_e4m3fn, 7), "e5m2": (ml_dtypes.float8_e5m2, 14)}[fmt]
    v = np.moveaxis(np.asarray(x, np.float32).astype(ml_dtypes.bfloat16).astype(np.float64), axis, -1)
    blocks = v.reshape(v.shape[:-1] + (-1, 32))
    amax = np.abs(blocks).max(-1, keepdims=True)
    byte = np.maximum(np.where(amax > 0, np.frexp(amax)[1] - 1 + 127, 0) - down, 1)
    scale = np.exp2(byte - 127.0)
    codes = (blocks / scale).astype(np.float32).astype(dtype).astype(np.float64)
    return np.moveaxis((codes * scale).reshape(v.shape), -1, axis)


WIDE = False


def mx_kscale(k):
    if not WIDE:
        return np.ones(k)
    levels = np.array([10, -10, 5, -5, 0])
    if k % 512:
        return np.exp2(np.random.permutation(np.resize(levels, k // 32))).repeat(32)
    a = np.empty((k // 512, 16))
    for p in range(k // 512):
        a[p, :8] = np.random.permutation(np.resize(levels, 8))
        for g in range(8):
            far = levels[np.abs(levels - a[p, g]) >= 10]
            a[p, g + 8] = far[np.random.randint(len(far))]
    return np.exp2(a.ravel()).repeat(32)


def f64(x):
    return np.asarray(x).astype(np.float64)


def striped(idx):
    return np.tile(idx.reshape(-1, 16).T, (8, 1)).astype(np.uint16)


def unstriped(offs):
    return offs[:16].T.reshape(-1).astype(np.int64)


E2M1 = np.array([0.0, 0.5, 1.0, 1.5, 2.0, 3.0, 4.0, 6.0, -0.0, -0.5, -1.0, -1.5, -2.0, -3.0, -4.0, -6.0])


def pack_weight(w, fmt):
    k, n = w.shape
    w = f64(np.asarray(w, np.float32).astype(ml_dtypes.bfloat16)).reshape(k // 32, 32, n)
    amax = np.abs(w).max(1)
    if fmt == "e4m3":
        byte = np.frexp(amax)[1] - 1 + 127 - 7
    else:
        mant, ex = np.frexp(amax / 6.0)
        byte = np.where(mant > 0.5, ex, ex - 1) + 127
    byte = np.clip(np.where(amax > 0, byte, 1), 1, 254)
    scaled = (w * np.exp2(127.0 - byte)[:, None, :]).reshape(k, n).astype(np.float32)
    by_word = np.ascontiguousarray(scaled.reshape(k // 512, 128, 4, n).transpose(0, 1, 3, 2))
    if fmt == "e4m3":
        words = by_word.astype(ml_dtypes.float8_e4m3fn).view(np.uint8)
    else:
        c = by_word.astype(ml_dtypes.float4_e2m1fn).view(np.uint8) & 0xF
        words = (c[..., 0::2] | (c[..., 1::2] << 4)).reshape(k // 512, 128, 2 * n)
    return np.ascontiguousarray(words), np.ascontiguousarray(byte.astype(np.uint8).reshape(k // 512, 16, n))


def unpack_weight(words, scales, fmt):
    g, _, n = scales.shape
    words = np.ascontiguousarray(words).reshape(g, 128, n, -1)
    if fmt == "e4m3":
        vals = words.view(ml_dtypes.float8_e4m3fn).astype(np.float64)
    else:
        nib = np.empty((g, 128, n, 4), np.uint8)
        nib[..., 0::2] = words & 0xF
        nib[..., 1::2] = words >> 4
        vals = E2M1[nib]
    vals = vals * np.repeat(np.exp2(scales.astype(np.float64) - 127.0), 8, axis=1)[..., None]
    return vals.transpose(0, 1, 3, 2).reshape(g * 512, n)


def relu(v):
    return np.maximum(v, 0.0)


K, T, E, C, H, N = 1024, 1536, 4, 256, 512, 512


def by_expert(wq, xq):
    return np.concatenate([wq[e].T @ xq[:, e * C:(e + 1) * C] for e in range(E)], axis=1)


def setup_inputs():
    n = np.random.standard_normal
    s = mx_kscale(K)[:, None]
    u = mx_kscale(H)
    x = pack_weight(n((K, T)) * s, "e4m3")
    return {
        "x_words": x[0],
        "x_scales": x[1],
        "w1": (n((E, K, H)) / np.sqrt(K) / s[None]).astype(np.float32),
        "w3": (n((E, K, H)) / np.sqrt(K) / s[None] * u[None, None, :]).astype(np.float32),
        "w2": (n((E, H, N)) / np.sqrt(H) / u[None, :, None]).astype(np.float32),
        "gate": np.tile(np.random.uniform(0.2, 1.0, E * C), (N, 1)).astype(np.float32),
        "offs": striped(np.random.permutation(T)[:E * C]),
        "dst": striped(np.random.permutation(T)[:E * C]),
    }


def reference(x_words, x_scales, w1, w3, w2, gate, offs, dst):
    idx = unstriped(offs)
    xq = unpack_weight(x_words, x_scales, "e4m3")[:, idx]
    h = relu(by_expert(mxq(f64(w1), 1, "e4m3"), xq))
    h = h * by_expert(mxq(f64(w3), 1, "e4m3"), xq)
    y = by_expert(mxq(f64(w2), 1, "e4m3"), mxq(h, 0, "e4m3"))
    out = np.zeros((N, T))
    out[:, unstriped(dst)] = f64(gate) * y
    return out

@@ -1,0 +1,219 @@
+from contextlib import ExitStack
+
+import concourse.mybir as mybir
+
+K, T, E, C, H, N = 1024, 1536, 4, 256, 512, 512
+S = E * C
+FLOPS = 2 * S * (2 * K * H + H * N)
+
+F32 = mybir.dt.float32
+BF16 = mybir.dt.bfloat16
+I32 = mybir.dt.int32
+U32 = mybir.dt.uint32
+U16 = mybir.dt.uint16
+U8 = mybir.dt.uint8
+FP8X4 = mybir.dt.float8_e4m3fn_x4
+ALU = mybir.AluOpType
+
+P = 128
+PACK = 4
+K_PASS = P * PACK
+PASSES = K // K_PASS
+HALF = 128
+HALVES = C // HALF
+BLOCKS = N // P
+LIST_COLS = C // 16
+Y_AT = PACK * C
+VECTOR_SHARE = [(0, 0, 0, 64, 64), (64, 0, 0, 32, 32), (48, 16, 16, 0, 0), (48, 16, 16, 48, 0)]
+
+
+def tile_moe_two_glu_relu_kernel(
+    tc, x_words, x_scales, w1, w3, w2, gate, offs, dst, out
+):
+    nc = tc.nc
+
+    with ExitStack() as ctx:
+        keep = ctx.enter_context(tc.tile_pool(name="keep", bufs=1))
+        raws = ctx.enter_context(tc.tile_pool(name="raws", bufs=12))
+        rounded = ctx.enter_context(tc.tile_pool(name="rounded", bufs=4))
+        coded = ctx.enter_context(tc.tile_pool(name="coded", bufs=8))
+        hidden = ctx.enter_context(tc.tile_pool(name="hidden", bufs=2))
+        psum_a = ctx.enter_context(tc.psum_pool(name="psum_a", bufs=2))
+        psum_b = ctx.enter_context(tc.psum_pool(name="psum_b", bufs=2))
+        psum_y = ctx.enter_context(tc.psum_pool(name="psum_y", bufs=4))
+
+        offs_sb = keep.tile([P, S // 16], U16, name="offs_sb")
+        dst_sb = keep.tile([P, S // 16], U16, name="dst_sb")
+        token_words = [keep.tile([P, T], I32, name=f"token_words{o}") for o in range(PASSES)]
+        token_scales = keep.tile([P, T], U8, name="token_scales")
+        slot_words = [keep.tile([P, S], U32, name=f"slot_words{o}", align_bytes=64) for o in range(PASSES)]
+        slot_scales = keep.tile([P, S], U8, name="slot_scales", align_bytes=64)
+        gates = [keep.tile([P, BLOCKS, C], F32, name=f"gate{e}") for e in range(E)]
+        windows = [keep.tile([P, T], F32, name=f"window{b}") for b in range(BLOCKS)]
+
+        def load(rows):
+            raw = raws.tile([P, PACK, H], F32, name="raw")
+            nc.sync.dma_start(out=raw[:], in_=rows.rearrange("(p j) c -> p j c", j=PACK))
+            return raw
+
+        def quantize(raw, permute, vector_share, calls):
+            grouped = rounded.tile([P, PACK * H], BF16, name="grouped", align_bytes=64)
+            if permute:
+                src = raw[:].rearrange("p j (m t) -> p m j t", t=4)
+                into = grouped[:].rearrange("p (t m j) -> p m j t", t=4, j=PACK)
+            else:
+                src = raw[:].rearrange("p j (m t) -> p m j t", t=4)
+                into = grouped[:].rearrange("p (m t j) -> p m j t", t=4, j=PACK)
+            cut = P - vector_share
+            if cut > 0:
+                nc.scalar.copy(out=into[:, :cut], in_=src[:, :cut])
+            if vector_share > 0:
+                nc.vector.tensor_copy(out=into[:, cut:], in_=src[:, cut:])
+            codes = coded.tile([P, H], U32, name="codes", align_bytes=64)
+            scales = coded.tile([P, H], U8, name="scales", align_bytes=64)
+            width = H // calls
+            for q in range(calls):
+                cols = slice(q * width, (q + 1) * width)
+                nc.vector.quantize_mx(
+                    out=codes[:, cols].bitcast(FP8X4),
+                    scales=scales[:, cols],
+                    in_=grouped[:, PACK * q * width : PACK * (q + 1) * width],
+                )
+            return codes, scales
+
+        def first_layer(e, pool, operands):
+            banks = [pool.tile([P, PACK, HALF], F32, name="bank") for half in range(HALVES)]
+            for t in range(PACK):
+                cols = slice(t * P, (t + 1) * P)
+                for half in range(HALVES):
+                    slots = slice(e * C + half * HALF, e * C + (half + 1) * HALF)
+                    for o in range(PASSES):
+                        codes, scales = operands[o]
+                        nc.tensor.matmul_mx(
+                            out=banks[half][:, t, :],
+                            lhsT=codes[:, cols].bitcast(FP8X4),
+                            lhsT_scale=scales[:, cols],
+                            rhs=slot_words[o][:, slots].bitcast(FP8X4),
+                            rhs_scale=slot_scales[4 * o :, slots],
+                            start=(o == 0),
+                            stop=(o == PASSES - 1),
+                        )
+            return banks
+
+        nc.vector.memset(token_scales[:].bitcast(I32), 0)
+        for b in range(BLOCKS):
+            nc.vector.memset(windows[b][:], 0.0)
+
+        def flat(raw):
+            return raw[:].rearrange("p j c -> p (j c)")
+
+        def put_back(e, b, bank, raw):
+            y = flat(raw)[:, Y_AT : Y_AT + C]
+            nc.scalar.copy(out=y, in_=bank[:])
+            nc.vector.tensor_tensor(
+                windows[b][:].indirect(dst_sb[:, e * LIST_COLS : (e + 1) * LIST_COLS]),
+                y,
+                gates[e][:, b, :],
+                ALU.mult,
+            )
+            if e == E - 1:
+                nc.sync.dma_start(out=out[b * P : (b + 1) * P, :], in_=windows[b][:])
+
+        def copy_b(banks, raw):
+            b_sb = flat(raw)[:, : PACK * C].rearrange("p (u s t) -> p u s t", u=HALVES, t=PACK)
+            for half in range(HALVES):
+                nc.scalar.copy(out=b_sb[:, half], in_=banks[half][:].rearrange("p t s -> p s t"))
+            return b_sb
+
+        banks_y = []
+        pending = []
+        for e in range(E):
+            first, last = e == 0, e == E - 1
+            raw3 = [load(w3[e, 0:K_PASS, :])]
+            if first:
+                for q in range(4):
+                    nc.sync.dma_start(
+                        out=token_scales[32 * q : 32 * q + 4 * PASSES, :].bitcast(I32),
+                        in_=x_scales[:, 4 * q : 4 * q + 4, :].bitcast(I32),
+                    )
+                nc.sync.dma_start(offs_sb[:], offs)
+                for o in range(PASSES):
+                    nc.sync.dma_start(
+                        out=token_words[o][:],
+                        in_=x_words[o].rearrange("p t r -> p (t r)").bitcast(I32),
+                    )
+            raw3.append(load(w3[e, K_PASS:K, :]))
+            raw1 = [load(w1[e, o * K_PASS : (o + 1) * K_PASS, :]) for o in range(PASSES)]
+            raw2 = load(w2[e])
+            nc.sync.dma_start(
+                out=gates[e][:], in_=gate[:, e * C : (e + 1) * C].rearrange("(b p) s -> p b s", p=P)
+            )
+            if first:
+                nc.sync.dma_start(dst_sb[:], dst)
+                nc.vector.tensor_copy(slot_scales[:], token_scales[:].indirect(offs_sb[:]))
+                for o in range(PASSES):
+                    nc.vector.tensor_copy(slot_words[o][:], token_words[o][:].bitcast(U32).indirect(offs_sb[:]))
+
+            share = VECTOR_SHARE[e]
+            hosts = [raw3[0], raw3[1], raw1[0], raw1[1]]
+
+            def drain(i):
+                if i < len(pending):
+                    put_back(e - 1, pending[i], banks_y[pending[i]], hosts[i])
+
+            q3 = [quantize(raw3[0], True, share[0], 1)]
+            drain(0)
+            q3.append(quantize(raw3[1], True, share[1], 1))
+            banks_b = first_layer(e, psum_b, q3)
+            drain(1)
+            q1 = [quantize(raw1[0], True, share[2], 1)]
+            drain(2)
+            if first or last:
+                b_sb = copy_b(banks_b, raw1[0])
+            q1.append(quantize(raw1[1], True, share[3], PACK))
+            banks_a = first_layer(e, psum_a, q1)
+            drain(3)
+            if not (first or last):
+                b_sb = copy_b(banks_b, raw1[1])
+            h = hidden.tile([P, HALVES, HALF, PACK], BF16, name="h", align_bytes=64)
+            for half in range(HALVES):
+                nc.vector.scalar_tensor_tensor(
+                    out=h[:, half],
+                    in0=banks_a[half][:].rearrange("p t s -> p s t"),
+                    scalar=0.0,
+                    in1=b_sb[:, half],
+                    op0=ALU.max,
+                    op1=ALU.mult,
+                )
+            h_codes = hidden.tile([P, C], U32, name="h_codes", align_bytes=64)
+            h_scales = hidden.tile([P, C], U8, name="h_scales", align_bytes=64)
+            for half in range(HALVES):
+                cols = slice(half * HALF, (half + 1) * HALF)
+                nc.vector.quantize_mx(
+                    out=h_codes[:, cols].bitcast(FP8X4),
+                    scales=h_scales[:, cols],
+                    in_=h[:, half].rearrange("p s t -> p (s t)"),
+                )
+
+            codes2, scales2 = quantize(raw2, False, share[4], 1)
+            banks_y = []
+            for b in range(BLOCKS):
+                cols = slice(b * P, (b + 1) * P)
+                bank_y = psum_y.tile([P, C], F32, name="bank_y")
+                nc.tensor.matmul_mx(
+                    out=bank_y[:],
+                    lhsT=codes2[:, cols].bitcast(FP8X4),
+                    lhsT_scale=scales2[:, cols],
+                    rhs=h_codes[:].bitcast(FP8X4),
+                    rhs_scale=h_scales[:],
+                    start=True,
+                    stop=True,
+                )
+                banks_y.append(bank_y)
+            pending = list(range(BLOCKS))
+            if first:
+                put_back(e, pending[0], banks_y[0], raw2)
+                pending = pending[1:]
+
+        for b in pending:
+            put_back(E - 1, b, banks_y[b], [raw2, raw3[0], raw3[1], raw1[0]][b])

@@ -24,7 +24,9 @@ HALVES = C // HALF
 BLOCKS = N // P
 LIST_COLS = C // 16
 Y_AT = PACK * C
-VECTOR_SHARE = [(0, 0, 0, 64, 64), (64, 0, 0, 32, 32), (48, 16, 16, 0, 0), (48, 16, 16, 48, 0)]
+VECTOR_SHARE = [[64,48,64,64,0],[96,32,64,0,64],[16,16,0,32,64],[0,96,0,0,0]]
+PUT_BACK_AFTER = [[0,2,2,3],[1,1,2,4],[2,2,3,4]]
+PLAN = [[3,0,1],[3,0,1],[1,1,1],[3,0,1]]
 
 
 def tile_moe_two_glu_relu_kernel(
@@ -100,15 +102,27 @@ def tile_moe_two_glu_relu_kernel(
                         )
             return banks
 
-        nc.vector.memset(token_scales[:].bitcast(I32), 0)
-        for b in range(BLOCKS):
-            nc.vector.memset(windows[b][:], 0.0)
+        nc.gpsimd.memset(token_scales[:].bitcast(I32), 0)
+        for q in range(4):
+            nc.sync.dma_start(
+                out=token_scales[32 * q : 32 * q + 4 * PASSES, :].bitcast(I32),
+                in_=x_scales[:, 4 * q : 4 * q + 4, :].bitcast(I32),
+            )
+        nc.vector.memset(windows[0][:], 0.0)
+        for b in range(1, BLOCKS):
+            nc.scalar.copy(out=windows[b][:], in_=windows[0][:])
+        nc.sync.dma_start(offs_sb[:], offs)
+        for o in range(PASSES):
+            nc.sync.dma_start(
+                out=token_words[o][:],
+                in_=x_words[o].rearrange("p t r -> p (t r)").bitcast(I32),
+            )
 
         def flat(raw):
             return raw[:].rearrange("p j c -> p (j c)")
 
         def put_back(e, b, bank, raw):
-            y = flat(raw)[:, Y_AT : Y_AT + C]
+            y = flat(raw)[:, Y_AT + b * C : Y_AT + (b + 1) * C]
             nc.scalar.copy(out=y, in_=bank[:])
             nc.vector.tensor_tensor(
                 windows[b][:].indirect(dst_sb[:, e * LIST_COLS : (e + 1) * LIST_COLS]),
@@ -125,56 +139,7 @@ def tile_moe_two_glu_relu_kernel(
                 nc.scalar.copy(out=b_sb[:, half], in_=banks[half][:].rearrange("p t s -> p s t"))
             return b_sb
 
-        banks_y = []
-        pending = []
-        for e in range(E):
-            first, last = e == 0, e == E - 1
-            raw3 = [load(w3[e, 0:K_PASS, :])]
-            if first:
-                for q in range(4):
-                    nc.sync.dma_start(
-                        out=token_scales[32 * q : 32 * q + 4 * PASSES, :].bitcast(I32),
-                        in_=x_scales[:, 4 * q : 4 * q + 4, :].bitcast(I32),
-                    )
-                nc.sync.dma_start(offs_sb[:], offs)
-                for o in range(PASSES):
-                    nc.sync.dma_start(
-                        out=token_words[o][:],
-                        in_=x_words[o].rearrange("p t r -> p (t r)").bitcast(I32),
-                    )
-            raw3.append(load(w3[e, K_PASS:K, :]))
-            raw1 = [load(w1[e, o * K_PASS : (o + 1) * K_PASS, :]) for o in range(PASSES)]
-            raw2 = load(w2[e])
-            nc.sync.dma_start(
-                out=gates[e][:], in_=gate[:, e * C : (e + 1) * C].rearrange("(b p) s -> p b s", p=P)
-            )
-            if first:
-                nc.sync.dma_start(dst_sb[:], dst)
-                nc.vector.tensor_copy(slot_scales[:], token_scales[:].indirect(offs_sb[:]))
-                for o in range(PASSES):
-                    nc.vector.tensor_copy(slot_words[o][:], token_words[o][:].bitcast(U32).indirect(offs_sb[:]))
-
-            share = VECTOR_SHARE[e]
-            hosts = [raw3[0], raw3[1], raw1[0], raw1[1]]
-
-            def drain(i):
-                if i < len(pending):
-                    put_back(e - 1, pending[i], banks_y[pending[i]], hosts[i])
-
-            q3 = [quantize(raw3[0], True, share[0], 1)]
-            drain(0)
-            q3.append(quantize(raw3[1], True, share[1], 1))
-            banks_b = first_layer(e, psum_b, q3)
-            drain(1)
-            q1 = [quantize(raw1[0], True, share[2], 1)]
-            drain(2)
-            if first or last:
-                b_sb = copy_b(banks_b, raw1[0])
-            q1.append(quantize(raw1[1], True, share[3], PACK))
-            banks_a = first_layer(e, psum_a, q1)
-            drain(3)
-            if not (first or last):
-                b_sb = copy_b(banks_b, raw1[1])
+        def hidden_layer(banks_a, b_sb):
             h = hidden.tile([P, HALVES, HALF, PACK], BF16, name="h", align_bytes=64)
             for half in range(HALVES):
                 nc.vector.scalar_tensor_tensor(
@@ -194,8 +159,47 @@ def tile_moe_two_glu_relu_kernel(
                     scales=h_scales[:, cols],
                     in_=h[:, half].rearrange("p s t -> p (s t)"),
                 )
+            return h_codes, h_scales
 
-            codes2, scales2 = quantize(raw2, False, share[4], 1)
+        banks_y = []
+        for e in range(E):
+            b_after, w2_early, split = PLAN[e]
+            order = ["3a", "3b", "1a", "2", "1b"] if w2_early else ["3a", "3b", "1a", "1b", "2"]
+            rows = {
+                "3a": w3[e, :K_PASS, :],
+                "3b": w3[e, K_PASS:, :],
+                "1a": w1[e, :K_PASS, :],
+                "1b": w1[e, K_PASS:, :],
+                "2": w2[e],
+            }
+            hosts = [load(rows[n]) for n in order]
+            nc.sync.dma_start(
+                out=gates[e][:], in_=gate[:, e * C : (e + 1) * C].rearrange("(b p) s -> p b s", p=P)
+            )
+            if e == 0:
+                nc.sync.dma_start(dst_sb[:], dst)
+            slots = slice(e * C, (e + 1) * C)
+            picks = offs_sb[:, e * LIST_COLS : (e + 1) * LIST_COLS]
+            nc.vector.tensor_copy(slot_scales[:, slots], token_scales[:].indirect(picks))
+            for o in range(PASSES):
+                nc.vector.tensor_copy(slot_words[o][:, slots], token_words[o][:].bitcast(U32).indirect(picks))
+
+            share = VECTOR_SHARE[e]
+            done = {}
+            for i, n in enumerate(order):
+                done[n] = quantize(hosts[i], n != "2", share[i], split if n == "1b" else 1)
+                if n == "3b":
+                    banks_b = first_layer(e, psum_b, [done["3a"], done["3b"]])
+                if n == "1b":
+                    banks_a = first_layer(e, psum_a, [done["1a"], done["1b"]])
+                for b in range(BLOCKS):
+                    if e > 0 and PUT_BACK_AFTER[e - 1][b] == i:
+                        put_back(e - 1, b, banks_y[b], hosts[i])
+                if i == b_after:
+                    b_sb = copy_b(banks_b, hosts[i])
+                if i == max(b_after, order.index("1b")):
+                    h_codes, h_scales = hidden_layer(banks_a, b_sb)
+            codes2, scales2 = done["2"]
             banks_y = []
             for b in range(BLOCKS):
                 cols = slice(b * P, (b + 1) * P)
@@ -210,10 +214,6 @@ def tile_moe_two_glu_relu_kernel(
                     stop=True,
                 )
                 banks_y.append(bank_y)
-            pending = list(range(BLOCKS))
-            if first:
-                put_back(e, pending[0], banks_y[0], raw2)
-                pending = pending[1:]
-
-        for b in pending:
-            put_back(E - 1, b, banks_y[b], [raw2, raw3[0], raw3[1], raw1[0]][b])
+            for b in range(BLOCKS):
+                if e == E - 1 or PUT_BACK_AFTER[e][b] < 0:
+                    put_back(e, b, banks_y[b], hosts[-1])

@@ -24,9 +24,9 @@ HALVES = C // HALF
 BLOCKS = N // P
 LIST_COLS = C // 16
 Y_AT = PACK * C
-VECTOR_SHARE = [[64,48,64,64,0],[96,32,64,0,64],[16,16,0,32,64],[0,96,0,0,0]]
-PUT_BACK_AFTER = [[0,2,2,3],[1,1,2,4],[2,2,3,4]]
-PLAN = [[3,0,1],[3,0,1],[1,1,1],[3,0,1]]
+VECTOR_SHARE = [[64,16,16,48,48],[32,16,32,0,96],[16,0,32,64,0],[16,0,32,0,0]]
+PUT_BACK_AFTER = [[0,2,2,3],[1,2,2,4],[1,1,3,4]]
+PLAN = [[4,0,4],[3,0,1],[1,1,1],[3,0,1]]
 
 
 def tile_moe_two_glu_relu_kernel(
@@ -37,7 +37,7 @@ def tile_moe_two_glu_relu_kernel(
     with ExitStack() as ctx:
         keep = ctx.enter_context(tc.tile_pool(name="keep", bufs=1))
         raws = ctx.enter_context(tc.tile_pool(name="raws", bufs=12))
-        rounded = ctx.enter_context(tc.tile_pool(name="rounded", bufs=4))
+        rounded = ctx.enter_context(tc.tile_pool(name="rounded", bufs=3))
         coded = ctx.enter_context(tc.tile_pool(name="coded", bufs=8))
         hidden = ctx.enter_context(tc.tile_pool(name="hidden", bufs=2))
         psum_a = ctx.enter_context(tc.psum_pool(name="psum_a", bufs=2))
@@ -102,12 +102,7 @@ def tile_moe_two_glu_relu_kernel(
                         )
             return banks
 
-        nc.gpsimd.memset(token_scales[:].bitcast(I32), 0)
-        for q in range(4):
-            nc.sync.dma_start(
-                out=token_scales[32 * q : 32 * q + 4 * PASSES, :].bitcast(I32),
-                in_=x_scales[:, 4 * q : 4 * q + 4, :].bitcast(I32),
-            )
+        nc.vector.memset(token_scales[:].bitcast(I32), 0)
         nc.vector.memset(windows[0][:], 0.0)
         for b in range(1, BLOCKS):
             nc.scalar.copy(out=windows[b][:], in_=windows[0][:])
@@ -172,7 +167,14 @@ def tile_moe_two_glu_relu_kernel(
                 "1b": w1[e, K_PASS:, :],
                 "2": w2[e],
             }
-            hosts = [load(rows[n]) for n in order]
+            hosts = [load(rows[order[0]])]
+            if e == 0:
+                for q in range(4):
+                    nc.sync.dma_start(
+                        out=token_scales[32 * q : 32 * q + 4 * PASSES, :].bitcast(I32),
+                        in_=x_scales[:, 4 * q : 4 * q + 4, :].bitcast(I32),
+                    )
+            hosts.extend([load(rows[n]) for n in order[1:]])
             nc.sync.dma_start(
                 out=gates[e][:], in_=gate[:, e * C : (e + 1) * C].rearrange("(b p) s -> p b s", p=P)
             )

@@ -24,9 +24,9 @@ HALVES = C // HALF
 BLOCKS = N // P
 LIST_COLS = C // 16
 Y_AT = PACK * C
-VECTOR_SHARE = [[64,16,16,48,48],[32,16,32,0,96],[16,0,32,64,0],[16,0,32,0,0]]
-PUT_BACK_AFTER = [[0,2,2,3],[1,2,2,4],[1,1,3,4]]
-PLAN = [[4,0,4],[3,0,1],[1,1,1],[3,0,1]]
+VECTOR_SHARE = [[32,64,48,64,16],[0,0,0,0,32],[0,0,0,0,0],[0,0,0,0,0]]
+PUT_BACK_AFTER = [[-1,-1,0,2],[-1,-1,1,3],[-1,-1,1,3]]
+PLAN = [[3,0,4],[4,0,1],[3,0,1],[3,0,1]]
 
 
 def tile_moe_two_glu_relu_kernel(
@@ -37,7 +37,7 @@ def tile_moe_two_glu_relu_kernel(
     with ExitStack() as ctx:
         keep = ctx.enter_context(tc.tile_pool(name="keep", bufs=1))
         raws = ctx.enter_context(tc.tile_pool(name="raws", bufs=12))
-        rounded = ctx.enter_context(tc.tile_pool(name="rounded", bufs=3))
+        rounded = ctx.enter_context(tc.tile_pool(name="rounded", bufs=4))
         coded = ctx.enter_context(tc.tile_pool(name="coded", bufs=8))
         hidden = ctx.enter_context(tc.tile_pool(name="hidden", bufs=2))
         psum_a = ctx.enter_context(tc.psum_pool(name="psum_a", bufs=2))
@@ -58,7 +58,7 @@ def tile_moe_two_glu_relu_kernel(
             nc.sync.dma_start(out=raw[:], in_=rows.rearrange("(p j) c -> p j c", j=PACK))
             return raw
 
-        def quantize(raw, permute, vector_share, calls):
+        def round_bf16(raw, permute, vector_share):
             grouped = rounded.tile([P, PACK * H], BF16, name="grouped", align_bytes=64)
             if permute:
                 src = raw[:].rearrange("p j (m t) -> p m j t", t=4)
@@ -71,6 +71,9 @@ def tile_moe_two_glu_relu_kernel(
                 nc.scalar.copy(out=into[:, :cut], in_=src[:, :cut])
             if vector_share > 0:
                 nc.vector.tensor_copy(out=into[:, cut:], in_=src[:, cut:])
+            return grouped
+
+        def quantize(grouped, calls):
             codes = coded.tile([P, H], U32, name="codes", align_bytes=64)
             scales = coded.tile([P, H], U8, name="scales", align_bytes=64)
             width = H // calls
@@ -116,15 +119,13 @@ def tile_moe_two_glu_relu_kernel(
         def flat(raw):
             return raw[:].rearrange("p j c -> p (j c)")
 
-        def put_back(e, b, bank, raw):
+        def weigh(e, b, bank, raw):
             y = flat(raw)[:, Y_AT + b * C : Y_AT + (b + 1) * C]
-            nc.scalar.copy(out=y, in_=bank[:])
-            nc.vector.tensor_tensor(
-                windows[b][:].indirect(dst_sb[:, e * LIST_COLS : (e + 1) * LIST_COLS]),
-                y,
-                gates[e][:, b, :],
-                ALU.mult,
-            )
+            nc.vector.tensor_tensor(y, bank[:], gates[e][:, b, :], ALU.mult)
+            return y
+
+        def put_back(e, b, y):
+            nc.vector.tensor_copy(windows[b][:].indirect(dst_sb[:, e * LIST_COLS : (e + 1) * LIST_COLS]), y)
             if e == E - 1:
                 nc.sync.dma_start(out=out[b * P : (b + 1) * P, :], in_=windows[b][:])
 
@@ -189,14 +190,16 @@ def tile_moe_two_glu_relu_kernel(
             share = VECTOR_SHARE[e]
             done = {}
             for i, n in enumerate(order):
-                done[n] = quantize(hosts[i], n != "2", share[i], split if n == "1b" else 1)
+                grouped = round_bf16(hosts[i], n != "2", share[i])
+                due = [b for b in range(BLOCKS) if e > 0 and PUT_BACK_AFTER[e - 1][b] == i]
+                ys = [weigh(e - 1, b, banks_y[b], hosts[i]) for b in due]
+                done[n] = quantize(grouped, split if n == "1b" else 1)
                 if n == "3b":
                     banks_b = first_layer(e, psum_b, [done["3a"], done["3b"]])
                 if n == "1b":
                     banks_a = first_layer(e, psum_a, [done["1a"], done["1b"]])
-                for b in range(BLOCKS):
-                    if e > 0 and PUT_BACK_AFTER[e - 1][b] == i:
-                        put_back(e - 1, b, banks_y[b], hosts[i])
+                for b, y in zip(due, ys):
+                    put_back(e - 1, b, y)
                 if i == b_after:
                     b_sb = copy_b(banks_b, hosts[i])
                 if i == max(b_after, order.index("1b")):
@@ -218,4 +221,4 @@ def tile_moe_two_glu_relu_kernel(
                 banks_y.append(bank_y)
             for b in range(BLOCKS):
                 if e == E - 1 or PUT_BACK_AFTER[e][b] < 0:
-                    put_back(e, b, banks_y[b], hosts[-1])
+                    put_back(e, b, weigh(e, b, banks_y[b], hosts[-1]))

@@ -3,8 +3,8 @@ from contextlib import ExitStack
 import concourse.mybir as mybir
 
 K, T, E, C, H, N = 1024, 1536, 4, 256, 512, 512
-S = E * C
-FLOPS = 2 * S * (2 * K * H + H * N)
+SLOTS = E * C
+FLOPS = 2 * SLOTS * (2 * K * H + H * N)
 
 F32 = mybir.dt.float32
 BF16 = mybir.dt.bfloat16
@@ -19,14 +19,37 @@ P = 128
 PACK = 4
 K_PASS = P * PACK
 PASSES = K // K_PASS
+QUADRANT = 32
+SCALE_ROWS = 4
 HALF = 128
 HALVES = C // HALF
 BLOCKS = N // P
 LIST_COLS = C // 16
+LAST = E - 1
+
+W3_LO, W3_HI, W1_LO, W1_HI, W2 = range(5)
+PIECES = 5
+QUADS = H // 4
+
+VECTOR_QUADS = [
+    [32, 64, 48, 64, 16],
+    [0, 0, 0, 0, 32],
+    [0, 0, 0, 0, 0],
+    [32, 0, 0, 48, 0],
+]
+NOW = -1
+SCATTER_BEHIND = [
+    [NOW, NOW, W3_LO, W1_LO],
+    [NOW, NOW, W3_HI, W1_HI],
+    [NOW, NOW, W1_HI, W2],
+]
+HELD_FROM = 2
+COPY_B_BEHIND = [W1_HI, W2, W1_HI, W1_HI]
 Y_AT = PACK * C
-VECTOR_SHARE = [[32,64,48,64,16],[0,0,0,0,32],[0,0,0,0,0],[0,0,0,0,0]]
-PUT_BACK_AFTER = [[-1,-1,0,2],[-1,-1,1,3],[-1,-1,1,3]]
-PLAN = [[3,0,4],[4,0,1],[3,0,1],[3,0,1]]
+
+RAW_BUFS = 12
+ROUNDED_BUFS = 4
+CODED_BUFS = 8
 
 
 def tile_moe_two_glu_relu_kernel(
@@ -36,111 +59,93 @@ def tile_moe_two_glu_relu_kernel(
 
     with ExitStack() as ctx:
         keep = ctx.enter_context(tc.tile_pool(name="keep", bufs=1))
-        raws = ctx.enter_context(tc.tile_pool(name="raws", bufs=12))
-        rounded = ctx.enter_context(tc.tile_pool(name="rounded", bufs=4))
-        coded = ctx.enter_context(tc.tile_pool(name="coded", bufs=8))
+        raws = ctx.enter_context(tc.tile_pool(name="raws", bufs=RAW_BUFS))
+        rounded = ctx.enter_context(tc.tile_pool(name="rounded", bufs=ROUNDED_BUFS))
+        coded = ctx.enter_context(tc.tile_pool(name="coded", bufs=CODED_BUFS))
         hidden = ctx.enter_context(tc.tile_pool(name="hidden", bufs=2))
-        psum_a = ctx.enter_context(tc.psum_pool(name="psum_a", bufs=2))
-        psum_b = ctx.enter_context(tc.psum_pool(name="psum_b", bufs=2))
-        psum_y = ctx.enter_context(tc.psum_pool(name="psum_y", bufs=4))
+        psum_a = ctx.enter_context(tc.psum_pool(name="psum_a", bufs=HALVES))
+        psum_b = ctx.enter_context(tc.psum_pool(name="psum_b", bufs=HALVES))
+        psum_y = ctx.enter_context(tc.psum_pool(name="psum_y", bufs=BLOCKS))
 
-        offs_sb = keep.tile([P, S // 16], U16, name="offs_sb")
-        dst_sb = keep.tile([P, S // 16], U16, name="dst_sb")
+        offs_sb = keep.tile([P, SLOTS // 16], U16, name="offs_sb")
+        dst_sb = keep.tile([P, SLOTS // 16], U16, name="dst_sb")
         token_words = [keep.tile([P, T], I32, name=f"token_words{o}") for o in range(PASSES)]
         token_scales = keep.tile([P, T], U8, name="token_scales")
-        slot_words = [keep.tile([P, S], U32, name=f"slot_words{o}", align_bytes=64) for o in range(PASSES)]
-        slot_scales = keep.tile([P, S], U8, name="slot_scales", align_bytes=64)
+        slot_words = [keep.tile([P, SLOTS], U32, name=f"slot_words{o}", align_bytes=64) for o in range(PASSES)]
+        slot_scales = keep.tile([P, SLOTS], U8, name="slot_scales", align_bytes=64)
         gates = [keep.tile([P, BLOCKS, C], F32, name=f"gate{e}") for e in range(E)]
-        windows = [keep.tile([P, T], F32, name=f"window{b}") for b in range(BLOCKS)]
+        windows = [keep.tile([P, T], F32, name=f"window{r}") for r in range(BLOCKS)]
 
-        def load(rows):
+        def load_piece(rows):
             raw = raws.tile([P, PACK, H], F32, name="raw")
             nc.sync.dma_start(out=raw[:], in_=rows.rearrange("(p j) c -> p j c", j=PACK))
             return raw
 
-        def round_bf16(raw, permute, vector_share):
+        def load_gate(e, first, end):
+            nc.sync.dma_start(
+                out=gates[e][:, first:end, :],
+                in_=gate[first * P : end * P, e * C : (e + 1) * C].rearrange("(r p) s -> p r s", p=P),
+            )
+
+        def round_piece(raw, first_layer, vector_quads):
             grouped = rounded.tile([P, PACK * H], BF16, name="grouped", align_bytes=64)
-            if permute:
-                src = raw[:].rearrange("p j (m t) -> p m j t", t=4)
-                into = grouped[:].rearrange("p (t m j) -> p m j t", t=4, j=PACK)
-            else:
-                src = raw[:].rearrange("p j (m t) -> p m j t", t=4)
-                into = grouped[:].rearrange("p (m t j) -> p m j t", t=4, j=PACK)
-            cut = P - vector_share
-            if cut > 0:
-                nc.scalar.copy(out=into[:, :cut], in_=src[:, :cut])
-            if vector_share > 0:
+            src = raw[:].rearrange("p j (m u) -> p m j u", u=4)
+            layout = "p (u m j) -> p m j u" if first_layer else "p (m u j) -> p m j u"
+            into = grouped[:].rearrange(layout, u=4, j=PACK)
+            cut = QUADS - vector_quads
+            nc.scalar.copy(out=into[:, :cut], in_=src[:, :cut])
+            if vector_quads > 0:
                 nc.vector.tensor_copy(out=into[:, cut:], in_=src[:, cut:])
             return grouped
 
-        def quantize(grouped, calls):
+        def quantize_piece(grouped, calls):
             codes = coded.tile([P, H], U32, name="codes", align_bytes=64)
             scales = coded.tile([P, H], U8, name="scales", align_bytes=64)
             width = H // calls
-            for q in range(calls):
-                cols = slice(q * width, (q + 1) * width)
+            for call in range(calls):
+                cols = slice(call * width, (call + 1) * width)
                 nc.vector.quantize_mx(
                     out=codes[:, cols].bitcast(FP8X4),
                     scales=scales[:, cols],
-                    in_=grouped[:, PACK * q * width : PACK * (q + 1) * width],
+                    in_=grouped[:, PACK * call * width : PACK * (call + 1) * width],
                 )
             return codes, scales
 
-        def first_layer(e, pool, operands):
+        def first_product(e, pool, operands, bank_by_bank):
             banks = [pool.tile([P, PACK, HALF], F32, name="bank") for half in range(HALVES)]
-            for t in range(PACK):
-                cols = slice(t * P, (t + 1) * P)
-                for half in range(HALVES):
-                    slots = slice(e * C + half * HALF, e * C + (half + 1) * HALF)
-                    for o in range(PASSES):
-                        codes, scales = operands[o]
-                        nc.tensor.matmul_mx(
-                            out=banks[half][:, t, :],
-                            lhsT=codes[:, cols].bitcast(FP8X4),
-                            lhsT_scale=scales[:, cols],
-                            rhs=slot_words[o][:, slots].bitcast(FP8X4),
-                            rhs_scale=slot_scales[4 * o :, slots],
-                            start=(o == 0),
-                            stop=(o == PASSES - 1),
-                        )
+            if bank_by_bank:
+                groups = [(j, half) for half in range(HALVES) for j in range(PACK)]
+            else:
+                groups = [(j, half) for j in range(PACK) for half in range(HALVES)]
+            for j, half in groups:
+                cols = slice(j * P, (j + 1) * P)
+                slots = slice(e * C + half * HALF, e * C + (half + 1) * HALF)
+                for o in range(PASSES):
+                    codes, scales = operands[o]
+                    nc.tensor.matmul_mx(
+                        out=banks[half][:, j, :],
+                        lhsT=codes[:, cols].bitcast(FP8X4),
+                        lhsT_scale=scales[:, cols],
+                        rhs=slot_words[o][:, slots].bitcast(FP8X4),
+                        rhs_scale=slot_scales[SCALE_ROWS * o :, slots],
+                        start=(o == 0),
+                        stop=(o == PASSES - 1),
+                    )
             return banks
 
-        nc.vector.memset(token_scales[:].bitcast(I32), 0)
-        nc.vector.memset(windows[0][:], 0.0)
-        for b in range(1, BLOCKS):
-            nc.scalar.copy(out=windows[b][:], in_=windows[0][:])
-        nc.sync.dma_start(offs_sb[:], offs)
-        for o in range(PASSES):
-            nc.sync.dma_start(
-                out=token_words[o][:],
-                in_=x_words[o].rearrange("p t r -> p (t r)").bitcast(I32),
-            )
-
-        def flat(raw):
-            return raw[:].rearrange("p j c -> p (j c)")
-
-        def weigh(e, b, bank, raw):
-            y = flat(raw)[:, Y_AT + b * C : Y_AT + (b + 1) * C]
-            nc.vector.tensor_tensor(y, bank[:], gates[e][:, b, :], ALU.mult)
-            return y
-
-        def put_back(e, b, y):
-            nc.vector.tensor_copy(windows[b][:].indirect(dst_sb[:, e * LIST_COLS : (e + 1) * LIST_COLS]), y)
-            if e == E - 1:
-                nc.sync.dma_start(out=out[b * P : (b + 1) * P, :], in_=windows[b][:])
-
-        def copy_b(banks, raw):
-            b_sb = flat(raw)[:, : PACK * C].rearrange("p (u s t) -> p u s t", u=HALVES, t=PACK)
+        def copy_b(banks, freed):
+            flat = freed[:].rearrange("p j c -> p (j c)")
+            b_sb = flat[:, :Y_AT].rearrange("p (half s j) -> p half s j", half=HALVES, j=PACK)
             for half in range(HALVES):
-                nc.scalar.copy(out=b_sb[:, half], in_=banks[half][:].rearrange("p t s -> p s t"))
+                nc.scalar.copy(out=b_sb[:, half], in_=banks[half][:].rearrange("p j s -> p s j"))
             return b_sb
 
-        def hidden_layer(banks_a, b_sb):
+        def quantize_h(banks_a, b_sb):
             h = hidden.tile([P, HALVES, HALF, PACK], BF16, name="h", align_bytes=64)
             for half in range(HALVES):
                 nc.vector.scalar_tensor_tensor(
                     out=h[:, half],
-                    in0=banks_a[half][:].rearrange("p t s -> p s t"),
+                    in0=banks_a[half][:].rearrange("p j s -> p s j"),
                     scalar=0.0,
                     in1=b_sb[:, half],
                     op0=ALU.max,
@@ -153,72 +158,94 @@ def tile_moe_two_glu_relu_kernel(
                 nc.vector.quantize_mx(
                     out=h_codes[:, cols].bitcast(FP8X4),
                     scales=h_scales[:, cols],
-                    in_=h[:, half].rearrange("p s t -> p (s t)"),
+                    in_=h[:, half].rearrange("p s j -> p (s j)"),
                 )
             return h_codes, h_scales
 
+        def y_room(freed, r):
+            return freed[:].rearrange("p j c -> p (j c)")[:, Y_AT + r * C : Y_AT + (r + 1) * C]
+
+        def places(e, r):
+            return windows[r][:].indirect(dst_sb[:, e * LIST_COLS : (e + 1) * LIST_COLS])
+
+        def gate_y(e, r, bank, freed):
+            y = y_room(freed, r)
+            nc.vector.tensor_tensor(y, bank[:], gates[e][:, r, :], ALU.mult)
+            return y
+
+        nc.vector.memset(token_scales[:].bitcast(I32), 0)
+        nc.vector.memset(windows[0][:], 0.0)
+        for r in range(1, BLOCKS):
+            nc.scalar.copy(out=windows[r][:], in_=windows[0][:])
+        nc.sync.dma_start(offs_sb[:], offs)
+        for o in range(PASSES):
+            nc.sync.dma_start(
+                out=token_words[o][:],
+                in_=x_words[o].rearrange("p t j -> p (t j)").bitcast(I32),
+            )
+
         banks_y = []
         for e in range(E):
-            b_after, w2_early, split = PLAN[e]
-            order = ["3a", "3b", "1a", "2", "1b"] if w2_early else ["3a", "3b", "1a", "1b", "2"]
-            rows = {
-                "3a": w3[e, :K_PASS, :],
-                "3b": w3[e, K_PASS:, :],
-                "1a": w1[e, :K_PASS, :],
-                "1b": w1[e, K_PASS:, :],
-                "2": w2[e],
-            }
-            hosts = [load(rows[order[0]])]
+            rows = [w3[e, :K_PASS, :], w3[e, K_PASS:, :], w1[e, :K_PASS, :], w1[e, K_PASS:, :], w2[e]]
+            raw = [load_piece(rows[W3_LO])]
             if e == 0:
-                for q in range(4):
+                for q in range(P // QUADRANT):
                     nc.sync.dma_start(
-                        out=token_scales[32 * q : 32 * q + 4 * PASSES, :].bitcast(I32),
-                        in_=x_scales[:, 4 * q : 4 * q + 4, :].bitcast(I32),
+                        out=token_scales[QUADRANT * q : QUADRANT * q + SCALE_ROWS * PASSES, :].bitcast(I32),
+                        in_=x_scales[:, SCALE_ROWS * q : SCALE_ROWS * (q + 1), :].bitcast(I32),
                     )
-            hosts.extend([load(rows[n]) for n in order[1:]])
-            nc.sync.dma_start(
-                out=gates[e][:], in_=gate[:, e * C : (e + 1) * C].rearrange("(b p) s -> p b s", p=P)
-            )
+            raw.extend([load_piece(rows[piece]) for piece in (W3_HI, W1_LO, W1_HI)])
+            if e == LAST:
+                load_gate(LAST - 1, HELD_FROM, BLOCKS)
+            raw.append(load_piece(rows[W2]))
+            load_gate(e, 0, HELD_FROM if e == LAST - 1 else BLOCKS)
             if e == 0:
                 nc.sync.dma_start(dst_sb[:], dst)
+
             slots = slice(e * C, (e + 1) * C)
             picks = offs_sb[:, e * LIST_COLS : (e + 1) * LIST_COLS]
             nc.vector.tensor_copy(slot_scales[:, slots], token_scales[:].indirect(picks))
             for o in range(PASSES):
                 nc.vector.tensor_copy(slot_words[o][:, slots], token_words[o][:].bitcast(U32).indirect(picks))
 
-            share = VECTOR_SHARE[e]
-            done = {}
-            for i, n in enumerate(order):
-                grouped = round_bf16(hosts[i], n != "2", share[i])
-                due = [b for b in range(BLOCKS) if e > 0 and PUT_BACK_AFTER[e - 1][b] == i]
-                ys = [weigh(e - 1, b, banks_y[b], hosts[i]) for b in due]
-                done[n] = quantize(grouped, split if n == "1b" else 1)
-                if n == "3b":
-                    banks_b = first_layer(e, psum_b, [done["3a"], done["3b"]])
-                if n == "1b":
-                    banks_a = first_layer(e, psum_a, [done["1a"], done["1b"]])
-                for b, y in zip(due, ys):
-                    put_back(e - 1, b, y)
-                if i == b_after:
-                    b_sb = copy_b(banks_b, hosts[i])
-                if i == max(b_after, order.index("1b")):
-                    h_codes, h_scales = hidden_layer(banks_a, b_sb)
-            codes2, scales2 = done["2"]
+            quantized = []
+            for piece in range(PIECES):
+                grouped = round_piece(raw[piece], piece != W2, VECTOR_QUADS[e][piece])
+                due = [r for r in range(BLOCKS) if e > 0 and SCATTER_BEHIND[e - 1][r] == piece]
+                gated = [gate_y(e - 1, r, banks_y[r], raw[piece]) for r in due]
+                by_columns = e == 0 and piece == W1_HI
+                quantized.append(quantize_piece(grouped, PACK if by_columns else 1))
+                if piece == W3_HI:
+                    banks_b = first_product(e, psum_b, quantized[W3_LO : W3_HI + 1], True)
+                if piece == W1_HI:
+                    banks_a = first_product(e, psum_a, quantized[W1_LO : W1_HI + 1], not by_columns)
+                for r, y in zip(due, gated):
+                    nc.vector.tensor_copy(places(e - 1, r), y)
+                if piece == COPY_B_BEHIND[e]:
+                    h_codes, h_scales = quantize_h(banks_a, copy_b(banks_b, raw[piece]))
+
+            codes, scales = quantized[W2]
             banks_y = []
-            for b in range(BLOCKS):
-                cols = slice(b * P, (b + 1) * P)
+            for r in range(BLOCKS):
+                cols = slice(r * P, (r + 1) * P)
                 bank_y = psum_y.tile([P, C], F32, name="bank_y")
                 nc.tensor.matmul_mx(
                     out=bank_y[:],
-                    lhsT=codes2[:, cols].bitcast(FP8X4),
-                    lhsT_scale=scales2[:, cols],
+                    lhsT=codes[:, cols].bitcast(FP8X4),
+                    lhsT_scale=scales[:, cols],
                     rhs=h_codes[:].bitcast(FP8X4),
                     rhs_scale=h_scales[:],
                     start=True,
                     stop=True,
                 )
                 banks_y.append(bank_y)
-            for b in range(BLOCKS):
-                if e == E - 1 or PUT_BACK_AFTER[e][b] < 0:
-                    put_back(e, b, weigh(e, b, banks_y[b], hosts[-1]))
+
+            for r in range(BLOCKS):
+                if e == LAST:
+                    y = y_room(raw[W2], r)
+                    nc.scalar.copy(out=y, in_=banks_y[r][:])
+                    nc.vector.tensor_tensor(places(e, r), y, gates[e][:, r, :], ALU.mult)
+                    nc.sync.dma_start(out=out[r * P : (r + 1) * P, :], in_=windows[r][:])
+                elif SCATTER_BEHIND[e][r] == NOW:
+                    y = gate_y(e, r, banks_y[r], raw[W2])
+                    nc.vector.tensor_copy(places(e, r), y)

@@ -1,6 +1,7 @@
 from contextlib import ExitStack
 
 import concourse.mybir as mybir
+from concourse.masks import make_identity
 
 K, T, E, C, H, N = 1024, 1536, 4, 256, 512, 512
 SLOTS = E * C
@@ -26,28 +27,20 @@ HALVES = C // HALF
 BLOCKS = N // P
 LIST_COLS = C // 16
 LAST = E - 1
+PAIR = 2
+OCTETS = H // 8
+ROOM = 256
+GATE_COLS = SLOTS // P
 
 W3_LO, W3_HI, W1_LO, W1_HI, W2 = range(5)
 PIECES = 5
-QUADS = H // 4
 
-VECTOR_QUADS = [
-    [32, 64, 48, 64, 16],
-    [0, 0, 0, 0, 32],
-    [0, 0, 0, 0, 0],
-    [32, 0, 0, 48, 0],
-]
 NOW = -1
-SCATTER_BEHIND = [
-    [NOW, NOW, W3_LO, W1_LO],
-    [NOW, NOW, W3_HI, W1_HI],
-    [NOW, NOW, W1_HI, W2],
-]
-HELD_FROM = 2
-COPY_B_BEHIND = [W1_HI, W2, W1_HI, W1_HI]
-Y_AT = PACK * C
+VECTOR_OCTETS = [[32, 32, 32, 32, 0], [16, 0, 0, 0, 32], [16, 0, 0, 0, 32], [0, 0, 0, 16, 0]]
+SCATTER_BEHIND = [[W3_LO, W3_LO, W3_LO, W1_LO], [W3_HI, W3_HI, W1_LO, W2], [W3_HI, W3_HI, W1_HI, W2]]
+COPY_B_BEHIND = [W1_HI, W1_HI, W1_HI, W1_HI]
 
-RAW_BUFS = 12
+RAW_BUFS = 14
 ROUNDED_BUFS = 4
 CODED_BUFS = 8
 
@@ -73,28 +66,35 @@ def tile_moe_two_glu_relu_kernel(
         token_scales = keep.tile([P, T], U8, name="token_scales")
         slot_words = [keep.tile([P, SLOTS], U32, name=f"slot_words{o}", align_bytes=64) for o in range(PASSES)]
         slot_scales = keep.tile([P, SLOTS], U8, name="slot_scales", align_bytes=64)
-        gates = [keep.tile([P, BLOCKS, C], F32, name=f"gate{e}") for e in range(E)]
+        gate_cols = keep.tile([P, GATE_COLS], F32, name="gate_cols")
+        gates = keep.tile([P, SLOTS], F32, name="gates")
+        identity = keep.tile([P, P], F32, name="identity")
+        first_y = keep.tile([P, BLOCKS, C], F32, name="first_y")
         windows = [keep.tile([P, T], F32, name=f"window{r}") for r in range(BLOCKS)]
 
-        def load_piece(rows):
+        def load_piece(e, piece):
             raw = raws.tile([P, PACK, H], F32, name="raw")
-            nc.sync.dma_start(out=raw[:], in_=rows.rearrange("(p j) c -> p j c", j=PACK))
+            if piece == W2:
+                rows = w2[e].rearrange("(g j b) c -> b g j c", j=PACK, b=PAIR)
+                for b in range(PAIR):
+                    nc.sync.dma_start(out=raw[b:P:PAIR], in_=rows[b])
+            else:
+                w = w3 if piece in (W3_LO, W3_HI) else w1
+                o = 0 if piece in (W3_LO, W1_LO) else 1
+                rows = w[e, o * K_PASS : (o + 1) * K_PASS, :]
+                nc.sync.dma_start(out=raw[:], in_=rows.rearrange("(p j) c -> p j c", j=PACK))
             return raw
 
-        def load_gate(e, first, end):
-            nc.sync.dma_start(
-                out=gates[e][:, first:end, :],
-                in_=gate[first * P : end * P, e * C : (e + 1) * C].rearrange("(r p) s -> p r s", p=P),
-            )
-
-        def round_piece(raw, first_layer, vector_quads):
+        def round_piece(raw, first_layer, vector_octets, frees_room):
             grouped = rounded.tile([P, PACK * H], BF16, name="grouped", align_bytes=64)
-            src = raw[:].rearrange("p j (m u) -> p m j u", u=4)
-            layout = "p (u m j) -> p m j u" if first_layer else "p (m u j) -> p m j u"
-            into = grouped[:].rearrange(layout, u=4, j=PACK)
-            cut = QUADS - vector_quads
-            nc.scalar.copy(out=into[:, :cut], in_=src[:, :cut])
-            if vector_quads > 0:
+            src = raw[:].rearrange("p k (g j b) -> p g j k b", j=PACK, b=PAIR)
+            layout = "p (j g b k) -> p g j k b" if first_layer else "p (g j b k) -> p g j k b"
+            into = grouped[:].rearrange(layout, j=PACK, b=PAIR, k=PACK)
+            cut = OCTETS - vector_octets
+            edges = [0, ROOM // 8, cut] if frees_room and cut > ROOM // 8 else [0, cut]
+            for first, end in zip(edges, edges[1:]):
+                nc.scalar.copy(out=into[:, first:end], in_=src[:, first:end])
+            if vector_octets > 0:
                 nc.vector.tensor_copy(out=into[:, cut:], in_=src[:, cut:])
             return grouped
 
@@ -133,21 +133,27 @@ def tile_moe_two_glu_relu_kernel(
                     )
             return banks
 
-        def copy_b(banks, freed):
-            flat = freed[:].rearrange("p j c -> p (j c)")
-            b_sb = flat[:, :Y_AT].rearrange("p (half s j) -> p half s j", half=HALVES, j=PACK)
+        def copy_b(banks, freed, taken):
+            rooms = []
             for half in range(HALVES):
-                nc.scalar.copy(out=b_sb[:, half], in_=banks[half][:].rearrange("p j s -> p s j"))
-            return b_sb
+                row = taken + 2 * half
+                if row + 2 <= PACK:
+                    room = freed[:, row : row + 2, :ROOM]
+                else:
+                    room = freed[:, :2, ROOM:]
+                room = room.rearrange("p a (s j) -> p a s j", j=PACK)
+                nc.scalar.copy(out=room, in_=banks[half][:].rearrange("p j (a s) -> p a s j", a=2))
+                rooms.append(room)
+            return rooms
 
-        def quantize_h(banks_a, b_sb):
+        def quantize_h(banks_a, b_rooms):
             h = hidden.tile([P, HALVES, HALF, PACK], BF16, name="h", align_bytes=64)
             for half in range(HALVES):
                 nc.vector.scalar_tensor_tensor(
-                    out=h[:, half],
-                    in0=banks_a[half][:].rearrange("p j s -> p s j"),
+                    out=h[:, half].rearrange("p (a s) j -> p a s j", a=2),
+                    in0=banks_a[half][:].rearrange("p j (a s) -> p a s j", a=2),
                     scalar=0.0,
-                    in1=b_sb[:, half],
+                    in1=b_rooms[half],
                     op0=ALU.max,
                     op1=ALU.mult,
                 )
@@ -162,67 +168,77 @@ def tile_moe_two_glu_relu_kernel(
                 )
             return h_codes, h_scales
 
-        def y_room(freed, r):
-            return freed[:].rearrange("p j c -> p (j c)")[:, Y_AT + r * C : Y_AT + (r + 1) * C]
-
         def places(e, r):
             return windows[r][:].indirect(dst_sb[:, e * LIST_COLS : (e + 1) * LIST_COLS])
 
-        def gate_y(e, r, bank, freed):
-            y = y_room(freed, r)
-            nc.vector.tensor_tensor(y, bank[:], gates[e][:, r, :], ALU.mult)
-            return y
+        def scatter(e, r, y):
+            nc.vector.tensor_tensor(places(e, r), y, gates[:, e * C : (e + 1) * C], ALU.mult)
 
         nc.vector.memset(token_scales[:].bitcast(I32), 0)
         nc.vector.memset(windows[0][:], 0.0)
         for r in range(1, BLOCKS):
             nc.scalar.copy(out=windows[r][:], in_=windows[0][:])
+        make_identity(nc, identity[:])
         nc.sync.dma_start(offs_sb[:], offs)
+        nc.sync.dma_start(out=gate_cols[:], in_=gate[0, :].rearrange("(p c) -> p c", c=GATE_COLS))
         for o in range(PASSES):
             nc.sync.dma_start(
                 out=token_words[o][:],
                 in_=x_words[o].rearrange("p t j -> p (t j)").bitcast(I32),
             )
 
+        raw = []
+        for e in range(E):
+            raw.append([])
+            for piece in range(PIECES):
+                raw[e].append(load_piece(e, piece))
+                if e == 0 and piece == 0:
+                    for q in range(P // QUADRANT):
+                        nc.sync.dma_start(
+                            out=token_scales[QUADRANT * q : QUADRANT * q + SCALE_ROWS * PASSES, :].bitcast(I32),
+                            in_=x_scales[:, SCALE_ROWS * q : SCALE_ROWS * (q + 1), :].bitcast(I32),
+                        )
+                if e == 0 and piece == W1_HI:
+                    nc.sync.dma_start(dst_sb[:], dst)
+
+        for o in range(PASSES):
+            nc.vector.tensor_copy(slot_words[o][:], token_words[o][:].bitcast(U32).indirect(offs_sb[:]))
+        nc.vector.tensor_copy(slot_scales[:], token_scales[:].indirect(offs_sb[:]))
+
+        for group in range(GATE_COLS // 4):
+            spread = psum_y.tile([P, 4, P], F32, name="bank_y")
+            for c in range(4):
+                col = 4 * group + c
+                nc.tensor.transpose(spread[:, c, :], gate_cols[:, col : col + 1].to_broadcast([P, P]), identity[:])
+            nc.scalar.copy(
+                out=gates[:].rearrange("p (s c) -> p s c", c=GATE_COLS)[:, :, 4 * group : 4 * group + 4],
+                in_=spread[:].rearrange("p c s -> p s c"),
+            )
+
         banks_y = []
         for e in range(E):
-            rows = [w3[e, :K_PASS, :], w3[e, K_PASS:, :], w1[e, :K_PASS, :], w1[e, K_PASS:, :], w2[e]]
-            raw = [load_piece(rows[W3_LO])]
-            if e == 0:
-                for q in range(P // QUADRANT):
-                    nc.sync.dma_start(
-                        out=token_scales[QUADRANT * q : QUADRANT * q + SCALE_ROWS * PASSES, :].bitcast(I32),
-                        in_=x_scales[:, SCALE_ROWS * q : SCALE_ROWS * (q + 1), :].bitcast(I32),
-                    )
-            raw.extend([load_piece(rows[piece]) for piece in (W3_HI, W1_LO, W1_HI)])
-            if e == LAST:
-                load_gate(LAST - 1, HELD_FROM, BLOCKS)
-            raw.append(load_piece(rows[W2]))
-            load_gate(e, 0, HELD_FROM if e == LAST - 1 else BLOCKS)
-            if e == 0:
-                nc.sync.dma_start(dst_sb[:], dst)
-
-            slots = slice(e * C, (e + 1) * C)
-            picks = offs_sb[:, e * LIST_COLS : (e + 1) * LIST_COLS]
-            nc.vector.tensor_copy(slot_scales[:, slots], token_scales[:].indirect(picks))
-            for o in range(PASSES):
-                nc.vector.tensor_copy(slot_words[o][:, slots], token_words[o][:].bitcast(U32).indirect(picks))
-
             quantized = []
             for piece in range(PIECES):
-                grouped = round_piece(raw[piece], piece != W2, VECTOR_QUADS[e][piece])
                 due = [r for r in range(BLOCKS) if e > 0 and SCATTER_BEHIND[e - 1][r] == piece]
-                gated = [gate_y(e - 1, r, banks_y[r], raw[piece]) for r in due]
-                by_columns = e == 0 and piece == W1_HI
-                quantized.append(quantize_piece(grouped, PACK if by_columns else 1))
-                if piece == W3_HI:
-                    banks_b = first_product(e, psum_b, quantized[W3_LO : W3_HI + 1], True)
-                if piece == W1_HI:
-                    banks_a = first_product(e, psum_a, quantized[W1_LO : W1_HI + 1], not by_columns)
-                for r, y in zip(due, gated):
-                    nc.vector.tensor_copy(places(e - 1, r), y)
+                grouped = round_piece(
+                    raw[e][piece], piece != W2, VECTOR_OCTETS[e][piece], len(due) > 0 or piece == COPY_B_BEHIND[e]
+                )
+                staged = []
+                for row, r in enumerate(due):
+                    nc.scalar.copy(out=raw[e][piece][:, row, :ROOM], in_=banks_y[r][:])
+                    staged.append(raw[e][piece][:, row, :ROOM])
                 if piece == COPY_B_BEHIND[e]:
-                    h_codes, h_scales = quantize_h(banks_a, copy_b(banks_b, raw[piece]))
+                    b_rooms = copy_b(banks_b, raw[e][piece], len(due))
+                by_columns = e == 0 and piece == W1_HI
+                quantized.append(quantize_piece(grouped, 2 if by_columns else 1))
+                if piece == W3_HI:
+                    banks_b = first_product(e, psum_b, [quantized[W3_LO], quantized[W3_HI]], True)
+                if piece == W1_HI:
+                    banks_a = first_product(e, psum_a, [quantized[W1_LO], quantized[W1_HI]], not by_columns)
+                for r, y in zip(due, staged):
+                    scatter(e - 1, r, y)
+                if piece == W1_HI:
+                    h_codes, h_scales = quantize_h(banks_a, b_rooms)
 
             codes, scales = quantized[W2]
             banks_y = []
@@ -240,12 +256,15 @@ def tile_moe_two_glu_relu_kernel(
                 )
                 banks_y.append(bank_y)
 
-            for r in range(BLOCKS):
-                if e == LAST:
-                    y = y_room(raw[W2], r)
+            now = [r for r in range(BLOCKS) if e == LAST or SCATTER_BEHIND[e][r] == NOW]
+            if e == LAST:
+                for r in now:
+                    y = first_y[:, r, :]
                     nc.scalar.copy(out=y, in_=banks_y[r][:])
-                    nc.vector.tensor_tensor(places(e, r), y, gates[e][:, r, :], ALU.mult)
+                    scatter(e, r, y)
                     nc.sync.dma_start(out=out[r * P : (r + 1) * P, :], in_=windows[r][:])
-                elif SCATTER_BEHIND[e][r] == NOW:
-                    y = gate_y(e, r, banks_y[r], raw[W2])
-                    nc.vector.tensor_copy(places(e, r), y)
+            else:
+                for r in now:
+                    nc.vector.tensor_tensor(first_y[:, r, :], banks_y[r][:], gates[:, e * C : (e + 1) * C], ALU.mult)
+                for r in now:
+                    nc.vector.tensor_copy(places(e, r), first_y[:, r, :])

@@ -1,4 +1,5 @@
 from contextlib import ExitStack
+from itertools import product
 
 import concourse.mybir as mybir
 from concourse.masks import make_identity
@@ -36,13 +37,14 @@ W3_LO, W3_HI, W1_LO, W1_HI, W2 = range(5)
 PIECES = 5
 
 NOW = -1
-VECTOR_OCTETS = [[32, 32, 32, 32, 0], [16, 0, 0, 0, 32], [16, 0, 0, 0, 32], [0, 0, 0, 16, 0]]
-SCATTER_BEHIND = [[W3_LO, W3_LO, W3_LO, W1_LO], [W3_HI, W3_HI, W1_LO, W2], [W3_HI, W3_HI, W1_HI, W2]]
+VECTOR_OCTETS = [[0, 0, 32, 32, 0], [0, 0, 0, 0, 32], [16, 0, 0, 0, 32], [0, 0, 0, 16, 0]]
+SCATTER_BEHIND = [[NOW, NOW, W3_HI, W1_HI], [W3_HI, W3_HI, W1_HI, W2], [W3_HI, W3_HI, W1_HI, W2]]
 COPY_B_BEHIND = [W1_HI, W1_HI, W1_HI, W1_HI]
 
 RAW_BUFS = 14
-ROUNDED_BUFS = 4
-CODED_BUFS = 8
+ROUNDED_BUFS = 3
+CODED_BUFS = 3
+JOINED = [[], [], [], []]
 
 
 def tile_moe_two_glu_relu_kernel(
@@ -85,43 +87,38 @@ def tile_moe_two_glu_relu_kernel(
                 nc.sync.dma_start(out=raw[:], in_=rows.rearrange("(p j) c -> p j c", j=PACK))
             return raw
 
-        def round_piece(raw, first_layer, vector_octets, frees_room):
-            grouped = rounded.tile([P, PACK * H], BF16, name="grouped", align_bytes=64)
+        def round_piece(raw, grouped, first_layer, vector_octets, frees_room):
             src = raw[:].rearrange("p k (g j b) -> p g j k b", j=PACK, b=PAIR)
             layout = "p (j g b k) -> p g j k b" if first_layer else "p (g j b k) -> p g j k b"
-            into = grouped[:].rearrange(layout, j=PACK, b=PAIR, k=PACK)
+            into = grouped.rearrange(layout, j=PACK, b=PAIR, k=PACK)
             cut = OCTETS - vector_octets
             edges = [0, ROOM // 8, cut] if frees_room and cut > ROOM // 8 else [0, cut]
             for first, end in zip(edges, edges[1:]):
                 nc.scalar.copy(out=into[:, first:end], in_=src[:, first:end])
             if vector_octets > 0:
                 nc.vector.tensor_copy(out=into[:, cut:], in_=src[:, cut:])
-            return grouped
 
-        def quantize_piece(grouped, calls):
-            codes = coded.tile([P, H], U32, name="codes", align_bytes=64)
-            scales = coded.tile([P, H], U8, name="scales", align_bytes=64)
-            width = H // calls
-            for call in range(calls):
-                cols = slice(call * width, (call + 1) * width)
-                nc.vector.quantize_mx(
-                    out=codes[:, cols].bitcast(FP8X4),
-                    scales=scales[:, cols],
-                    in_=grouped[:, PACK * call * width : PACK * (call + 1) * width],
-                )
-            return codes, scales
+        def new_matrix(passes):
+            grouped = rounded.tile([P, passes * PACK * H], BF16, name=f"grouped{passes}", align_bytes=64)
+            codes = coded.tile([P, passes * H], U32, name=f"codes{passes}", align_bytes=64)
+            scales = coded.tile([P, passes * H], U8, name=f"scales{passes}", align_bytes=64)
+            return grouped, codes, scales
 
-        def first_product(e, pool, operands, bank_by_bank):
+        def quantize(matrix, first, end):
+            grouped, codes, scales = matrix
+            nc.vector.quantize_mx(
+                out=codes[:, first:end].bitcast(FP8X4),
+                scales=scales[:, first:end],
+                in_=grouped[:, PACK * first : PACK * end],
+            )
+
+        def first_product(e, pool, matrix):
+            grouped, codes, scales = matrix
             banks = [pool.tile([P, PACK, HALF], F32, name="bank") for half in range(HALVES)]
-            if bank_by_bank:
-                groups = [(j, half) for half in range(HALVES) for j in range(PACK)]
-            else:
-                groups = [(j, half) for j in range(PACK) for half in range(HALVES)]
-            for j, half in groups:
-                cols = slice(j * P, (j + 1) * P)
+            for half, j in product(range(HALVES), range(PACK)):
                 slots = slice(e * C + half * HALF, e * C + (half + 1) * HALF)
                 for o in range(PASSES):
-                    codes, scales = operands[o]
+                    cols = slice(o * H + j * P, o * H + (j + 1) * P)
                     nc.tensor.matmul_mx(
                         out=banks[half][:, j, :],
                         lhsT=codes[:, cols].bitcast(FP8X4),
@@ -146,7 +143,7 @@ def tile_moe_two_glu_relu_kernel(
                 rooms.append(room)
             return rooms
 
-        def quantize_h(banks_a, b_rooms):
+        def quantize_h(banks_a, b_rooms, calls):
             h = hidden.tile([P, HALVES, HALF, PACK], BF16, name="h", align_bytes=64)
             for half in range(HALVES):
                 nc.vector.scalar_tensor_tensor(
@@ -159,12 +156,14 @@ def tile_moe_two_glu_relu_kernel(
                 )
             h_codes = hidden.tile([P, C], U32, name="h_codes", align_bytes=64)
             h_scales = hidden.tile([P, C], U8, name="h_scales", align_bytes=64)
-            for half in range(HALVES):
-                cols = slice(half * HALF, (half + 1) * HALF)
+            flat = h[:].rearrange("p half s j -> p (half s j)")
+            width = C // calls
+            for call in range(calls):
+                cols = slice(call * width, (call + 1) * width)
                 nc.vector.quantize_mx(
                     out=h_codes[:, cols].bitcast(FP8X4),
                     scales=h_scales[:, cols],
-                    in_=h[:, half].rearrange("p s j -> p (s j)"),
+                    in_=flat[:, PACK * call * width : PACK * (call + 1) * width],
                 )
             return h_codes, h_scales
 
@@ -175,17 +174,19 @@ def tile_moe_two_glu_relu_kernel(
             nc.vector.tensor_tensor(places(e, r), y, gates[:, e * C : (e + 1) * C], ALU.mult)
 
         nc.vector.memset(token_scales[:].bitcast(I32), 0)
-        nc.vector.memset(windows[0][:], 0.0)
-        for r in range(1, BLOCKS):
+        for r in range(BLOCKS // 2):
+            nc.vector.memset(windows[r][:], 0.0)
+        for r in range(BLOCKS // 2, BLOCKS):
             nc.scalar.copy(out=windows[r][:], in_=windows[0][:])
         make_identity(nc, identity[:])
-        nc.sync.dma_start(offs_sb[:], offs)
-        nc.sync.dma_start(out=gate_cols[:], in_=gate[0, :].rearrange("(p c) -> p c", c=GATE_COLS))
         for o in range(PASSES):
             nc.sync.dma_start(
                 out=token_words[o][:],
                 in_=x_words[o].rearrange("p t j -> p (t j)").bitcast(I32),
             )
+            if o == 0:
+                nc.sync.dma_start(offs_sb[:], offs)
+        nc.sync.dma_start(out=gate_cols[:], in_=gate[0, :].rearrange("(p c) -> p c", c=GATE_COLS))
 
         raw = []
         for e in range(E):
@@ -217,36 +218,51 @@ def tile_moe_two_glu_relu_kernel(
 
         banks_y = []
         for e in range(E):
-            quantized = []
+            matrices = {W3_LO: new_matrix(PASSES), W1_LO: new_matrix(PASSES), W2: new_matrix(1)}
+            matrices[W3_HI], matrices[W1_HI] = matrices[W3_LO], matrices[W1_LO]
             for piece in range(PIECES):
+                matrix = matrices[piece]
+                o = 1 if piece in (W3_HI, W1_HI) else 0
                 due = [r for r in range(BLOCKS) if e > 0 and SCATTER_BEHIND[e - 1][r] == piece]
-                grouped = round_piece(
-                    raw[e][piece], piece != W2, VECTOR_OCTETS[e][piece], len(due) > 0 or piece == COPY_B_BEHIND[e]
-                )
-                staged = []
-                for row, r in enumerate(due):
-                    nc.scalar.copy(out=raw[e][piece][:, row, :ROOM], in_=banks_y[r][:])
-                    staged.append(raw[e][piece][:, row, :ROOM])
+                in_halves = piece == W2 and e in (0, LAST)
+                frees_room = len(due) > 0 or piece == COPY_B_BEHIND[e] or in_halves
+                grouped = matrix[0][:, o * PACK * H : (o + 1) * PACK * H]
+                round_piece(raw[e][piece], grouped, piece != W2, VECTOR_OCTETS[e][piece], frees_room)
+                rooms = raw[e][piece][:, :, :ROOM]
+                for pair in range(BLOCKS // 2):
+                    both = [r for r in due if r // 2 == pair]
+                    if both:
+                        row = due.index(both[0])
+                        nc.scalar.copy(
+                            out=rooms[:, row : row + len(both), :],
+                            in_=banks_y[pair][:, both[0] % 2 : both[-1] % 2 + 1, :],
+                        )
                 if piece == COPY_B_BEHIND[e]:
                     b_rooms = copy_b(banks_b, raw[e][piece], len(due))
-                by_columns = e == 0 and piece == W1_HI
-                quantized.append(quantize_piece(grouped, 2 if by_columns else 1))
+                if in_halves:
+                    quantize(matrix, 0, H // 2)
+                    quantize(matrix, H // 2, H)
+                elif piece + 1 in JOINED[e]:
+                    pass
+                elif piece in JOINED[e]:
+                    quantize(matrix, 0, PASSES * H)
+                else:
+                    quantize(matrix, o * H, (o + 1) * H)
                 if piece == W3_HI:
-                    banks_b = first_product(e, psum_b, [quantized[W3_LO], quantized[W3_HI]], True)
+                    banks_b = first_product(e, psum_b, matrix)
                 if piece == W1_HI:
-                    banks_a = first_product(e, psum_a, [quantized[W1_LO], quantized[W1_HI]], not by_columns)
-                for r, y in zip(due, staged):
-                    scatter(e - 1, r, y)
+                    banks_a = first_product(e, psum_a, matrix)
+                for row, r in enumerate(due):
+                    scatter(e - 1, r, rooms[:, row, :])
                 if piece == W1_HI:
-                    h_codes, h_scales = quantize_h(banks_a, b_rooms)
+                    h_codes, h_scales = quantize_h(banks_a, b_rooms, HALVES if e == 0 else 1)
 
-            codes, scales = quantized[W2]
-            banks_y = []
+            grouped, codes, scales = matrices[W2]
+            banks_y = [psum_y.tile([P, 2, C], F32, name="bank_y") for pair in range(BLOCKS // 2)]
             for r in range(BLOCKS):
                 cols = slice(r * P, (r + 1) * P)
-                bank_y = psum_y.tile([P, C], F32, name="bank_y")
                 nc.tensor.matmul_mx(
-                    out=bank_y[:],
+                    out=banks_y[r // 2][:, r % 2, :],
                     lhsT=codes[:, cols].bitcast(FP8X4),
                     lhsT_scale=scales[:, cols],
                     rhs=h_codes[:].bitcast(FP8X4),
@@ -254,17 +270,17 @@ def tile_moe_two_glu_relu_kernel(
                     start=True,
                     stop=True,
                 )
-                banks_y.append(bank_y)
 
             now = [r for r in range(BLOCKS) if e == LAST or SCATTER_BEHIND[e][r] == NOW]
             if e == LAST:
                 for r in now:
-                    y = first_y[:, r, :]
-                    nc.scalar.copy(out=y, in_=banks_y[r][:])
-                    scatter(e, r, y)
+                    if r % 2 == 0:
+                        nc.scalar.copy(out=first_y[:, r : r + 2, :], in_=banks_y[r // 2][:])
+                    scatter(e, r, first_y[:, r, :])
                     nc.sync.dma_start(out=out[r * P : (r + 1) * P, :], in_=windows[r][:])
             else:
                 for r in now:
-                    nc.vector.tensor_tensor(first_y[:, r, :], banks_y[r][:], gates[:, e * C : (e + 1) * C], ALU.mult)
+                    y = banks_y[r // 2][:, r % 2, :]
+                    nc.vector.tensor_tensor(first_y[:, r, :], y, gates[:, e * C : (e + 1) * C], ALU.mult)
                 for r in now:
                     nc.vector.tensor_copy(places(e, r), first_y[:, r, :])

@@ -37,11 +37,14 @@ W3_LO, W3_HI, W1_LO, W1_HI, W2 = range(5)
 PIECES = 5
 
 NOW = -1
-VECTOR_OCTETS = [[0, 0, 32, 32, 0], [0, 0, 0, 0, 32], [16, 0, 0, 0, 32], [0, 0, 0, 16, 0]]
-SCATTER_BEHIND = [[NOW, NOW, W3_HI, W1_HI], [W3_HI, W3_HI, W1_HI, W2], [W3_HI, W3_HI, W1_HI, W2]]
+BY_MATRIX = [W3_LO, W3_HI, W1_LO, W1_HI, W2]
+BY_PASS = [W3_LO, W1_LO, W3_HI, W1_HI, W2]
+ORDER = [BY_MATRIX, BY_MATRIX, BY_MATRIX, BY_MATRIX]
+VECTOR_OCTETS = [[0, 0, 32, 32, 0], [0, 0, 0, 24, 0], [0, 0, 0, 24, 0], [0, 0, 0, 24, 0]]
+SCATTER_BEHIND = [[NOW, NOW, W1_HI, W2], [W3_LO, W3_LO, W1_HI, W2], [W3_LO, W3_LO, W1_HI, W2]]
 COPY_B_BEHIND = [W1_HI, W1_HI, W1_HI, W1_HI]
 
-RAW_BUFS = 14
+RAW_BUFS = 12
 ROUNDED_BUFS = 3
 CODED_BUFS = 3
 JOINED = [[], [], [], []]
@@ -75,7 +78,8 @@ def tile_moe_two_glu_relu_kernel(
         windows = [keep.tile([P, T], F32, name=f"window{r}") for r in range(BLOCKS)]
 
         def load_piece(e, piece):
-            raw = raws.tile([P, PACK, H], F32, name="raw")
+            room = raws.tile([P, PACK * H + ROOM], F32, name="raw")
+            raw = room[:, : PACK * H].rearrange("p (j c) -> p j c", j=PACK)
             if piece == W2:
                 rows = w2[e].rearrange("(g j b) c -> b g j c", j=PACK, b=PAIR)
                 for b in range(PAIR):
@@ -84,11 +88,11 @@ def tile_moe_two_glu_relu_kernel(
                 w = w3 if piece in (W3_LO, W3_HI) else w1
                 o = 0 if piece in (W3_LO, W1_LO) else 1
                 rows = w[e, o * K_PASS : (o + 1) * K_PASS, :]
-                nc.sync.dma_start(out=raw[:], in_=rows.rearrange("(p j) c -> p j c", j=PACK))
-            return raw
+                nc.sync.dma_start(out=raw, in_=rows.rearrange("(p j) c -> p j c", j=PACK))
+            return room
 
         def round_piece(raw, grouped, first_layer, vector_octets, frees_room):
-            src = raw[:].rearrange("p k (g j b) -> p g j k b", j=PACK, b=PAIR)
+            src = raw[:, : PACK * H].rearrange("p (k g j b) -> p g j k b", k=PACK, j=PACK, b=PAIR)
             layout = "p (j g b k) -> p g j k b" if first_layer else "p (g j b k) -> p g j k b"
             into = grouped.rearrange(layout, j=PACK, b=PAIR, k=PACK)
             cut = OCTETS - vector_octets
@@ -130,18 +134,19 @@ def tile_moe_two_glu_relu_kernel(
                     )
             return banks
 
+        def rooms(freed, first, count):
+            return freed[:, first * H : (first + count - 1) * H + ROOM].rearrange("p (a c) -> p a c", a=1) if count == 1 else spaced(freed, first)
+
+        def spaced(freed, first):
+            return freed[:].rearrange("p (a c) -> p a c", c=ROOM)[:, 2 * first : 2 * first + 3 : 2, :]
+
         def copy_b(banks, freed, taken):
-            rooms = []
+            held = []
             for half in range(HALVES):
-                row = taken + 2 * half
-                if row + 2 <= PACK:
-                    room = freed[:, row : row + 2, :ROOM]
-                else:
-                    room = freed[:, :2, ROOM:]
-                room = room.rearrange("p a (s j) -> p a s j", j=PACK)
+                room = rooms(freed, taken + 2 * half, 2).rearrange("p a (s j) -> p a s j", j=PACK)
                 nc.scalar.copy(out=room, in_=banks[half][:].rearrange("p j (a s) -> p a s j", a=2))
-                rooms.append(room)
-            return rooms
+                held.append(room)
+            return held
 
         def quantize_h(banks_a, b_rooms, calls):
             h = hidden.tile([P, HALVES, HALF, PACK], BF16, name="h", align_bytes=64)
@@ -190,9 +195,9 @@ def tile_moe_two_glu_relu_kernel(
 
         raw = []
         for e in range(E):
-            raw.append([])
-            for piece in range(PIECES):
-                raw[e].append(load_piece(e, piece))
+            raw.append({})
+            for piece in ORDER[e]:
+                raw[e][piece] = load_piece(e, piece)
                 if e == 0 and piece == 0:
                     for q in range(P // QUADRANT):
                         nc.sync.dma_start(
@@ -220,7 +225,7 @@ def tile_moe_two_glu_relu_kernel(
         for e in range(E):
             matrices = {W3_LO: new_matrix(PASSES), W1_LO: new_matrix(PASSES), W2: new_matrix(1)}
             matrices[W3_HI], matrices[W1_HI] = matrices[W3_LO], matrices[W1_LO]
-            for piece in range(PIECES):
+            for piece in ORDER[e]:
                 matrix = matrices[piece]
                 o = 1 if piece in (W3_HI, W1_HI) else 0
                 due = [r for r in range(BLOCKS) if e > 0 and SCATTER_BEHIND[e - 1][r] == piece]
@@ -228,13 +233,12 @@ def tile_moe_two_glu_relu_kernel(
                 frees_room = len(due) > 0 or piece == COPY_B_BEHIND[e] or in_halves
                 grouped = matrix[0][:, o * PACK * H : (o + 1) * PACK * H]
                 round_piece(raw[e][piece], grouped, piece != W2, VECTOR_OCTETS[e][piece], frees_room)
-                rooms = raw[e][piece][:, :, :ROOM]
                 for pair in range(BLOCKS // 2):
                     both = [r for r in due if r // 2 == pair]
                     if both:
                         row = due.index(both[0])
                         nc.scalar.copy(
-                            out=rooms[:, row : row + len(both), :],
+                            out=rooms(raw[e][piece], row, len(both)),
                             in_=banks_y[pair][:, both[0] % 2 : both[-1] % 2 + 1, :],
                         )
                 if piece == COPY_B_BEHIND[e]:
@@ -253,7 +257,7 @@ def tile_moe_two_glu_relu_kernel(
                 if piece == W1_HI:
                     banks_a = first_product(e, psum_a, matrix)
                 for row, r in enumerate(due):
-                    scatter(e - 1, r, rooms[:, row, :])
+                    scatter(e - 1, r, raw[e][piece][:, row * H : row * H + ROOM])
                 if piece == W1_HI:
                     h_codes, h_scales = quantize_h(banks_a, b_rooms, HALVES if e == 0 else 1)
 

@@ -16,6 +16,7 @@ U16 = mybir.dt.uint16
 U8 = mybir.dt.uint8
 FP8X4 = mybir.dt.float8_e4m3fn_x4
 ALU = mybir.AluOpType
+COPY = mybir.ActivationFunctionType.Copy
 
 P = 128
 PACK = 4
@@ -30,24 +31,23 @@ LIST_COLS = C // 16
 LAST = E - 1
 PAIR = 2
 OCTETS = H // 8
-ROOM = 256
 GATE_COLS = SLOTS // P
 
 W3_LO, W3_HI, W1_LO, W1_HI, W2 = range(5)
 PIECES = 5
+NOW, MID, END = -1, 0, 1
 
-NOW = -1
-BY_MATRIX = [W3_LO, W3_HI, W1_LO, W1_HI, W2]
-BY_PASS = [W3_LO, W1_LO, W3_HI, W1_HI, W2]
-ORDER = [BY_MATRIX, BY_MATRIX, BY_MATRIX, BY_MATRIX]
-VECTOR_OCTETS = [[0, 0, 32, 32, 0], [0, 0, 0, 24, 0], [0, 0, 0, 24, 0], [0, 0, 0, 24, 0]]
-SCATTER_BEHIND = [[NOW, NOW, W1_HI, W2], [W3_LO, W3_LO, W1_HI, W2], [W3_LO, W3_LO, W1_HI, W2]]
-COPY_B_BEHIND = [W1_HI, W1_HI, W1_HI, W1_HI]
+SCALAR_OCTETS = [[64,64,0,24,64],[64,0,0,0,0],[64,0,0,0,0],[64,0,0,0,0]]
+GATE_AT = [[NOW,[W3_HI,END],[W1_LO,END],[W1_HI,END]],[NOW,[W3_HI,END],[W1_LO,END],[W1_HI,END]],[NOW,[W3_HI,END],[W1_LO,END],[W1_HI,END]]]
+B_HELD = [1,0,0,0]
+TAIL_ON_VECTOR = [0,2]
+W2_HALVES = [0,1,2,3]
+HI_CALLS = [1,1,1,1]
 
+H_HELD = [1,2,3]
 RAW_BUFS = 12
-ROUNDED_BUFS = 3
-CODED_BUFS = 3
-JOINED = [[], [], [], []]
+ROUNDED_BUFS = 5
+CODED_BUFS = 6
 
 
 def tile_moe_two_glu_relu_kernel(
@@ -74,12 +74,12 @@ def tile_moe_two_glu_relu_kernel(
         gate_cols = keep.tile([P, GATE_COLS], F32, name="gate_cols")
         gates = keep.tile([P, SLOTS], F32, name="gates")
         identity = keep.tile([P, P], F32, name="identity")
-        first_y = keep.tile([P, BLOCKS, C], F32, name="first_y")
+        free_y = keep.tile([P, 2 * BLOCKS, C], F32, name="free_y")
         windows = [keep.tile([P, T], F32, name=f"window{r}") for r in range(BLOCKS)]
 
         def load_piece(e, piece):
-            room = raws.tile([P, PACK * H + ROOM], F32, name="raw")
-            raw = room[:, : PACK * H].rearrange("p (j c) -> p j c", j=PACK)
+            room = raws.tile([P, PACK * H], F32, name="raw", align_bytes=64)
+            raw = room[:].rearrange("p (j c) -> p j c", j=PACK)
             if piece == W2:
                 rows = w2[e].rearrange("(g j b) c -> b g j c", j=PACK, b=PAIR)
                 for b in range(PAIR):
@@ -91,97 +91,97 @@ def tile_moe_two_glu_relu_kernel(
                 nc.sync.dma_start(out=raw, in_=rows.rearrange("(p j) c -> p j c", j=PACK))
             return room
 
-        def round_piece(raw, grouped, first_layer, vector_octets, frees_room):
-            src = raw[:, : PACK * H].rearrange("p (k g j b) -> p g j k b", k=PACK, j=PACK, b=PAIR)
+        def round_part(raw, grouped, first_layer, first, end, on_scalar):
+            src = raw[:].rearrange("p (k g j b) -> p g j k b", k=PACK, j=PACK, b=PAIR)
             layout = "p (j g b k) -> p g j k b" if first_layer else "p (g j b k) -> p g j k b"
-            into = grouped.rearrange(layout, j=PACK, b=PAIR, k=PACK)
-            cut = OCTETS - vector_octets
-            edges = [0, ROOM // 8, cut] if frees_room and cut > ROOM // 8 else [0, cut]
-            for first, end in zip(edges, edges[1:]):
+            into = grouped[:].rearrange(layout, j=PACK, b=PAIR, k=PACK)
+            if on_scalar:
                 nc.scalar.copy(out=into[:, first:end], in_=src[:, first:end])
-            if vector_octets > 0:
-                nc.vector.tensor_copy(out=into[:, cut:], in_=src[:, cut:])
+            else:
+                nc.vector.tensor_copy(out=into[:, first:end], in_=src[:, first:end])
 
-        def new_matrix(passes):
-            grouped = rounded.tile([P, passes * PACK * H], BF16, name=f"grouped{passes}", align_bytes=64)
-            codes = coded.tile([P, passes * H], U32, name=f"codes{passes}", align_bytes=64)
-            scales = coded.tile([P, passes * H], U8, name=f"scales{passes}", align_bytes=64)
-            return grouped, codes, scales
-
-        def quantize(matrix, first, end):
-            grouped, codes, scales = matrix
+        def quantize(grouped, codes, scales, first, end):
             nc.vector.quantize_mx(
                 out=codes[:, first:end].bitcast(FP8X4),
                 scales=scales[:, first:end],
                 in_=grouped[:, PACK * first : PACK * end],
             )
 
-        def first_product(e, pool, matrix):
-            grouped, codes, scales = matrix
-            banks = [pool.tile([P, PACK, HALF], F32, name="bank") for half in range(HALVES)]
+        def first_layer_pass(e, o, banks, codes, scales):
             for half, j in product(range(HALVES), range(PACK)):
                 slots = slice(e * C + half * HALF, e * C + (half + 1) * HALF)
-                for o in range(PASSES):
-                    cols = slice(o * H + j * P, o * H + (j + 1) * P)
-                    nc.tensor.matmul_mx(
-                        out=banks[half][:, j, :],
-                        lhsT=codes[:, cols].bitcast(FP8X4),
-                        lhsT_scale=scales[:, cols],
-                        rhs=slot_words[o][:, slots].bitcast(FP8X4),
-                        rhs_scale=slot_scales[SCALE_ROWS * o :, slots],
-                        start=(o == 0),
-                        stop=(o == PASSES - 1),
-                    )
-            return banks
+                cols = slice(j * P, (j + 1) * P)
+                nc.tensor.matmul_mx(
+                    out=banks[half][:, j, :],
+                    lhsT=codes[:, cols].bitcast(FP8X4),
+                    lhsT_scale=scales[:, cols],
+                    rhs=slot_words[o][:, slots].bitcast(FP8X4),
+                    rhs_scale=slot_scales[SCALE_ROWS * o :, slots],
+                    start=(o == 0 and j == 0),
+                    stop=(o == PASSES - 1 and j == PACK - 1),
+                )
 
-        def rooms(freed, first, count):
-            return freed[:, first * H : (first + count - 1) * H + ROOM].rearrange("p (a c) -> p a c", a=1) if count == 1 else spaced(freed, first)
+        def rows_of(raw):
+            return raw[:].rearrange("p (k c) -> p k c", k=PACK)
 
-        def spaced(freed, first):
-            return freed[:].rearrange("p (a c) -> p a c", c=ROOM)[:, 2 * first : 2 * first + 3 : 2, :]
-
-        def copy_b(banks, freed, taken):
-            held = []
+        def copy_b(banks, raw, held):
+            result = []
             for half in range(HALVES):
-                room = rooms(freed, taken + 2 * half, 2).rearrange("p a (s j) -> p a s j", j=PACK)
-                nc.scalar.copy(out=room, in_=banks[half][:].rearrange("p j (a s) -> p a s j", a=2))
-                held.append(room)
-            return held
+                if half < held:
+                    room = rows_of(raw)[:, :, half * HALF : (half + 1) * HALF]
+                else:
+                    spare = hidden.tile([P, PACK * HALF], F32, name=f"b_free{half}")
+                    room = rows_of(spare)
+                room = room.rearrange("p a (s j) -> p a s j", j=PACK)
+                nc.scalar.copy(out=room, in_=banks[half][:].rearrange("p j (a s) -> p a s j", a=PACK))
+                result.append(room)
+            return result
 
-        def quantize_h(banks_a, b_rooms, calls):
-            h = hidden.tile([P, HALVES, HALF, PACK], BF16, name="h", align_bytes=64)
+        def make_h(banks_a, b_rooms, raw):
+            if raw is None:
+                own = hidden.tile([P, HALVES, HALF * PACK], BF16, name="h", align_bytes=64)
+                h = [own[:, half, :] for half in range(HALVES)]
+            else:
+                h = [raw[:, half * H : half * H + C].bitcast(BF16) for half in range(HALVES)]
             for half in range(HALVES):
                 nc.vector.scalar_tensor_tensor(
-                    out=h[:, half].rearrange("p (a s) j -> p a s j", a=2),
-                    in0=banks_a[half][:].rearrange("p j (a s) -> p a s j", a=2),
+                    out=h[half].rearrange("p (a s j) -> p a s j", a=PACK, j=PACK),
+                    in0=banks_a[half][:].rearrange("p j (a s) -> p a s j", a=PACK),
                     scalar=0.0,
                     in1=b_rooms[half],
                     op0=ALU.max,
                     op1=ALU.mult,
                 )
+            return h
+
+        def quantize_h(h):
             h_codes = hidden.tile([P, C], U32, name="h_codes", align_bytes=64)
             h_scales = hidden.tile([P, C], U8, name="h_scales", align_bytes=64)
-            flat = h[:].rearrange("p half s j -> p (half s j)")
-            width = C // calls
-            for call in range(calls):
-                cols = slice(call * width, (call + 1) * width)
-                nc.vector.quantize_mx(
-                    out=h_codes[:, cols].bitcast(FP8X4),
-                    scales=h_scales[:, cols],
-                    in_=flat[:, PACK * call * width : PACK * (call + 1) * width],
-                )
+            for half in range(HALVES):
+                cols = slice(half * HALF, (half + 1) * HALF)
+                nc.vector.quantize_mx(out=h_codes[:, cols].bitcast(FP8X4), scales=h_scales[:, cols], in_=h[half])
             return h_codes, h_scales
 
         def places(e, r):
             return windows[r][:].indirect(dst_sb[:, e * LIST_COLS : (e + 1) * LIST_COLS])
 
-        def scatter(e, r, y):
-            nc.vector.tensor_tensor(places(e, r), y, gates[:, e * C : (e + 1) * C], ALU.mult)
+        def gate_blocks(e, y, into, count):
+            weight = gates[:, e * C : (e + 1) * C].unsqueeze(1).to_broadcast([P, count, C])
+            nc.vector.tensor_tensor(into, y, weight, ALU.mult)
+
+        def leave(e, due, banks, rooms):
+            for pair in range(BLOCKS // 2):
+                both = [r for r in due if r // 2 == pair]
+                if both:
+                    row = due.index(both[0])
+                    y = banks[pair][:, both[0] % 2 : both[-1] % 2 + 1, :]
+                    gate_blocks(e, y, rooms[:, row : row + len(both), :], len(both))
+                    for n, r in enumerate(both):
+                        nc.scalar.activation(places(e, r), rooms[:, row + n, :], COPY)
 
         nc.vector.memset(token_scales[:].bitcast(I32), 0)
-        for r in range(BLOCKS // 2):
-            nc.vector.memset(windows[r][:], 0.0)
-        for r in range(BLOCKS // 2, BLOCKS):
+        nc.vector.memset(windows[0][:], 0.0)
+        for r in range(1, BLOCKS):
             nc.scalar.copy(out=windows[r][:], in_=windows[0][:])
         make_identity(nc, identity[:])
         for o in range(PASSES):
@@ -191,19 +191,18 @@ def tile_moe_two_glu_relu_kernel(
             )
             if o == 0:
                 nc.sync.dma_start(offs_sb[:], offs)
+                for q in range(P // QUADRANT):
+                    nc.scalar.dma_start(
+                        out=token_scales[QUADRANT * q : QUADRANT * q + SCALE_ROWS * PASSES, :].bitcast(I32),
+                        in_=x_scales[:, SCALE_ROWS * q : SCALE_ROWS * (q + 1), :].bitcast(I32),
+                    )
         nc.sync.dma_start(out=gate_cols[:], in_=gate[0, :].rearrange("(p c) -> p c", c=GATE_COLS))
 
         raw = []
         for e in range(E):
             raw.append({})
-            for piece in ORDER[e]:
+            for piece in range(PIECES):
                 raw[e][piece] = load_piece(e, piece)
-                if e == 0 and piece == 0:
-                    for q in range(P // QUADRANT):
-                        nc.sync.dma_start(
-                            out=token_scales[QUADRANT * q : QUADRANT * q + SCALE_ROWS * PASSES, :].bitcast(I32),
-                            in_=x_scales[:, SCALE_ROWS * q : SCALE_ROWS * (q + 1), :].bitcast(I32),
-                        )
                 if e == 0 and piece == W1_HI:
                     nc.sync.dma_start(dst_sb[:], dst)
 
@@ -223,50 +222,53 @@ def tile_moe_two_glu_relu_kernel(
 
         banks_y = []
         for e in range(E):
-            matrices = {W3_LO: new_matrix(PASSES), W1_LO: new_matrix(PASSES), W2: new_matrix(1)}
-            matrices[W3_HI], matrices[W1_HI] = matrices[W3_LO], matrices[W1_LO]
-            for piece in ORDER[e]:
-                matrix = matrices[piece]
-                o = 1 if piece in (W3_HI, W1_HI) else 0
-                due = [r for r in range(BLOCKS) if e > 0 and SCATTER_BEHIND[e - 1][r] == piece]
-                in_halves = piece == W2 and e in (0, LAST)
-                frees_room = len(due) > 0 or piece == COPY_B_BEHIND[e] or in_halves
-                grouped = matrix[0][:, o * PACK * H : (o + 1) * PACK * H]
-                round_piece(raw[e][piece], grouped, piece != W2, VECTOR_OCTETS[e][piece], frees_room)
-                for pair in range(BLOCKS // 2):
-                    both = [r for r in due if r // 2 == pair]
-                    if both:
-                        row = due.index(both[0])
-                        nc.scalar.copy(
-                            out=rooms(raw[e][piece], row, len(both)),
-                            in_=banks_y[pair][:, both[0] % 2 : both[-1] % 2 + 1, :],
-                        )
-                if piece == COPY_B_BEHIND[e]:
-                    b_rooms = copy_b(banks_b, raw[e][piece], len(due))
-                if in_halves:
-                    quantize(matrix, 0, H // 2)
-                    quantize(matrix, H // 2, H)
-                elif piece + 1 in JOINED[e]:
-                    pass
-                elif piece in JOINED[e]:
-                    quantize(matrix, 0, PASSES * H)
-                else:
-                    quantize(matrix, o * H, (o + 1) * H)
-                if piece == W3_HI:
-                    banks_b = first_product(e, psum_b, matrix)
+            for piece in range(PIECES):
+                grouped = rounded.tile([P, PACK * H], BF16, name="grouped", align_bytes=64)
+                codes = coded.tile([P, H], U32, name="codes", align_bytes=64)
+                scales = coded.tile([P, H], U8, name="scales", align_bytes=64)
+                here = raw[e][piece]
+                mid = [r for r in range(BLOCKS) if e > 0 and GATE_AT[e - 1][r] == [piece, MID]]
+                end = [r for r in range(BLOCKS) if e > 0 and GATE_AT[e - 1][r] == [piece, END]]
+                share = SCALAR_OCTETS[e][piece]
+                halved = len(mid) + len(end) > 0 or (piece == W2 and (e in W2_HALVES or e in H_HELD)) or (piece == W1_HI and B_HELD[e] > 0 and share > 32)
+                edges = sorted(set([0, share, OCTETS] + ([OCTETS // 2] if halved else [])))
+                rooms = rows_of(here)[:, :, :C]
+                for first, stop in zip(edges, edges[1:]):
+                    round_part(here, grouped, piece != W2, first, stop, stop <= share)
+                    if stop == OCTETS // 2:
+                        leave(e - 1, mid, banks_y, rooms)
+                        if piece == W2 and e in H_HELD:
+                            h = make_h(banks_a, b_rooms, here)
+                if piece == W2 and e in H_HELD:
+                    h_codes, h_scales = quantize_h(h)
+                leave(e - 1, end, banks_y, rooms[:, len(mid) :, :])
                 if piece == W1_HI:
-                    banks_a = first_product(e, psum_a, matrix)
-                for row, r in enumerate(due):
-                    scatter(e - 1, r, raw[e][piece][:, row * H : row * H + ROOM])
-                if piece == W1_HI:
-                    h_codes, h_scales = quantize_h(banks_a, b_rooms, HALVES if e == 0 else 1)
+                    b_rooms = copy_b(banks_b, here, B_HELD[e])
+                calls = 2 if (piece == W2 and e in W2_HALVES) else (HI_CALLS[e] if piece == W1_HI else 1)
+                for call in range(calls):
+                    quantize(grouped, codes, scales, call * H // calls, (call + 1) * H // calls)
+                if piece == W3_LO:
+                    banks_b = [psum_b.tile([P, PACK, HALF], F32, name="bank") for half in range(HALVES)]
+                if piece == W1_LO:
+                    banks_a = [psum_a.tile([P, PACK, HALF], F32, name="bank") for half in range(HALVES)]
+                if piece in (W3_LO, W3_HI):
+                    first_layer_pass(e, piece - W3_LO, banks_b, codes, scales)
+                if piece in (W1_LO, W1_HI):
+                    first_layer_pass(e, piece - W1_LO, banks_a, codes, scales)
+                if piece == W1_HI and e not in H_HELD:
+                    h_codes, h_scales = quantize_h(make_h(banks_a, b_rooms, None))
 
-            grouped, codes, scales = matrices[W2]
-            banks_y = [psum_y.tile([P, 2, C], F32, name="bank_y") for pair in range(BLOCKS // 2)]
+            if e < LAST:
+                banks_y = [psum_y.tile([P, 2, C], F32, name="bank_y") for pair in range(BLOCKS // 2)]
+                sums = [banks_y[r // 2][:, r % 2, :] for r in range(BLOCKS)]
+            else:
+                own = [psum_y.tile([P, C], F32, name="bank_y") for r in range(2)]
+                own = own + [psum_b.tile([P, C], F32, name="bank") for r in range(2)]
+                sums = [bank[:] for bank in own]
             for r in range(BLOCKS):
                 cols = slice(r * P, (r + 1) * P)
                 nc.tensor.matmul_mx(
-                    out=banks_y[r // 2][:, r % 2, :],
+                    out=sums[r],
                     lhsT=codes[:, cols].bitcast(FP8X4),
                     lhsT_scale=scales[:, cols],
                     rhs=h_codes[:].bitcast(FP8X4),
@@ -275,16 +277,21 @@ def tile_moe_two_glu_relu_kernel(
                     stop=True,
                 )
 
-            now = [r for r in range(BLOCKS) if e == LAST or SCATTER_BEHIND[e][r] == NOW]
-            if e == LAST:
-                for r in now:
-                    if r % 2 == 0:
-                        nc.scalar.copy(out=first_y[:, r : r + 2, :], in_=banks_y[r // 2][:])
-                    scatter(e, r, first_y[:, r, :])
-                    nc.sync.dma_start(out=out[r * P : (r + 1) * P, :], in_=windows[r][:])
+            if e < LAST:
+                now = [r for r in range(BLOCKS) if GATE_AT[e][r] == NOW]
+                leave(e, now, banks_y, free_y[:, BLOCKS:, :])
             else:
-                for r in now:
-                    y = banks_y[r // 2][:, r % 2, :]
-                    nc.vector.tensor_tensor(first_y[:, r, :], y, gates[:, e * C : (e + 1) * C], ALU.mult)
-                for r in now:
-                    nc.vector.tensor_copy(places(e, r), first_y[:, r, :])
+                weight = gates[:, e * C : (e + 1) * C]
+                for pair in range(BLOCKS // 2):
+                    both = [2 * pair, 2 * pair + 1]
+                    for r in both:
+                        if r in TAIL_ON_VECTOR:
+                            nc.scalar.copy(out=free_y[:, r, :], in_=sums[r])
+                        else:
+                            nc.vector.tensor_tensor(free_y[:, r, :], sums[r], weight, ALU.mult)
+                    for r in both:
+                        if r in TAIL_ON_VECTOR:
+                            nc.vector.tensor_tensor(places(e, r), free_y[:, r, :], weight, ALU.mult)
+                        else:
+                            nc.scalar.activation(places(e, r), free_y[:, r, :], COPY)
+                        nc.sync.dma_start(out=out[r * P : (r + 1) * P, :], in_=windows[r][:])

@@ -35,17 +35,24 @@ GATE_COLS = SLOTS // P
 
 W3_LO, W3_HI, W1_LO, W1_HI, W2 = range(5)
 PIECES = 5
-NOW, MID, END = -1, 0, 1
+NOW, BACK, MID, END, AFTER = -1, -2, 0, 1, 2
 
-SCALAR_OCTETS = [[64,64,0,24,64],[64,0,0,0,0],[64,0,0,0,0],[64,0,0,0,0]]
-GATE_AT = [[NOW,[W3_HI,END],[W1_LO,END],[W1_HI,END]],[NOW,[W3_HI,END],[W1_LO,END],[W1_HI,END]],[NOW,[W3_HI,END],[W1_LO,END],[W1_HI,END]]]
+SCALAR_OCTETS = [[64,64,0,24,64],[64,0,0,0,0],[64,0,0,0,0],[64,0,0,24,64]]
+GATE_AT = [[NOW,[W3_HI,END],[W1_LO,END],[W1_HI,END]],[NOW,[W3_HI,END],[W1_LO,END],[W1_HI,END]],[NOW,[W3_HI,END],[W1_HI,END],[W1_HI,AFTER]]]
 B_HELD = [1,0,0,0]
-TAIL_ON_VECTOR = [0,2]
+TAIL_ON_VECTOR = [1,2]
 W2_HALVES = [0,1,2,3]
 HI_CALLS = [1,1,1,1]
 
-H_HELD = [1,2,3]
-RAW_BUFS = 12
+H_HELD = [1,2]
+STORE_ORDER = [0,1,2,3]
+KEPT = [[],[],[3]]
+Q_HELD = []
+SEAT = [0,1,2,3]
+SCALAR_LAST = [[3,3]]
+FIRST = 8
+LEAD = 512 - 8 * FIRST
+RAW_BUFS = 9
 ROUNDED_BUFS = 5
 CODED_BUFS = 6
 
@@ -74,11 +81,19 @@ def tile_moe_two_glu_relu_kernel(
         gate_cols = keep.tile([P, GATE_COLS], F32, name="gate_cols")
         gates = keep.tile([P, SLOTS], F32, name="gates")
         identity = keep.tile([P, P], F32, name="identity")
-        free_y = keep.tile([P, 2 * BLOCKS, C], F32, name="free_y")
+        free_y = keep.tile([P, BLOCKS, C], F32, name="free_y")
+        kept_y = keep.tile([P, BLOCKS, C], F32, name="kept_y")
         windows = [keep.tile([P, T], F32, name=f"window{r}") for r in range(BLOCKS)]
 
+        leads = []
+
         def load_piece(e, piece):
-            room = raws.tile([P, PACK * H], F32, name="raw", align_bytes=64)
+            if piece == W2:
+                whole = keep.tile([P, LEAD + PACK * H], F32, name=f"raw_w2_{e}", align_bytes=64)
+                leads.append(whole)
+                room = whole[:, LEAD:]
+            else:
+                room = raws.tile([P, PACK * H], F32, name="raw", align_bytes=64)
             raw = room[:].rearrange("p (j c) -> p j c", j=PACK)
             if piece == W2:
                 rows = w2[e].rearrange("(g j b) c -> b g j c", j=PACK, b=PAIR)
@@ -107,8 +122,8 @@ def tile_moe_two_glu_relu_kernel(
                 in_=grouped[:, PACK * first : PACK * end],
             )
 
-        def first_layer_pass(e, o, banks, codes, scales):
-            for half, j in product(range(HALVES), range(PACK)):
+        def first_layer_pass(e, o, banks, codes, scales, groups):
+            for half, j in product(reversed(range(HALVES)), groups):
                 slots = slice(e * C + half * HALF, e * C + (half + 1) * HALF)
                 cols = slice(j * P, (j + 1) * P)
                 nc.tensor.matmul_mx(
@@ -124,28 +139,31 @@ def tile_moe_two_glu_relu_kernel(
         def rows_of(raw):
             return raw[:].rearrange("p (k c) -> p k c", k=PACK)
 
+        spares = []
+
         def copy_b(banks, raw, held):
-            result = []
-            for half in range(HALVES):
-                if half < held:
-                    room = rows_of(raw)[:, :, half * HALF : (half + 1) * HALF]
+            result = {}
+            for half in reversed(range(HALVES)):
+                if half >= HALVES - held:
+                    room = rows_of(raw)[:, :, (1 - half) * HALF : (2 - half) * HALF]
                 else:
-                    spare = hidden.tile([P, PACK * HALF], F32, name=f"b_free{half}")
+                    spare = hidden.tile([P, PACK * HALF], F32, name=f"b_free{half}", align_bytes=64)
+                    spares.append(spare)
                     room = rows_of(spare)
                 room = room.rearrange("p a (s j) -> p a s j", j=PACK)
                 nc.scalar.copy(out=room, in_=banks[half][:].rearrange("p j (a s) -> p a s j", a=PACK))
-                result.append(room)
+                result[half] = room
             return result
 
-        def make_h(banks_a, b_rooms, raw):
-            if raw is None:
-                own = hidden.tile([P, HALVES, HALF * PACK], BF16, name="h", align_bytes=64)
-                h = [own[:, half, :] for half in range(HALVES)]
+        def make_h(banks_a, b_rooms, whole):
+            if whole is None:
+                own = hidden.tile([P, C * PACK], BF16, name="h", align_bytes=64)
+                h = own[:]
             else:
-                h = [raw[:, half * H : half * H + C].bitcast(BF16) for half in range(HALVES)]
-            for half in range(HALVES):
+                h = whole[:, : 2 * C].bitcast(BF16)
+            for half in reversed(range(HALVES)):
                 nc.vector.scalar_tensor_tensor(
-                    out=h[half].rearrange("p (a s j) -> p a s j", a=PACK, j=PACK),
+                    out=h[:, half * H : (half + 1) * H].rearrange("p (a s j) -> p a s j", a=PACK, j=PACK),
                     in0=banks_a[half][:].rearrange("p j (a s) -> p a s j", a=PACK),
                     scalar=0.0,
                     in1=b_rooms[half],
@@ -154,12 +172,11 @@ def tile_moe_two_glu_relu_kernel(
                 )
             return h
 
-        def quantize_h(h):
+        def quantize_h(h, calls):
             h_codes = hidden.tile([P, C], U32, name="h_codes", align_bytes=64)
             h_scales = hidden.tile([P, C], U8, name="h_scales", align_bytes=64)
-            for half in range(HALVES):
-                cols = slice(half * HALF, (half + 1) * HALF)
-                nc.vector.quantize_mx(out=h_codes[:, cols].bitcast(FP8X4), scales=h_scales[:, cols], in_=h[half])
+            for call in reversed(range(calls)):
+                quantize(h, h_codes, h_scales, call * C // calls, (call + 1) * C // calls)
             return h_codes, h_scales
 
         def places(e, r):
@@ -169,15 +186,19 @@ def tile_moe_two_glu_relu_kernel(
             weight = gates[:, e * C : (e + 1) * C].unsqueeze(1).to_broadcast([P, count, C])
             nc.vector.tensor_tensor(into, y, weight, ALU.mult)
 
-        def leave(e, due, banks, rooms):
+        def leave(e, due, banks, rooms, backlog):
+            due = sorted(due, key=lambda r: SEAT[r])
             for pair in range(BLOCKS // 2):
-                both = [r for r in due if r // 2 == pair]
+                both = [r for r in due if SEAT[r] // 2 == pair]
                 if both:
                     row = due.index(both[0])
-                    y = banks[pair][:, both[0] % 2 : both[-1] % 2 + 1, :]
+                    y = banks[pair][:, SEAT[both[0]] % 2 : SEAT[both[-1]] % 2 + 1, :]
                     gate_blocks(e, y, rooms[:, row : row + len(both), :], len(both))
                     for n, r in enumerate(both):
-                        nc.scalar.activation(places(e, r), rooms[:, row + n, :], COPY)
+                        if r in KEPT[e]:
+                            backlog[e, r] = rooms[:, row + n, :]
+                        else:
+                            nc.scalar.activation(places(e, r), rooms[:, row + n, :], COPY)
 
         nc.vector.memset(token_scales[:].bitcast(I32), 0)
         nc.vector.memset(windows[0][:], 0.0)
@@ -221,50 +242,66 @@ def tile_moe_two_glu_relu_kernel(
             )
 
         banks_y = []
+        backlog = {}
+        waiting = None
         for e in range(E):
             for piece in range(PIECES):
                 grouped = rounded.tile([P, PACK * H], BF16, name="grouped", align_bytes=64)
                 codes = coded.tile([P, H], U32, name="codes", align_bytes=64)
-                scales = coded.tile([P, H], U8, name="scales", align_bytes=64)
                 here = raw[e][piece]
+                if [e, piece] in Q_HELD:
+                    scales = raw[e][piece + 1][:, 3 * H : 3 * H + H // 4].bitcast(U8)
+                else:
+                    scales = coded.tile([P, H], U8, name="scales", align_bytes=64)
                 mid = [r for r in range(BLOCKS) if e > 0 and GATE_AT[e - 1][r] == [piece, MID]]
                 end = [r for r in range(BLOCKS) if e > 0 and GATE_AT[e - 1][r] == [piece, END]]
+                after = [r for r in range(BLOCKS) if e > 0 and GATE_AT[e - 1][r] == [piece, AFTER]]
                 share = SCALAR_OCTETS[e][piece]
-                halved = len(mid) + len(end) > 0 or (piece == W2 and (e in W2_HALVES or e in H_HELD)) or (piece == W1_HI and B_HELD[e] > 0 and share > 32)
-                edges = sorted(set([0, share, OCTETS] + ([OCTETS // 2] if halved else [])))
+                halved = len(mid) + len(end) + len(after) > 0 or [e, piece - 1] in Q_HELD or (piece == W2 and (e in W2_HALVES or e in H_HELD)) or (piece == W1_HI and B_HELD[e] > 0 and share > 32)
+                late = [e, piece] in SCALAR_LAST
+                edges = sorted(set([0, OCTETS - share if late else share, OCTETS] + ([OCTETS // 2] if halved else []) + ([FIRST] if piece == W2 and e in H_HELD else []) + ([OCTETS // 4] if piece == W2 and e == LAST else [])))
                 rooms = rows_of(here)[:, :, :C]
                 for first, stop in zip(edges, edges[1:]):
-                    round_part(here, grouped, piece != W2, first, stop, stop <= share)
+                    round_part(here, grouped, piece != W2, first, stop, first >= OCTETS - share if late else stop <= share)
                     if stop == OCTETS // 2:
-                        leave(e - 1, mid, banks_y, rooms)
+                        leave(e - 1, mid, banks_y, rooms, backlog)
                         if piece == W2 and e in H_HELD:
-                            h = make_h(banks_a, b_rooms, here)
-                if piece == W2 and e in H_HELD:
-                    h_codes, h_scales = quantize_h(h)
-                leave(e - 1, end, banks_y, rooms[:, len(mid) :, :])
+                            h = make_h(banks_a, b_rooms, leads[e])
+                leave(e - 1, end, banks_y, rooms[:, len(mid) :, :], backlog)
                 if piece == W1_HI:
                     b_rooms = copy_b(banks_b, here, B_HELD[e])
-                calls = 2 if (piece == W2 and e in W2_HALVES) else (HI_CALLS[e] if piece == W1_HI else 1)
-                for call in range(calls):
-                    quantize(grouped, codes, scales, call * H // calls, (call + 1) * H // calls)
                 if piece == W3_LO:
                     banks_b = [psum_b.tile([P, PACK, HALF], F32, name="bank") for half in range(HALVES)]
                 if piece == W1_LO:
                     banks_a = [psum_a.tile([P, PACK, HALF], F32, name="bank") for half in range(HALVES)]
-                if piece in (W3_LO, W3_HI):
-                    first_layer_pass(e, piece - W3_LO, banks_b, codes, scales)
-                if piece in (W1_LO, W1_HI):
-                    first_layer_pass(e, piece - W1_LO, banks_a, codes, scales)
+                ready = [] if waiting is None else [waiting]
+                waiting = None
+                if [e, piece] in Q_HELD:
+                    waiting = (piece, grouped, codes, scales)
+                else:
+                    ready.append((piece, grouped, codes, scales))
+                for done, its_values, its_codes, its_scales in ready:
+                    calls = 2 if (done == W2 and e in W2_HALVES) else (HI_CALLS[e] if done == W1_HI else 1)
+                    cuts = [0, P, 2 * P, H] if done == W2 and e == LAST else [call * H // calls for call in range(calls + 1)]
+                    for call in range(len(cuts) - 1):
+                        quantize(its_values, its_codes, its_scales, cuts[call], cuts[call + 1])
+                        if done == W2 and e in H_HELD and call == 0:
+                            h_codes, h_scales = quantize_h(h, 1)
+                        groups = range(call * PACK // calls, (call + 1) * PACK // calls)
+                        if done in (W3_LO, W3_HI):
+                            first_layer_pass(e, done - W3_LO, banks_b, its_codes, its_scales, groups)
+                        if done in (W1_LO, W1_HI):
+                            first_layer_pass(e, done - W1_LO, banks_a, its_codes, its_scales, groups)
+                leave(e - 1, after, banks_y, rooms[:, len(mid) + len(end) :, :], backlog)
                 if piece == W1_HI and e not in H_HELD:
-                    h_codes, h_scales = quantize_h(make_h(banks_a, b_rooms, None))
+                    h_codes, h_scales = quantize_h(make_h(banks_a, b_rooms, None), HALVES)
 
-            if e < LAST:
-                banks_y = [psum_y.tile([P, 2, C], F32, name="bank_y") for pair in range(BLOCKS // 2)]
-                sums = [banks_y[r // 2][:, r % 2, :] for r in range(BLOCKS)]
-            else:
-                own = [psum_y.tile([P, C], F32, name="bank_y") for r in range(2)]
-                own = own + [psum_b.tile([P, C], F32, name="bank") for r in range(2)]
-                sums = [bank[:] for bank in own]
+            banks_y = [psum_y.tile([P, 2, C], F32, name="bank_y") for pair in range(BLOCKS // 2)]
+            seats = SEAT if e < LAST else list(range(BLOCKS))
+            sums = [banks_y[seats[r] // 2][:, seats[r] % 2, :] for r in range(BLOCKS)]
+            if e == LAST:
+                alone = psum_y.tile([P, 2, C], F32, name="bank_y")
+                sums[1] = alone[:, 0, :]
             for r in range(BLOCKS):
                 cols = slice(r * P, (r + 1) * P)
                 nc.tensor.matmul_mx(
@@ -278,20 +315,24 @@ def tile_moe_two_glu_relu_kernel(
                 )
 
             if e < LAST:
+                for r in range(BLOCKS):
+                    if GATE_AT[e][r] == BACK:
+                        row = e * BLOCKS + r
+                        gate_blocks(e, banks_y[SEAT[r] // 2][:, SEAT[r] % 2 : SEAT[r] % 2 + 1, :], kept_y[:, row : row + 1, :], 1)
+                        backlog[e, r] = kept_y[:, row, :]
                 now = [r for r in range(BLOCKS) if GATE_AT[e][r] == NOW]
-                leave(e, now, banks_y, free_y[:, BLOCKS:, :])
+                leave(e, now, banks_y, free_y[:], backlog)
             else:
-                weight = gates[:, e * C : (e + 1) * C]
-                for pair in range(BLOCKS // 2):
-                    both = [2 * pair, 2 * pair + 1]
-                    for r in both:
-                        if r in TAIL_ON_VECTOR:
-                            nc.scalar.copy(out=free_y[:, r, :], in_=sums[r])
-                        else:
-                            nc.vector.tensor_tensor(free_y[:, r, :], sums[r], weight, ALU.mult)
-                    for r in both:
-                        if r in TAIL_ON_VECTOR:
-                            nc.vector.tensor_tensor(places(e, r), free_y[:, r, :], weight, ALU.mult)
-                        else:
-                            nc.scalar.activation(places(e, r), free_y[:, r, :], COPY)
-                        nc.sync.dma_start(out=out[r * P : (r + 1) * P, :], in_=windows[r][:])
+                leaving = [([0], banks_y[0][:, 0:1, :]), ([1], alone[:, 0:1, :]), ([2, 3], banks_y[1][:])]
+                for blocks, y in leaving:
+                    gate_blocks(e, y, kept_y[:, blocks[0] : blocks[-1] + 1, :], len(blocks))
+                    for r in blocks:
+                        for source in range(LAST, -1, -1):
+                            if source == LAST or (source, r) in backlog:
+                                gated = kept_y[:, r, :] if source == LAST else backlog[source, r]
+                                if r in TAIL_ON_VECTOR:
+                                    nc.vector.tensor_copy(places(source, r), gated)
+                                else:
+                                    nc.scalar.activation(places(source, r), gated, COPY)
+                for r in STORE_ORDER:
+                    nc.sync.dma_start(out=out[r * P : (r + 1) * P, :], in_=windows[r][:])

@@ -35,26 +35,24 @@ GATE_COLS = SLOTS // P
 
 W3_LO, W3_HI, W1_LO, W1_HI, W2 = range(5)
 PIECES = 5
-NOW, BACK, MID, END, AFTER = -1, -2, 0, 1, 2
+S, V, G = 0, 1, 2
+NOW, END, AFTER = -1, 1, 2
 
-SCALAR_OCTETS = [[64,64,0,24,64],[64,0,0,0,0],[64,0,0,0,0],[64,0,0,24,64]]
-GATE_AT = [[NOW,[W3_HI,END],[W1_LO,END],[W1_HI,END]],[NOW,[W3_HI,END],[W1_LO,END],[W1_HI,END]],[NOW,[W3_HI,END],[W1_HI,END],[W1_HI,AFTER]]]
-B_HELD = [1,0,0,0]
-TAIL_ON_VECTOR = [1,2]
-W2_HALVES = [0,1,2,3]
-HI_CALLS = [1,1,1,1]
-
-H_HELD = [1,2]
-STORE_ORDER = [0,1,2,3]
+PARTS = [[[[0,64,S]],[[0,64,S]],[[0,64,V]],[[0,24,S],[24,64,V]],[[0,32,S],[32,64,S]]],[[[0,32,S],[32,64,S]],[[0,32,V],[32,64,V]],[[0,32,V],[32,64,V]],[[0,32,V],[32,64,V]],[[0,8,V],[8,32,V],[32,64,V]]],[[[0,32,S],[32,64,S]],[[0,32,V],[32,64,V]],[[0,32,V],[32,64,V]],[[0,32,V],[32,64,V]],[[0,8,V],[8,32,V],[32,64,V]]],[[[0,32,S],[32,64,S]],[[0,32,V],[32,64,V]],[[0,64,V]],[[0,32,V],[32,40,V],[40,64,S]],[[0,16,S],[16,32,S],[32,64,S]]]]
+GATE_AT = [[[W3_LO,END],[W3_HI,END],[W1_LO,END],[W1_HI,END]],[[W3_LO,END],[W3_HI,END],[W1_LO,END],[W1_HI,END]],[[W3_LO,END],[W3_HI,END],[W1_HI,END],[W1_HI,AFTER]]]
 KEPT = [[],[],[3]]
-Q_HELD = []
-SEAT = [0,1,2,3]
-SCALAR_LAST = [[3,3]]
-FIRST = 8
-LEAD = 512 - 8 * FIRST
-RAW_BUFS = 9
-ROUNDED_BUFS = 5
-CODED_BUFS = 6
+B_HELD = [1,0,0,0]
+H_HELD = [1,2]
+H_BEHIND = [0,1,1,0]
+JOINED = [[1,1],[2,1]]
+CUTS = [[[512],[512],[512],[512],[256,512]],[[512],[512],[512],[512],[256,512]],[[512],[512],[512],[512],[256,512]],[[512],[512],[512],[256,512],[128,256,512]]]
+H_CALLS = [2,1,1,2]
+LAST_BANKS = [[0],[1],[2],[3]]
+TAIL_ON_VECTOR = [0,2]
+STORE_ORDER = [0,1,2,3]
+ROOMS_RIGHT = []
+LEAD = 2 * C - 64
+RAW_BUFS = 8
 
 
 def tile_moe_two_glu_relu_kernel(
@@ -65,9 +63,10 @@ def tile_moe_two_glu_relu_kernel(
     with ExitStack() as ctx:
         keep = ctx.enter_context(tc.tile_pool(name="keep", bufs=1))
         raws = ctx.enter_context(tc.tile_pool(name="raws", bufs=RAW_BUFS))
-        rounded = ctx.enter_context(tc.tile_pool(name="rounded", bufs=ROUNDED_BUFS))
-        coded = ctx.enter_context(tc.tile_pool(name="coded", bufs=CODED_BUFS))
+        rounded = ctx.enter_context(tc.tile_pool(name="rounded", bufs=2))
+        coded = ctx.enter_context(tc.tile_pool(name="coded", bufs=2))
         hidden = ctx.enter_context(tc.tile_pool(name="hidden", bufs=2))
+        once = ctx.enter_context(tc.tile_pool(name="once", bufs=1))
         psum_a = ctx.enter_context(tc.psum_pool(name="psum_a", bufs=HALVES))
         psum_b = ctx.enter_context(tc.psum_pool(name="psum_b", bufs=HALVES))
         psum_y = ctx.enter_context(tc.psum_pool(name="psum_y", bufs=BLOCKS))
@@ -81,39 +80,51 @@ def tile_moe_two_glu_relu_kernel(
         gate_cols = keep.tile([P, GATE_COLS], F32, name="gate_cols")
         gates = keep.tile([P, SLOTS], F32, name="gates")
         identity = keep.tile([P, P], F32, name="identity")
-        free_y = keep.tile([P, BLOCKS, C], F32, name="free_y")
-        kept_y = keep.tile([P, BLOCKS, C], F32, name="kept_y")
+        free_y = keep.tile([P, 2, C], F32, name="free_y")
+        last_y = keep.tile([P, BLOCKS, C], F32, name="last_y")
         windows = [keep.tile([P, T], F32, name=f"window{r}") for r in range(BLOCKS)]
-
-        leads = []
+        w2_tiles = [keep.tile([P, LEAD + PACK * H], F32, name=f"raw_w2_{e}", align_bytes=64) for e in range(E)]
 
         def load_piece(e, piece):
             if piece == W2:
-                whole = keep.tile([P, LEAD + PACK * H], F32, name=f"raw_w2_{e}", align_bytes=64)
-                leads.append(whole)
-                room = whole[:, LEAD:]
-            else:
-                room = raws.tile([P, PACK * H], F32, name="raw", align_bytes=64)
-            raw = room[:].rearrange("p (j c) -> p j c", j=PACK)
-            if piece == W2:
+                room = w2_tiles[e][:, LEAD:]
+                raw = room.rearrange("p (j c) -> p j c", j=PACK)
                 rows = w2[e].rearrange("(g j b) c -> b g j c", j=PACK, b=PAIR)
                 for b in range(PAIR):
                     nc.sync.dma_start(out=raw[b:P:PAIR], in_=rows[b])
             else:
+                tile = raws.tile([P, PACK * H], F32, name="raw")
+                room = tile[:]
                 w = w3 if piece in (W3_LO, W3_HI) else w1
                 o = 0 if piece in (W3_LO, W1_LO) else 1
                 rows = w[e, o * K_PASS : (o + 1) * K_PASS, :]
-                nc.sync.dma_start(out=raw, in_=rows.rearrange("(p j) c -> p j c", j=PACK))
+                nc.sync.dma_start(out=room, in_=rows.rearrange("(p j) c -> p (j c)", j=PACK))
             return room
 
-        def round_part(raw, grouped, first_layer, first, end, on_scalar):
-            src = raw[:].rearrange("p (k g j b) -> p g j k b", k=PACK, j=PACK, b=PAIR)
+        def round_part(raw, grouped, first_layer, first, end, engine):
+            src = raw.rearrange("p (k g j b) -> p g j k b", k=PACK, j=PACK, b=PAIR)
             layout = "p (j g b k) -> p g j k b" if first_layer else "p (g j b k) -> p g j k b"
-            into = grouped[:].rearrange(layout, j=PACK, b=PAIR, k=PACK)
-            if on_scalar:
+            into = grouped.rearrange(layout, j=PACK, b=PAIR, k=PACK)
+            if engine == S:
                 nc.scalar.copy(out=into[:, first:end], in_=src[:, first:end])
-            else:
+            elif engine == V:
                 nc.vector.tensor_copy(out=into[:, first:end], in_=src[:, first:end])
+            else:
+                columns = slice(8 * first, 8 * end)
+                nc.gpsimd.tensor_scalar(
+                    grouped.rearrange("p (c k) -> p c k", k=PACK)[:, columns],
+                    raw.rearrange("p (k c) -> p c k", k=PACK)[:, columns],
+                    1.0,
+                    0.0,
+                    ALU.mult,
+                    ALU.add,
+                )
+
+        def new_matrix(name, passes):
+            grouped = rounded.tile([P, passes * PACK * H], BF16, name=f"grouped_{name}", align_bytes=64)
+            codes = coded.tile([P, passes * H], U32, name=f"codes_{name}", align_bytes=64)
+            scales = coded.tile([P, passes * H], U8, name=f"scales_{name}", align_bytes=64)
+            return grouped, codes, scales
 
         def quantize(grouped, codes, scales, first, end):
             nc.vector.quantize_mx(
@@ -125,7 +136,7 @@ def tile_moe_two_glu_relu_kernel(
         def first_layer_pass(e, o, banks, codes, scales, groups):
             for half, j in product(reversed(range(HALVES)), groups):
                 slots = slice(e * C + half * HALF, e * C + (half + 1) * HALF)
-                cols = slice(j * P, (j + 1) * P)
+                cols = slice(o * H + j * P, o * H + (j + 1) * P)
                 nc.tensor.matmul_mx(
                     out=banks[half][:, j, :],
                     lhsT=codes[:, cols].bitcast(FP8X4),
@@ -137,9 +148,7 @@ def tile_moe_two_glu_relu_kernel(
                 )
 
         def rows_of(raw):
-            return raw[:].rearrange("p (k c) -> p k c", k=PACK)
-
-        spares = []
+            return raw.rearrange("p (k c) -> p k c", k=PACK)
 
         def copy_b(banks, raw, held):
             result = {}
@@ -147,20 +156,14 @@ def tile_moe_two_glu_relu_kernel(
                 if half >= HALVES - held:
                     room = rows_of(raw)[:, :, (1 - half) * HALF : (2 - half) * HALF]
                 else:
-                    spare = hidden.tile([P, PACK * HALF], F32, name=f"b_free{half}", align_bytes=64)
-                    spares.append(spare)
-                    room = rows_of(spare)
+                    spare = once.tile([P, PACK * HALF], F32, name=f"b_free{half}")
+                    room = rows_of(spare[:])
                 room = room.rearrange("p a (s j) -> p a s j", j=PACK)
                 nc.scalar.copy(out=room, in_=banks[half][:].rearrange("p j (a s) -> p a s j", a=PACK))
                 result[half] = room
             return result
 
-        def make_h(banks_a, b_rooms, whole):
-            if whole is None:
-                own = hidden.tile([P, C * PACK], BF16, name="h", align_bytes=64)
-                h = own[:]
-            else:
-                h = whole[:, : 2 * C].bitcast(BF16)
+        def make_h(banks_a, b_rooms, h):
             for half in reversed(range(HALVES)):
                 nc.vector.scalar_tensor_tensor(
                     out=h[:, half * H : (half + 1) * H].rearrange("p (a s j) -> p a s j", a=PACK, j=PACK),
@@ -170,7 +173,6 @@ def tile_moe_two_glu_relu_kernel(
                     op0=ALU.max,
                     op1=ALU.mult,
                 )
-            return h
 
         def quantize_h(h, calls):
             h_codes = hidden.tile([P, C], U32, name="h_codes", align_bytes=64)
@@ -187,12 +189,11 @@ def tile_moe_two_glu_relu_kernel(
             nc.vector.tensor_tensor(into, y, weight, ALU.mult)
 
         def leave(e, due, banks, rooms, backlog):
-            due = sorted(due, key=lambda r: SEAT[r])
             for pair in range(BLOCKS // 2):
-                both = [r for r in due if SEAT[r] // 2 == pair]
+                both = [r for r in due if r // 2 == pair]
                 if both:
                     row = due.index(both[0])
-                    y = banks[pair][:, SEAT[both[0]] % 2 : SEAT[both[-1]] % 2 + 1, :]
+                    y = banks[pair][:, both[0] % 2 : both[-1] % 2 + 1, :]
                     gate_blocks(e, y, rooms[:, row : row + len(both), :], len(both))
                     for n, r in enumerate(both):
                         if r in KEPT[e]:
@@ -213,99 +214,91 @@ def tile_moe_two_glu_relu_kernel(
             if o == 0:
                 nc.sync.dma_start(offs_sb[:], offs)
                 for q in range(P // QUADRANT):
-                    nc.scalar.dma_start(
+                    nc.sync.dma_start(
                         out=token_scales[QUADRANT * q : QUADRANT * q + SCALE_ROWS * PASSES, :].bitcast(I32),
                         in_=x_scales[:, SCALE_ROWS * q : SCALE_ROWS * (q + 1), :].bitcast(I32),
                     )
-        nc.sync.dma_start(out=gate_cols[:], in_=gate[0, :].rearrange("(p c) -> p c", c=GATE_COLS))
 
         raw = []
         for e in range(E):
             raw.append({})
             for piece in range(PIECES):
                 raw[e][piece] = load_piece(e, piece)
+                if e == 0 and piece == W3_LO:
+                    nc.sync.dma_start(out=gate_cols[:], in_=gate[0, :].rearrange("(p c) -> p c", c=GATE_COLS))
                 if e == 0 and piece == W1_HI:
                     nc.sync.dma_start(dst_sb[:], dst)
 
         for o in range(PASSES):
             nc.vector.tensor_copy(slot_words[o][:], token_words[o][:].bitcast(U32).indirect(offs_sb[:]))
-        nc.vector.tensor_copy(slot_scales[:], token_scales[:].indirect(offs_sb[:]))
+            if o == 0:
+                nc.vector.tensor_copy(slot_scales[:], token_scales[:].indirect(offs_sb[:]))
 
         for group in range(GATE_COLS // 4):
             spread = psum_y.tile([P, 4, P], F32, name="bank_y")
             for c in range(4):
                 col = 4 * group + c
                 nc.tensor.transpose(spread[:, c, :], gate_cols[:, col : col + 1].to_broadcast([P, P]), identity[:])
-            nc.scalar.copy(
+            nc.vector.tensor_copy(
                 out=gates[:].rearrange("p (s c) -> p s c", c=GATE_COLS)[:, :, 4 * group : 4 * group + 4],
                 in_=spread[:].rearrange("p c s -> p s c"),
             )
 
         banks_y = []
         backlog = {}
-        waiting = None
         for e in range(E):
+            matrices = [new_matrix("w3", PASSES), new_matrix("w1", PASSES), new_matrix("w2", 1)]
+            banks_b = [psum_b.tile([P, PACK, HALF], F32, name="bank") for half in range(HALVES)]
+            banks_a = [psum_a.tile([P, PACK, HALF], F32, name="bank") for half in range(HALVES)]
+            if e in H_HELD:
+                h = w2_tiles[e][:, : 2 * C].bitcast(BF16)
+            else:
+                own = hidden.tile([P, C * PACK], BF16, name="h", align_bytes=64)
+                h = own[:]
             for piece in range(PIECES):
-                grouped = rounded.tile([P, PACK * H], BF16, name="grouped", align_bytes=64)
-                codes = coded.tile([P, H], U32, name="codes", align_bytes=64)
+                grouped, codes, scales = matrices[piece // 2]
+                o = piece % 2
                 here = raw[e][piece]
-                if [e, piece] in Q_HELD:
-                    scales = raw[e][piece + 1][:, 3 * H : 3 * H + H // 4].bitcast(U8)
-                else:
-                    scales = coded.tile([P, H], U8, name="scales", align_bytes=64)
-                mid = [r for r in range(BLOCKS) if e > 0 and GATE_AT[e - 1][r] == [piece, MID]]
                 end = [r for r in range(BLOCKS) if e > 0 and GATE_AT[e - 1][r] == [piece, END]]
                 after = [r for r in range(BLOCKS) if e > 0 and GATE_AT[e - 1][r] == [piece, AFTER]]
-                share = SCALAR_OCTETS[e][piece]
-                halved = len(mid) + len(end) + len(after) > 0 or [e, piece - 1] in Q_HELD or (piece == W2 and (e in W2_HALVES or e in H_HELD)) or (piece == W1_HI and B_HELD[e] > 0 and share > 32)
-                late = [e, piece] in SCALAR_LAST
-                edges = sorted(set([0, OCTETS - share if late else share, OCTETS] + ([OCTETS // 2] if halved else []) + ([FIRST] if piece == W2 and e in H_HELD else []) + ([OCTETS // 4] if piece == W2 and e == LAST else [])))
-                rooms = rows_of(here)[:, :, :C]
-                for first, stop in zip(edges, edges[1:]):
-                    round_part(here, grouped, piece != W2, first, stop, first >= OCTETS - share if late else stop <= share)
-                    if stop == OCTETS // 2:
-                        leave(e - 1, mid, banks_y, rooms, backlog)
-                        if piece == W2 and e in H_HELD:
-                            h = make_h(banks_a, b_rooms, leads[e])
-                leave(e - 1, end, banks_y, rooms[:, len(mid) :, :], backlog)
+                rooms = rows_of(here)[:, :, C:] if [e, piece] in ROOMS_RIGHT else rows_of(here)[:, :, :C]
+                for n, (first, stop, engine) in enumerate(PARTS[e][piece]):
+                    round_part(here, grouped[:, o * PACK * H : (o + 1) * PACK * H], piece != W2, first, stop, engine)
+                    if piece == W2 and e in H_HELD and n == H_BEHIND[e]:
+                        make_h(banks_a, b_rooms, h)
+                leave(e - 1, end, banks_y, rooms, backlog)
                 if piece == W1_HI:
                     b_rooms = copy_b(banks_b, here, B_HELD[e])
-                if piece == W3_LO:
-                    banks_b = [psum_b.tile([P, PACK, HALF], F32, name="bank") for half in range(HALVES)]
-                if piece == W1_LO:
-                    banks_a = [psum_a.tile([P, PACK, HALF], F32, name="bank") for half in range(HALVES)]
-                ready = [] if waiting is None else [waiting]
-                waiting = None
-                if [e, piece] in Q_HELD:
-                    waiting = (piece, grouped, codes, scales)
+                banks = banks_b if piece < W1_LO else banks_a
+                if [e, piece + 1] in JOINED:
+                    cuts = []
+                elif [e, piece] in JOINED:
+                    quantize(grouped, codes, scales, 0, PASSES * H)
+                    for both in range(PASSES):
+                        first_layer_pass(e, both, banks, codes, scales, range(PACK))
+                    cuts = []
                 else:
-                    ready.append((piece, grouped, codes, scales))
-                for done, its_values, its_codes, its_scales in ready:
-                    calls = 2 if (done == W2 and e in W2_HALVES) else (HI_CALLS[e] if done == W1_HI else 1)
-                    cuts = [0, P, 2 * P, H] if done == W2 and e == LAST else [call * H // calls for call in range(calls + 1)]
-                    for call in range(len(cuts) - 1):
-                        quantize(its_values, its_codes, its_scales, cuts[call], cuts[call + 1])
-                        if done == W2 and e in H_HELD and call == 0:
-                            h_codes, h_scales = quantize_h(h, 1)
-                        groups = range(call * PACK // calls, (call + 1) * PACK // calls)
-                        if done in (W3_LO, W3_HI):
-                            first_layer_pass(e, done - W3_LO, banks_b, its_codes, its_scales, groups)
-                        if done in (W1_LO, W1_HI):
-                            first_layer_pass(e, done - W1_LO, banks_a, its_codes, its_scales, groups)
-                leave(e - 1, after, banks_y, rooms[:, len(mid) + len(end) :, :], backlog)
+                    cuts = CUTS[e][piece]
+                first = 0
+                for stop in cuts:
+                    quantize(grouped, codes, scales, o * H + first, o * H + stop)
+                    if piece == W2 and e in H_HELD and first == 0:
+                        h_codes, h_scales = quantize_h(h, H_CALLS[e])
+                    if piece != W2:
+                        first_layer_pass(e, o, banks, codes, scales, range(first // P, stop // P))
+                    first = stop
+                leave(e - 1, after, banks_y, rooms[:, len(end) :, :], backlog)
                 if piece == W1_HI and e not in H_HELD:
-                    h_codes, h_scales = quantize_h(make_h(banks_a, b_rooms, None), HALVES)
+                    make_h(banks_a, b_rooms, h)
+                    h_codes, h_scales = quantize_h(h, H_CALLS[e])
 
-            banks_y = [psum_y.tile([P, 2, C], F32, name="bank_y") for pair in range(BLOCKS // 2)]
-            seats = SEAT if e < LAST else list(range(BLOCKS))
-            sums = [banks_y[seats[r] // 2][:, seats[r] % 2, :] for r in range(BLOCKS)]
-            if e == LAST:
-                alone = psum_y.tile([P, 2, C], F32, name="bank_y")
-                sums[1] = alone[:, 0, :]
+            seating = [[0, 1], [2, 3]] if e < LAST else LAST_BANKS
+            banks_y = [psum_y.tile([P, 2, C], F32, name="bank_y") for blocks in seating]
             for r in range(BLOCKS):
+                bank = [n for n, blocks in enumerate(seating) if r in blocks][0]
                 cols = slice(r * P, (r + 1) * P)
                 nc.tensor.matmul_mx(
-                    out=sums[r],
+                    out=banks_y[bank][:, seating[bank].index(r), :],
                     lhsT=codes[:, cols].bitcast(FP8X4),
                     lhsT_scale=scales[:, cols],
                     rhs=h_codes[:].bitcast(FP8X4),
@@ -315,24 +308,23 @@ def tile_moe_two_glu_relu_kernel(
                 )
 
             if e < LAST:
-                for r in range(BLOCKS):
-                    if GATE_AT[e][r] == BACK:
-                        row = e * BLOCKS + r
-                        gate_blocks(e, banks_y[SEAT[r] // 2][:, SEAT[r] % 2 : SEAT[r] % 2 + 1, :], kept_y[:, row : row + 1, :], 1)
-                        backlog[e, r] = kept_y[:, row, :]
                 now = [r for r in range(BLOCKS) if GATE_AT[e][r] == NOW]
                 leave(e, now, banks_y, free_y[:], backlog)
             else:
-                leaving = [([0], banks_y[0][:, 0:1, :]), ([1], alone[:, 0:1, :]), ([2, 3], banks_y[1][:])]
-                for blocks, y in leaving:
-                    gate_blocks(e, y, kept_y[:, blocks[0] : blocks[-1] + 1, :], len(blocks))
+                for bank, blocks in zip(banks_y, seating):
+                    into = last_y[:, blocks[0] : blocks[-1] + 1, :]
+                    y = bank[:, : len(blocks), :]
+                    if blocks[0] in TAIL_ON_VECTOR:
+                        nc.scalar.copy(into, y)
+                    else:
+                        gate_blocks(e, y, into, len(blocks))
                     for r in blocks:
-                        for source in range(LAST, -1, -1):
-                            if source == LAST or (source, r) in backlog:
-                                gated = kept_y[:, r, :] if source == LAST else backlog[source, r]
-                                if r in TAIL_ON_VECTOR:
-                                    nc.vector.tensor_copy(places(source, r), gated)
-                                else:
-                                    nc.scalar.activation(places(source, r), gated, COPY)
+                        if r in TAIL_ON_VECTOR:
+                            nc.vector.tensor_tensor(places(e, r), last_y[:, r, :], gates[:, e * C : (e + 1) * C], ALU.mult)
+                        else:
+                            nc.scalar.activation(places(e, r), last_y[:, r, :], COPY)
+                        for source in reversed(range(LAST)):
+                            if (source, r) in backlog:
+                                nc.scalar.activation(places(source, r), backlog[source, r], COPY)
                 for r in STORE_ORDER:
                     nc.sync.dma_start(out=out[r * P : (r + 1) * P, :], in_=windows[r][:])

@@ -38,14 +38,14 @@ PIECES = 5
 S, V, G = 0, 1, 2
 NOW, END, AFTER = -1, 1, 2
 
-PARTS = [[[[0,64,S]],[[0,64,S]],[[0,64,V]],[[0,24,S],[24,64,V]],[[0,32,S],[32,64,S]]],[[[0,32,S],[32,64,S]],[[0,32,V],[32,64,V]],[[0,32,V],[32,64,V]],[[0,32,V],[32,64,V]],[[0,8,V],[8,32,V],[32,64,V]]],[[[0,32,S],[32,64,S]],[[0,32,V],[32,64,V]],[[0,32,V],[32,64,V]],[[0,32,V],[32,64,V]],[[0,8,V],[8,32,V],[32,64,V]]],[[[0,32,S],[32,64,S]],[[0,32,V],[32,64,V]],[[0,64,V]],[[0,32,V],[32,40,V],[40,64,S]],[[0,16,S],[16,32,S],[32,64,S]]]]
+PARTS = [[[[0,64,S]],[[0,64,S]],[[0,64,V]],[[0,24,S],[24,64,V]],[[0,32,S],[32,64,S]]],[[[0,32,S],[32,64,S]],[[0,32,V],[32,64,V]],[[0,32,V],[32,64,V]],[[0,32,V],[32,64,V]],[[0,8,V],[8,48,V],[48,64,G]]],[[[0,32,S],[32,52,S],[52,64,V]],[[0,32,V],[32,64,V]],[[0,32,V],[32,64,V]],[[0,32,V],[32,64,V]],[[0,8,V],[8,48,V],[48,64,G]]],[[[0,32,S],[32,52,S],[52,64,V]],[[0,32,V],[32,64,V]],[[0,64,V]],[[0,32,V],[32,40,V],[40,64,S]],[[0,16,S],[16,32,S],[32,48,S],[48,64,G]]]]
 GATE_AT = [[[W3_LO,END],[W3_HI,END],[W1_LO,END],[W1_HI,END]],[[W3_LO,END],[W3_HI,END],[W1_LO,END],[W1_HI,END]],[[W3_LO,END],[W3_HI,END],[W1_HI,END],[W1_HI,AFTER]]]
 KEPT = [[],[],[3]]
 B_HELD = [1,0,0,0]
 H_HELD = [1,2]
 H_BEHIND = [0,1,1,0]
 JOINED = [[1,1],[2,1]]
-CUTS = [[[512],[512],[512],[512],[256,512]],[[512],[512],[512],[512],[256,512]],[[512],[512],[512],[512],[256,512]],[[512],[512],[512],[256,512],[128,256,512]]]
+CUTS = [[[512],[512],[512],[512],[256,512]],[[512],[512],[512],[512],[384,512]],[[512],[512],[512],[512],[384,512]],[[512],[512],[512],[256,512],[128,256,384,512]]]
 H_CALLS = [2,1,1,2]
 LAST_BANKS = [[0],[1],[2],[3]]
 TAIL_ON_VECTOR = [0,2]
@@ -101,6 +101,11 @@ def tile_moe_two_glu_relu_kernel(
                 nc.sync.dma_start(out=room, in_=rows.rearrange("(p j) c -> p (j c)", j=PACK))
             return room
 
+        def aside(raw, octets):
+            if e == LAST:
+                return matrices[1][0][:, (PASSES * PACK - 1) * H : (PASSES * PACK - 1) * H + 32 * octets]
+            return raw[:, 64 : 64 + 16 * octets].bitcast(BF16)
+
         def round_part(raw, grouped, first_layer, first, end, engine):
             src = raw.rearrange("p (k g j b) -> p g j k b", k=PACK, j=PACK, b=PAIR)
             layout = "p (j g b k) -> p g j k b" if first_layer else "p (g j b k) -> p g j k b"
@@ -112,7 +117,7 @@ def tile_moe_two_glu_relu_kernel(
             else:
                 columns = slice(8 * first, 8 * end)
                 nc.gpsimd.tensor_scalar(
-                    grouped.rearrange("p (c k) -> p c k", k=PACK)[:, columns],
+                    aside(raw, end - first).rearrange("p (c k) -> p c k", k=PACK),
                     raw.rearrange("p (k c) -> p c k", k=PACK)[:, columns],
                     1.0,
                     0.0,
@@ -281,7 +286,14 @@ def tile_moe_two_glu_relu_kernel(
                     cuts = CUTS[e][piece]
                 first = 0
                 for stop in cuts:
-                    quantize(grouped, codes, scales, o * H + first, o * H + stop)
+                    if piece == W2 and stop == H and PARTS[e][piece][-1][2] == G:
+                        nc.vector.quantize_mx(
+                            out=codes[:, first:stop].bitcast(FP8X4),
+                            scales=scales[:, first:stop],
+                            in_=aside(here, (stop - first) // 8),
+                        )
+                    else:
+                        quantize(grouped, codes, scales, o * H + first, o * H + stop)
                     if piece == W2 and e in H_HELD and first == 0:
                         h_codes, h_scales = quantize_h(h, H_CALLS[e])
                     if piece != W2:

@@ -38,7 +38,7 @@ PIECES = 5
 S, V, G = 0, 1, 2
 NOW, END, AFTER = -1, 1, 2
 
-PARTS = [[[[0,64,S]],[[0,64,S]],[[0,64,V]],[[0,24,S],[24,64,V]],[[0,32,S],[32,64,S]]],[[[0,32,S],[32,64,S]],[[0,32,V],[32,64,V]],[[0,32,V],[32,64,V]],[[0,32,V],[32,64,V]],[[0,8,V],[8,48,V],[48,64,G]]],[[[0,32,S],[32,52,S],[52,64,V]],[[0,32,V],[32,64,V]],[[0,32,V],[32,64,V]],[[0,32,V],[32,64,V]],[[0,8,V],[8,48,V],[48,64,G]]],[[[0,32,S],[32,52,S],[52,64,V]],[[0,32,V],[32,64,V]],[[0,64,V]],[[0,32,V],[32,40,V],[40,64,S]],[[0,16,S],[16,32,S],[32,48,S],[48,64,G]]]]
+PARTS = [[[[0,64,S]],[[0,64,S]],[[0,36,V],[36,64,V]],[[0,26,S],[26,64,V]],[[0,32,S],[32,64,S]]],[[[0,32,S],[32,64,S]],[[0,36,V],[36,64,V]],[[0,36,V],[36,64,V]],[[0,36,V],[36,64,V]],[[0,10,V],[10,48,V],[48,64,G]]],[[[0,32,S],[32,52,S],[52,64,V]],[[0,36,V],[36,64,V]],[[0,36,V],[36,64,V]],[[0,36,V],[36,64,V]],[[0,10,V],[10,48,V],[48,64,G]]],[[[0,32,S],[32,44,S],[44,64,V]],[[0,36,V],[36,64,V]],[[0,36,V],[36,64,V]],[[0,34,V],[34,40,V],[40,64,S]],[[0,16,S],[16,32,S],[32,48,S],[48,64,G]]]]
 GATE_AT = [[[W3_LO,END],[W3_HI,END],[W1_LO,END],[W1_HI,END]],[[W3_LO,END],[W3_HI,END],[W1_LO,END],[W1_HI,END]],[[W3_LO,END],[W3_HI,END],[W1_HI,END],[W1_HI,AFTER]]]
 KEPT = [[],[],[3]]
 B_HELD = [1,0,0,0]
@@ -51,6 +51,7 @@ LAST_BANKS = [[0],[1],[2],[3]]
 TAIL_ON_VECTOR = [0,2]
 STORE_ORDER = [0,1,2,3]
 ROOMS_RIGHT = []
+SEATING = [[0],[1],[2,3]]
 LEAD = 2 * C - 64
 RAW_BUFS = 8
 
@@ -102,7 +103,7 @@ def tile_moe_two_glu_relu_kernel(
             return room
 
         def aside(raw, octets):
-            if e == LAST:
+            if e not in H_HELD:
                 return matrices[1][0][:, (PASSES * PACK - 1) * H : (PASSES * PACK - 1) * H + 32 * octets]
             return raw[:, 64 : 64 + 16 * octets].bitcast(BF16)
 
@@ -194,11 +195,11 @@ def tile_moe_two_glu_relu_kernel(
             nc.vector.tensor_tensor(into, y, weight, ALU.mult)
 
         def leave(e, due, banks, rooms, backlog):
-            for pair in range(BLOCKS // 2):
-                both = [r for r in due if r // 2 == pair]
+            for bank, blocks in zip(banks, SEATING):
+                both = [r for r in due if r in blocks]
                 if both:
                     row = due.index(both[0])
-                    y = banks[pair][:, both[0] % 2 : both[-1] % 2 + 1, :]
+                    y = bank[:, blocks.index(both[0]) : blocks.index(both[-1]) + 1, :]
                     gate_blocks(e, y, rooms[:, row : row + len(both), :], len(both))
                     for n, r in enumerate(both):
                         if r in KEPT[e]:
@@ -286,7 +287,7 @@ def tile_moe_two_glu_relu_kernel(
                     cuts = CUTS[e][piece]
                 first = 0
                 for stop in cuts:
-                    if piece == W2 and stop == H and PARTS[e][piece][-1][2] == G:
+                    if piece == W2 and PARTS[e][piece][-1][2] == G and stop == 8 * PARTS[e][piece][-1][1]:
                         nc.vector.quantize_mx(
                             out=codes[:, first:stop].bitcast(FP8X4),
                             scales=scales[:, first:stop],
@@ -304,7 +305,7 @@ def tile_moe_two_glu_relu_kernel(
                     make_h(banks_a, b_rooms, h)
                     h_codes, h_scales = quantize_h(h, H_CALLS[e])
 
-            seating = [[0, 1], [2, 3]] if e < LAST else LAST_BANKS
+            seating = SEATING if e < LAST else LAST_BANKS
             banks_y = [psum_y.tile([P, 2, C], F32, name="bank_y") for blocks in seating]
             for r in range(BLOCKS):
                 bank = [n for n, blocks in enumerate(seating) if r in blocks][0]

@@ -28,32 +28,57 @@ HALF = 128
 HALVES = C // HALF
 BLOCKS = N // P
 LIST_COLS = C // 16
-LAST = E - 1
 PAIR = 2
-OCTETS = H // 8
+OCTET = PACK * PAIR
+OCTETS = H // OCTET
+BLOCK_OCTETS = P // OCTET
 GATE_COLS = SLOTS // P
+SPREAD = 4
+FIRST, LAST = 0, E - 1
 
 W3_LO, W3_HI, W1_LO, W1_HI, W2 = range(5)
 PIECES = 5
-S, V, G = 0, 1, 2
-NOW, END, AFTER = -1, 1, 2
+SCALAR, VECTOR, GPSIMD = range(3)
 
-PARTS = [[[[0,64,S]],[[0,64,S]],[[0,36,V],[36,64,V]],[[0,26,S],[26,64,V]],[[0,32,S],[32,64,S]]],[[[0,32,S],[32,64,S]],[[0,36,V],[36,64,V]],[[0,36,V],[36,64,V]],[[0,36,V],[36,64,V]],[[0,10,V],[10,48,V],[48,64,G]]],[[[0,32,S],[32,52,S],[52,64,V]],[[0,36,V],[36,64,V]],[[0,36,V],[36,64,V]],[[0,36,V],[36,64,V]],[[0,10,V],[10,48,V],[48,64,G]]],[[[0,32,S],[32,44,S],[44,64,V]],[[0,36,V],[36,64,V]],[[0,36,V],[36,64,V]],[[0,34,V],[34,40,V],[40,64,S]],[[0,16,S],[16,32,S],[32,48,S],[48,64,G]]]]
-GATE_AT = [[[W3_LO,END],[W3_HI,END],[W1_LO,END],[W1_HI,END]],[[W3_LO,END],[W3_HI,END],[W1_LO,END],[W1_HI,END]],[[W3_LO,END],[W3_HI,END],[W1_HI,END],[W1_HI,AFTER]]]
-KEPT = [[],[],[3]]
-B_HELD = [1,0,0,0]
-H_HELD = [1,2]
-H_BEHIND = [0,1,1,0]
-JOINED = [[1,1],[2,1]]
-CUTS = [[[512],[512],[512],[512],[256,512]],[[512],[512],[512],[512],[384,512]],[[512],[512],[512],[512],[384,512]],[[512],[512],[512],[256,512],[128,256,384,512]]]
-H_CALLS = [2,1,1,2]
-LAST_BANKS = [[0],[1],[2],[3]]
-TAIL_ON_VECTOR = [0,2]
-STORE_ORDER = [0,1,2,3]
-ROOMS_RIGHT = []
-SEATING = [[0],[1],[2,3]]
-LEAD = 2 * C - 64
+ROOM_OCTETS = C // OCTET
+W3_SHARE = 20
+W1_SHARE = 24
+H_OCTETS = 8
+LEAD = C * PACK // 2 - H_OCTETS * OCTET
+SEATS = [[0], [1], [2, 3]]
+KEPT_BLOCK = BLOCKS - 1
 RAW_BUFS = 8
+
+
+def rounding(e, piece):
+    if piece == W2:
+        last_block = (OCTETS - BLOCK_OCTETS, OCTETS, GPSIMD)
+        if e == FIRST:
+            return [(0, OCTETS // 2, SCALAR), (OCTETS // 2, OCTETS, SCALAR)]
+        if e == LAST:
+            return [(r * BLOCK_OCTETS, (r + 1) * BLOCK_OCTETS, SCALAR) for r in range(BLOCKS - 1)] + [last_block]
+        return [(0, H_OCTETS, VECTOR), (H_OCTETS, OCTETS - BLOCK_OCTETS, VECTOR), last_block]
+    if e == FIRST:
+        if piece == W1_HI:
+            return [(0, W1_SHARE, SCALAR), (W1_SHARE, OCTETS, VECTOR)]
+        return [(0, OCTETS, VECTOR if piece == W1_LO else SCALAR)]
+    if piece == W3_LO:
+        cut = OCTETS - W3_SHARE
+        return [(0, ROOM_OCTETS, SCALAR), (ROOM_OCTETS, cut, SCALAR), (cut, OCTETS, VECTOR)]
+    if e == LAST and piece == W1_LO:
+        return [(0, OCTETS, VECTOR)]
+    if e == LAST and piece == W1_HI:
+        cut = OCTETS - W1_SHARE
+        return [(0, ROOM_OCTETS, VECTOR), (ROOM_OCTETS, cut, VECTOR), (cut, OCTETS, SCALAR)]
+    return [(0, ROOM_OCTETS, VECTOR), (ROOM_OCTETS, OCTETS, VECTOR)]
+
+
+def leaving(e, piece):
+    if e == FIRST or piece == W2:
+        return []
+    if e == LAST:
+        return {W3_LO: [0], W3_HI: [1], W1_LO: [], W1_HI: [2]}[piece]
+    return [piece]
 
 
 def tile_moe_two_glu_relu_kernel(
@@ -81,65 +106,52 @@ def tile_moe_two_glu_relu_kernel(
         gate_cols = keep.tile([P, GATE_COLS], F32, name="gate_cols")
         gates = keep.tile([P, SLOTS], F32, name="gates")
         identity = keep.tile([P, P], F32, name="identity")
-        free_y = keep.tile([P, 2, C], F32, name="free_y")
         last_y = keep.tile([P, BLOCKS, C], F32, name="last_y")
         windows = [keep.tile([P, T], F32, name=f"window{r}") for r in range(BLOCKS)]
-        w2_tiles = [keep.tile([P, LEAD + PACK * H], F32, name=f"raw_w2_{e}", align_bytes=64) for e in range(E)]
+        leads = [0 if e in (FIRST, LAST) else LEAD for e in range(E)]
+        w2_tiles = [keep.tile([P, leads[e] + PACK * H], F32, name=f"raw_w2_{e}", align_bytes=64) for e in range(E)]
+
+        def rows_of(flat):
+            return flat.rearrange("p (k c) -> p k c", k=PACK)
 
         def load_piece(e, piece):
             if piece == W2:
-                room = w2_tiles[e][:, LEAD:]
-                raw = room.rearrange("p (j c) -> p j c", j=PACK)
-                rows = w2[e].rearrange("(g j b) c -> b g j c", j=PACK, b=PAIR)
-                for b in range(PAIR):
-                    nc.sync.dma_start(out=raw[b:P:PAIR], in_=rows[b])
-            else:
-                tile = raws.tile([P, PACK * H], F32, name="raw")
-                room = tile[:]
-                w = w3 if piece in (W3_LO, W3_HI) else w1
-                o = 0 if piece in (W3_LO, W1_LO) else 1
-                rows = w[e, o * K_PASS : (o + 1) * K_PASS, :]
-                nc.sync.dma_start(out=room, in_=rows.rearrange("(p j) c -> p (j c)", j=PACK))
-            return room
+                raw = w2_tiles[e][:, leads[e] :]
+                rows = w2[e].rearrange("(g j d) c -> d g j c", j=PACK, d=PAIR)
+                for d in range(PAIR):
+                    nc.sync.dma_start(out=rows_of(raw)[d:P:PAIR], in_=rows[d])
+                return raw
+            tile = raws.tile([P, PACK * H], F32, name="raw")
+            w = w3 if piece in (W3_LO, W3_HI) else w1
+            o = piece % PASSES
+            rows = w[e, o * K_PASS : (o + 1) * K_PASS, :]
+            nc.sync.dma_start(out=tile[:], in_=rows.rearrange("(p k) c -> p (k c)", k=PACK))
+            return tile[:]
 
-        def aside(raw, octets):
-            if e not in H_HELD:
-                return matrices[1][0][:, (PASSES * PACK - 1) * H : (PASSES * PACK - 1) * H + 32 * octets]
-            return raw[:, 64 : 64 + 16 * octets].bitcast(BF16)
-
-        def round_part(raw, grouped, first_layer, first, end, engine):
-            src = raw.rearrange("p (k g j b) -> p g j k b", k=PACK, j=PACK, b=PAIR)
-            layout = "p (j g b k) -> p g j k b" if first_layer else "p (g j b k) -> p g j k b"
-            into = grouped.rearrange(layout, j=PACK, b=PAIR, k=PACK)
-            if engine == S:
+        def round_octets(raw, values, piece, first, end, engine):
+            src = raw.rearrange("p (k g j d) -> p g j k d", k=PACK, j=PACK, d=PAIR)
+            layout = "p (g j d k) -> p g j k d" if piece == W2 else "p (j g d k) -> p g j k d"
+            into = values.rearrange(layout, j=PACK, d=PAIR, k=PACK)
+            if engine == SCALAR:
                 nc.scalar.copy(out=into[:, first:end], in_=src[:, first:end])
-            elif engine == V:
-                nc.vector.tensor_copy(out=into[:, first:end], in_=src[:, first:end])
             else:
-                columns = slice(8 * first, 8 * end)
-                nc.gpsimd.tensor_scalar(
-                    aside(raw, end - first).rearrange("p (c k) -> p c k", k=PACK),
-                    raw.rearrange("p (k c) -> p c k", k=PACK)[:, columns],
-                    1.0,
-                    0.0,
-                    ALU.mult,
-                    ALU.add,
-                )
+                nc.vector.tensor_copy(out=into[:, first:end], in_=src[:, first:end])
+
+        def round_on_gpsimd(raw, into, first, end):
+            src = raw.rearrange("p (k c) -> p c k", k=PACK)[:, OCTET * first : OCTET * end]
+            nc.gpsimd.tensor_scalar(into.rearrange("p (c k) -> p c k", k=PACK), src, 1.0, 0.0, ALU.mult, ALU.add)
 
         def new_matrix(name, passes):
-            grouped = rounded.tile([P, passes * PACK * H], BF16, name=f"grouped_{name}", align_bytes=64)
+            values = rounded.tile([P, passes * PACK * H], BF16, name=f"values_{name}", align_bytes=64)
             codes = coded.tile([P, passes * H], U32, name=f"codes_{name}", align_bytes=64)
             scales = coded.tile([P, passes * H], U8, name=f"scales_{name}", align_bytes=64)
-            return grouped, codes, scales
+            return values, codes, scales
 
-        def quantize(grouped, codes, scales, first, end):
-            nc.vector.quantize_mx(
-                out=codes[:, first:end].bitcast(FP8X4),
-                scales=scales[:, first:end],
-                in_=grouped[:, PACK * first : PACK * end],
-            )
+        def quantize(values, codes, scales, first, end):
+            nc.vector.quantize_mx(out=codes[:, first:end].bitcast(FP8X4), scales=scales[:, first:end], in_=values)
 
-        def first_layer_pass(e, o, banks, codes, scales, groups):
+        def first_layer_pass(e, o, banks, matrix, groups):
+            values, codes, scales = matrix
             for half, j in product(reversed(range(HALVES)), groups):
                 slots = slice(e * C + half * HALF, e * C + (half + 1) * HALF)
                 cols = slice(o * H + j * P, o * H + (j + 1) * P)
@@ -153,165 +165,60 @@ def tile_moe_two_glu_relu_kernel(
                     stop=(o == PASSES - 1 and j == PACK - 1),
                 )
 
-        def rows_of(raw):
-            return raw.rearrange("p (k c) -> p k c", k=PACK)
+        def quantize_first_layer(e, piece, matrix, banks):
+            values, codes, scales = matrix
+            o = piece % PASSES
+            if e not in (FIRST, LAST) and piece in (W3_LO, W3_HI):
+                if piece == W3_HI:
+                    quantize(values[:], codes, scales, 0, PASSES * H)
+                    for both in range(PASSES):
+                        first_layer_pass(e, both, banks, matrix, range(PACK))
+                return
+            calls = 2 if (e, piece) == (LAST, W1_HI) else 1
+            for call in range(calls):
+                first, end = o * H + call * H // calls, o * H + (call + 1) * H // calls
+                quantize(values[:, PACK * first : PACK * end], codes, scales, first, end)
+                first_layer_pass(e, o, banks, matrix, range(call * PACK // calls, (call + 1) * PACK // calls))
 
-        def copy_b(banks, raw, held):
-            result = {}
+        def copy_b(e, banks, raw):
+            b = {}
             for half in reversed(range(HALVES)):
-                if half >= HALVES - held:
-                    room = rows_of(raw)[:, :, (1 - half) * HALF : (2 - half) * HALF]
+                if e == FIRST and half == HALVES - 1:
+                    room = rows_of(raw)[:, :, :HALF]
                 else:
-                    spare = once.tile([P, PACK * HALF], F32, name=f"b_free{half}")
-                    room = rows_of(spare[:])
-                room = room.rearrange("p a (s j) -> p a s j", j=PACK)
-                nc.scalar.copy(out=room, in_=banks[half][:].rearrange("p j (a s) -> p a s j", a=PACK))
-                result[half] = room
-            return result
+                    tile = once.tile([P, PACK * HALF], F32, name=f"b{half}")
+                    room = rows_of(tile[:])
+                b[half] = room.rearrange("p a (s j) -> p a s j", j=PACK)
+                nc.scalar.copy(out=b[half], in_=banks[half][:].rearrange("p j (a s) -> p a s j", a=PACK))
+            return b
 
-        def make_h(banks_a, b_rooms, h):
+        def make_h(banks_a, b, h):
             for half in reversed(range(HALVES)):
                 nc.vector.scalar_tensor_tensor(
                     out=h[:, half * H : (half + 1) * H].rearrange("p (a s j) -> p a s j", a=PACK, j=PACK),
                     in0=banks_a[half][:].rearrange("p j (a s) -> p a s j", a=PACK),
                     scalar=0.0,
-                    in1=b_rooms[half],
+                    in1=b[half],
                     op0=ALU.max,
                     op1=ALU.mult,
                 )
 
         def quantize_h(h, calls):
-            h_codes = hidden.tile([P, C], U32, name="h_codes", align_bytes=64)
-            h_scales = hidden.tile([P, C], U8, name="h_scales", align_bytes=64)
+            codes = hidden.tile([P, C], U32, name="h_codes", align_bytes=64)
+            scales = hidden.tile([P, C], U8, name="h_scales", align_bytes=64)
             for call in reversed(range(calls)):
-                quantize(h, h_codes, h_scales, call * C // calls, (call + 1) * C // calls)
-            return h_codes, h_scales
+                first, end = call * C // calls, (call + 1) * C // calls
+                quantize(h[:, PACK * first : PACK * end], codes, scales, first, end)
+            return codes, scales
 
-        def places(e, r):
-            return windows[r][:].indirect(dst_sb[:, e * LIST_COLS : (e + 1) * LIST_COLS])
-
-        def gate_blocks(e, y, into, count):
-            weight = gates[:, e * C : (e + 1) * C].unsqueeze(1).to_broadcast([P, count, C])
-            nc.vector.tensor_tensor(into, y, weight, ALU.mult)
-
-        def leave(e, due, banks, rooms, backlog):
-            for bank, blocks in zip(banks, SEATING):
-                both = [r for r in due if r in blocks]
-                if both:
-                    row = due.index(both[0])
-                    y = bank[:, blocks.index(both[0]) : blocks.index(both[-1]) + 1, :]
-                    gate_blocks(e, y, rooms[:, row : row + len(both), :], len(both))
-                    for n, r in enumerate(both):
-                        if r in KEPT[e]:
-                            backlog[e, r] = rooms[:, row + n, :]
-                        else:
-                            nc.scalar.activation(places(e, r), rooms[:, row + n, :], COPY)
-
-        nc.vector.memset(token_scales[:].bitcast(I32), 0)
-        nc.vector.memset(windows[0][:], 0.0)
-        for r in range(1, BLOCKS):
-            nc.scalar.copy(out=windows[r][:], in_=windows[0][:])
-        make_identity(nc, identity[:])
-        for o in range(PASSES):
-            nc.sync.dma_start(
-                out=token_words[o][:],
-                in_=x_words[o].rearrange("p t j -> p (t j)").bitcast(I32),
-            )
-            if o == 0:
-                nc.sync.dma_start(offs_sb[:], offs)
-                for q in range(P // QUADRANT):
-                    nc.sync.dma_start(
-                        out=token_scales[QUADRANT * q : QUADRANT * q + SCALE_ROWS * PASSES, :].bitcast(I32),
-                        in_=x_scales[:, SCALE_ROWS * q : SCALE_ROWS * (q + 1), :].bitcast(I32),
-                    )
-
-        raw = []
-        for e in range(E):
-            raw.append({})
-            for piece in range(PIECES):
-                raw[e][piece] = load_piece(e, piece)
-                if e == 0 and piece == W3_LO:
-                    nc.sync.dma_start(out=gate_cols[:], in_=gate[0, :].rearrange("(p c) -> p c", c=GATE_COLS))
-                if e == 0 and piece == W1_HI:
-                    nc.sync.dma_start(dst_sb[:], dst)
-
-        for o in range(PASSES):
-            nc.vector.tensor_copy(slot_words[o][:], token_words[o][:].bitcast(U32).indirect(offs_sb[:]))
-            if o == 0:
-                nc.vector.tensor_copy(slot_scales[:], token_scales[:].indirect(offs_sb[:]))
-
-        for group in range(GATE_COLS // 4):
-            spread = psum_y.tile([P, 4, P], F32, name="bank_y")
-            for c in range(4):
-                col = 4 * group + c
-                nc.tensor.transpose(spread[:, c, :], gate_cols[:, col : col + 1].to_broadcast([P, P]), identity[:])
-            nc.vector.tensor_copy(
-                out=gates[:].rearrange("p (s c) -> p s c", c=GATE_COLS)[:, :, 4 * group : 4 * group + 4],
-                in_=spread[:].rearrange("p c s -> p s c"),
-            )
-
-        banks_y = []
-        backlog = {}
-        for e in range(E):
-            matrices = [new_matrix("w3", PASSES), new_matrix("w1", PASSES), new_matrix("w2", 1)]
-            banks_b = [psum_b.tile([P, PACK, HALF], F32, name="bank") for half in range(HALVES)]
-            banks_a = [psum_a.tile([P, PACK, HALF], F32, name="bank") for half in range(HALVES)]
-            if e in H_HELD:
-                h = w2_tiles[e][:, : 2 * C].bitcast(BF16)
-            else:
-                own = hidden.tile([P, C * PACK], BF16, name="h", align_bytes=64)
-                h = own[:]
-            for piece in range(PIECES):
-                grouped, codes, scales = matrices[piece // 2]
-                o = piece % 2
-                here = raw[e][piece]
-                end = [r for r in range(BLOCKS) if e > 0 and GATE_AT[e - 1][r] == [piece, END]]
-                after = [r for r in range(BLOCKS) if e > 0 and GATE_AT[e - 1][r] == [piece, AFTER]]
-                rooms = rows_of(here)[:, :, C:] if [e, piece] in ROOMS_RIGHT else rows_of(here)[:, :, :C]
-                for n, (first, stop, engine) in enumerate(PARTS[e][piece]):
-                    round_part(here, grouped[:, o * PACK * H : (o + 1) * PACK * H], piece != W2, first, stop, engine)
-                    if piece == W2 and e in H_HELD and n == H_BEHIND[e]:
-                        make_h(banks_a, b_rooms, h)
-                leave(e - 1, end, banks_y, rooms, backlog)
-                if piece == W1_HI:
-                    b_rooms = copy_b(banks_b, here, B_HELD[e])
-                banks = banks_b if piece < W1_LO else banks_a
-                if [e, piece + 1] in JOINED:
-                    cuts = []
-                elif [e, piece] in JOINED:
-                    quantize(grouped, codes, scales, 0, PASSES * H)
-                    for both in range(PASSES):
-                        first_layer_pass(e, both, banks, codes, scales, range(PACK))
-                    cuts = []
-                else:
-                    cuts = CUTS[e][piece]
-                first = 0
-                for stop in cuts:
-                    if piece == W2 and PARTS[e][piece][-1][2] == G and stop == 8 * PARTS[e][piece][-1][1]:
-                        nc.vector.quantize_mx(
-                            out=codes[:, first:stop].bitcast(FP8X4),
-                            scales=scales[:, first:stop],
-                            in_=aside(here, (stop - first) // 8),
-                        )
-                    else:
-                        quantize(grouped, codes, scales, o * H + first, o * H + stop)
-                    if piece == W2 and e in H_HELD and first == 0:
-                        h_codes, h_scales = quantize_h(h, H_CALLS[e])
-                    if piece != W2:
-                        first_layer_pass(e, o, banks, codes, scales, range(first // P, stop // P))
-                    first = stop
-                leave(e - 1, after, banks_y, rooms[:, len(end) :, :], backlog)
-                if piece == W1_HI and e not in H_HELD:
-                    make_h(banks_a, b_rooms, h)
-                    h_codes, h_scales = quantize_h(h, H_CALLS[e])
-
-            seating = SEATING if e < LAST else LAST_BANKS
-            banks_y = [psum_y.tile([P, 2, C], F32, name="bank_y") for blocks in seating]
+        def second_layer(matrix, h_codes, h_scales, seats):
+            values, codes, scales = matrix
+            banks = [psum_y.tile([P, 2, C], F32, name="bank_y") for blocks in seats]
+            y = {r: bank[:, blocks.index(r), :] for bank, blocks in zip(banks, seats) for r in blocks}
             for r in range(BLOCKS):
-                bank = [n for n, blocks in enumerate(seating) if r in blocks][0]
                 cols = slice(r * P, (r + 1) * P)
                 nc.tensor.matmul_mx(
-                    out=banks_y[bank][:, seating[bank].index(r), :],
+                    out=y[r],
                     lhsT=codes[:, cols].bitcast(FP8X4),
                     lhsT_scale=scales[:, cols],
                     rhs=h_codes[:].bitcast(FP8X4),
@@ -319,25 +226,117 @@ def tile_moe_two_glu_relu_kernel(
                     start=True,
                     stop=True,
                 )
+            return y
 
-            if e < LAST:
-                now = [r for r in range(BLOCKS) if GATE_AT[e][r] == NOW]
-                leave(e, now, banks_y, free_y[:], backlog)
+        def gates_of(e):
+            return gates[:, e * C : (e + 1) * C]
+
+        def places(e, r):
+            return windows[r][:].indirect(dst_sb[:, e * LIST_COLS : (e + 1) * LIST_COLS])
+
+        nc.vector.memset(token_scales[:].bitcast(I32), 0)
+        nc.vector.memset(windows[0][:], 0.0)
+        for r in range(1, BLOCKS):
+            nc.scalar.copy(out=windows[r][:], in_=windows[0][:])
+        make_identity(nc, identity[:])
+
+        for o in range(PASSES):
+            nc.sync.dma_start(out=token_words[o][:], in_=x_words[o].rearrange("p t r -> p (t r)").bitcast(I32))
+            if o == 0:
+                nc.sync.dma_start(offs_sb[:], offs)
+                for q in range(P // QUADRANT):
+                    nc.sync.dma_start(
+                        out=token_scales[QUADRANT * q : QUADRANT * q + SCALE_ROWS * PASSES, :].bitcast(I32),
+                        in_=x_scales[:, SCALE_ROWS * q : SCALE_ROWS * (q + 1), :].bitcast(I32),
+                    )
+        raw = {}
+        for e, piece in product(range(E), range(PIECES)):
+            raw[e, piece] = load_piece(e, piece)
+            if (e, piece) == (FIRST, W3_LO):
+                nc.sync.dma_start(out=gate_cols[:], in_=gate[0, :].rearrange("(p c) -> p c", c=GATE_COLS))
+            if (e, piece) == (FIRST, W1_HI):
+                nc.sync.dma_start(dst_sb[:], dst)
+
+        for o in range(PASSES):
+            nc.vector.tensor_copy(slot_words[o][:], token_words[o][:].bitcast(U32).indirect(offs_sb[:]))
+            if o == 0:
+                nc.vector.tensor_copy(slot_scales[:], token_scales[:].indirect(offs_sb[:]))
+
+        for group in range(GATE_COLS // SPREAD):
+            spread = psum_y.tile([P, SPREAD, P], F32, name="bank_y")
+            for n in range(SPREAD):
+                col = SPREAD * group + n
+                nc.tensor.transpose(spread[:, n, :], gate_cols[:, col : col + 1].to_broadcast([P, P]), identity[:])
+            nc.vector.tensor_copy(
+                out=gates[:].rearrange("p (s c) -> p s c", c=GATE_COLS)[:, :, SPREAD * group : SPREAD * (group + 1)],
+                in_=spread[:].rearrange("p c s -> p s c"),
+            )
+
+        y = {}
+        for e in range(E):
+            middle = e not in (FIRST, LAST)
+            matrices = [new_matrix("w3", PASSES), new_matrix("w1", PASSES), new_matrix("w2", 1)]
+            banks_b = [psum_b.tile([P, PACK, HALF], F32, name="bank") for half in range(HALVES)]
+            banks_a = [psum_a.tile([P, PACK, HALF], F32, name="bank") for half in range(HALVES)]
+            if middle:
+                h = w2_tiles[e][:, : C * PACK // 2].bitcast(BF16)
             else:
-                for bank, blocks in zip(banks_y, seating):
-                    into = last_y[:, blocks[0] : blocks[-1] + 1, :]
-                    y = bank[:, : len(blocks), :]
-                    if blocks[0] in TAIL_ON_VECTOR:
-                        nc.scalar.copy(into, y)
-                    else:
-                        gate_blocks(e, y, into, len(blocks))
-                    for r in blocks:
-                        if r in TAIL_ON_VECTOR:
-                            nc.vector.tensor_tensor(places(e, r), last_y[:, r, :], gates[:, e * C : (e + 1) * C], ALU.mult)
-                        else:
-                            nc.scalar.activation(places(e, r), last_y[:, r, :], COPY)
-                        for source in reversed(range(LAST)):
-                            if (source, r) in backlog:
-                                nc.scalar.activation(places(source, r), backlog[source, r], COPY)
-                for r in STORE_ORDER:
-                    nc.sync.dma_start(out=out[r * P : (r + 1) * P, :], in_=windows[r][:])
+                own = hidden.tile([P, C * PACK], BF16, name="h", align_bytes=64)
+                h = own[:]
+
+            for piece in range(W2):
+                matrix = matrices[piece // PASSES]
+                o = piece % PASSES
+                values = matrix[0][:, o * PACK * H : (o + 1) * PACK * H]
+                rooms = rows_of(raw[e, piece])[:, :, :C]
+                for first, end, engine in rounding(e, piece):
+                    round_octets(raw[e, piece], values, piece, first, end, engine)
+                for r in leaving(e, piece):
+                    nc.vector.tensor_tensor(rooms[:, 0, :], y[r], gates_of(e - 1), ALU.mult)
+                    nc.scalar.activation(places(e - 1, r), rooms[:, 0, :], COPY)
+                if piece == W1_HI:
+                    b = copy_b(e, banks_b, raw[e, piece])
+                quantize_first_layer(e, piece, matrix, banks_b if piece < W1_LO else banks_a)
+
+            if e == LAST:
+                kept = rows_of(raw[e, W1_HI])[:, 1, :C]
+                nc.vector.tensor_tensor(kept, y[KEPT_BLOCK], gates_of(e - 1), ALU.mult)
+            if not middle:
+                make_h(banks_a, b, h)
+                h_codes, h_scales = quantize_h(h, HALVES)
+
+            values, codes, scales = matrices[W2 // PASSES]
+            if middle:
+                aside = raw[e, W2][:, H_OCTETS * OCTET : H_OCTETS * OCTET + P * PACK // 2].bitcast(BF16)
+            else:
+                aside = matrices[W1_HI // PASSES][0][:, PASSES * PACK * H - P * PACK :]
+            parts = rounding(e, W2)
+            for first, end, engine in parts:
+                if engine == GPSIMD:
+                    if middle:
+                        make_h(banks_a, b, h)
+                    round_on_gpsimd(raw[e, W2], aside, first, end)
+                else:
+                    round_octets(raw[e, W2], values[:], W2, first, end, engine)
+            if middle:
+                parts = [(0, parts[1][1], VECTOR), parts[2]]
+            for first, end, engine in parts:
+                first, end = OCTET * first, OCTET * end
+                source = aside if engine == GPSIMD else values[:, PACK * first : PACK * end]
+                quantize(source, codes, scales, first, end)
+                if middle and first == 0:
+                    h_codes, h_scales = quantize_h(h, 1)
+
+            seats = [[r] for r in range(BLOCKS)] if e == LAST else SEATS
+            y = second_layer(matrices[W2 // PASSES], h_codes, h_scales, seats)
+
+        for r in range(BLOCKS):
+            if r % 2 == 0:
+                nc.scalar.copy(last_y[:, r, :], y[r])
+                nc.vector.tensor_tensor(places(LAST, r), last_y[:, r, :], gates_of(LAST), ALU.mult)
+            else:
+                nc.vector.tensor_tensor(last_y[:, r, :], y[r], gates_of(LAST), ALU.mult)
+                nc.scalar.activation(places(LAST, r), last_y[:, r, :], COPY)
+        nc.scalar.activation(places(LAST - 1, KEPT_BLOCK), kept, COPY)
+        for r in range(BLOCKS):
+            nc.sync.dma_start(out=out[r * P : (r + 1) * P, :], in_=windows[r][:])

@@ -41,7 +41,6 @@ PIECES = 5
 SCALAR, VECTOR, GPSIMD = range(3)
 
 ROOM_OCTETS = C // OCTET
-W3_SHARE = 20
 W1_SHARE = 24
 H_OCTETS = 8
 LEAD = C * PACK // 2 - H_OCTETS * OCTET
@@ -63,10 +62,12 @@ def rounding(e, piece):
             return [(0, W1_SHARE, SCALAR), (W1_SHARE, OCTETS, VECTOR)]
         return [(0, OCTETS, VECTOR if piece == W1_LO else SCALAR)]
     if piece == W3_LO:
-        cut = OCTETS - W3_SHARE
-        return [(0, ROOM_OCTETS, SCALAR), (ROOM_OCTETS, cut, SCALAR), (cut, OCTETS, VECTOR)]
+        return [(0, ROOM_OCTETS, SCALAR), (ROOM_OCTETS, OCTETS, VECTOR)]
     if e == LAST and piece == W1_LO:
         return [(0, OCTETS, VECTOR)]
+    if piece == W1_LO:
+        cut = OCTETS - BLOCK_OCTETS
+        return [(0, ROOM_OCTETS, VECTOR), (ROOM_OCTETS, cut, VECTOR), (cut, OCTETS, SCALAR)]
     if e == LAST and piece == W1_HI:
         cut = OCTETS - W1_SHARE
         return [(0, ROOM_OCTETS, VECTOR), (ROOM_OCTETS, cut, VECTOR), (cut, OCTETS, SCALAR)]

@@ -49,37 +49,41 @@ KEPT_BLOCK = BLOCKS - 1
 RAW_BUFS = 8
 
 
+BLOCK = P * PACK
+
+
+def halves_of(e):
+    return range(HALVES) if e == LAST else range(HALVES - 1, -1, -1)
+
+
+def blocks_ahead(e):
+    return BLOCKS - 1 if e == LAST - 1 else BLOCKS
+
+
 def rounding(e, piece):
     if piece == W2:
-        last_block = (OCTETS - BLOCK_OCTETS, OCTETS, GPSIMD)
+        end = blocks_ahead(e) * BLOCK_OCTETS
         if e == FIRST:
             return [(0, OCTETS // 2, SCALAR), (OCTETS // 2, OCTETS, SCALAR)]
-        if e == LAST:
-            return [(r * BLOCK_OCTETS, (r + 1) * BLOCK_OCTETS, SCALAR) for r in range(BLOCKS - 1)] + [last_block]
-        return [(0, H_OCTETS, VECTOR), (H_OCTETS, OCTETS - BLOCK_OCTETS, VECTOR), last_block]
+        return [(0, H_OCTETS, VECTOR), (H_OCTETS, end - BLOCK_OCTETS, VECTOR), (end - BLOCK_OCTETS, end, GPSIMD)]
     if e == FIRST:
         if piece == W1_HI:
             return [(0, W1_SHARE, SCALAR), (W1_SHARE, OCTETS, VECTOR)]
         return [(0, OCTETS, VECTOR if piece == W1_LO else SCALAR)]
     if piece == W3_LO:
         return [(0, ROOM_OCTETS, SCALAR), (ROOM_OCTETS, OCTETS, VECTOR)]
-    if e == LAST and piece == W1_LO:
-        return [(0, OCTETS, VECTOR)]
     if piece == W1_LO:
         cut = OCTETS - BLOCK_OCTETS
-        return [(0, ROOM_OCTETS, VECTOR), (ROOM_OCTETS, cut, VECTOR), (cut, OCTETS, SCALAR)]
-    if e == LAST and piece == W1_HI:
-        cut = OCTETS - W1_SHARE
         return [(0, ROOM_OCTETS, VECTOR), (ROOM_OCTETS, cut, VECTOR), (cut, OCTETS, SCALAR)]
     return [(0, ROOM_OCTETS, VECTOR), (ROOM_OCTETS, OCTETS, VECTOR)]
 
 
-def leaving(e, piece):
-    if e == FIRST or piece == W2:
-        return []
-    if e == LAST:
-        return {W3_LO: [0], W3_HI: [1], W1_LO: [], W1_HI: [2]}[piece]
-    return [piece]
+def last_rounding(piece):
+    if piece == W3_LO:
+        return [(0, 2, SCALAR), (2, 4, VECTOR)]
+    if piece == W1_HI:
+        return [(0, 2, VECTOR), (2, 3, VECTOR), (3, 4, SCALAR)]
+    return [(0, 2, VECTOR), (2, 4, VECTOR)]
 
 
 def tile_moe_two_glu_relu_kernel(
@@ -107,21 +111,39 @@ def tile_moe_two_glu_relu_kernel(
         gate_cols = keep.tile([P, GATE_COLS], F32, name="gate_cols")
         gates = keep.tile([P, SLOTS], F32, name="gates")
         identity = keep.tile([P, P], F32, name="identity")
-        last_y = keep.tile([P, BLOCKS, C], F32, name="last_y")
+        last_y = keep.tile([P, BLOCKS + 1, C], F32, name="last_y")
+        last_b = keep.tile([P, 2 * BLOCK], F32, name="last_b", align_bytes=64)
+        bench = keep.tile([P, 2 * BLOCK], F32, name="bench", align_bytes=64)
         windows = [keep.tile([P, T], F32, name=f"window{r}") for r in range(BLOCKS)]
-        leads = [0 if e in (FIRST, LAST) else LEAD for e in range(E)]
-        w2_tiles = [keep.tile([P, leads[e] + PACK * H], F32, name=f"raw_w2_{e}", align_bytes=64) for e in range(E)]
+        leads = [0 if e == FIRST else LEAD for e in range(LAST)]
+        widths = [blocks_ahead(e) * P for e in range(LAST)]
+        w2_tiles = [
+            keep.tile([P, leads[e] + PACK * widths[e]], F32, name=f"raw_w2_{e}", align_bytes=64) for e in range(LAST)
+        ]
 
         def rows_of(flat):
             return flat.rearrange("p (k c) -> p k c", k=PACK)
 
+        def load_w2(raw, e, first, end):
+            if (e, first) in []:
+                rows = w2[e].rearrange("(g j d) c -> j g d c", j=PACK, d=PAIR)
+                for j in range(PACK):
+                    nc.sync.dma_start(out=rows_of(raw)[:, j, :], in_=rows[j][:, :, first:end])
+                return raw
+            rows = w2[e].rearrange("(g j d) c -> d g j c", j=PACK, d=PAIR)
+            for d in range(PAIR):
+                nc.sync.dma_start(out=rows_of(raw)[d:P:PAIR], in_=rows[d][:, :, first:end])
+            return raw
+
+        def load_blocks(e, first, end, spare):
+            words = PACK * (end - first) * P
+            tile = keep.tile([P, words + spare], F32, name=f"raw_w2_{e}_{first}", align_bytes=64)
+            load_w2(tile[:, :words], e, first * P, end * P)
+            return tile
+
         def load_piece(e, piece):
             if piece == W2:
-                raw = w2_tiles[e][:, leads[e] :]
-                rows = w2[e].rearrange("(g j d) c -> d g j c", j=PACK, d=PAIR)
-                for d in range(PAIR):
-                    nc.sync.dma_start(out=rows_of(raw)[d:P:PAIR], in_=rows[d])
-                return raw
+                return load_w2(w2_tiles[e][:, leads[e] :], e, 0, widths[e])
             tile = raws.tile([P, PACK * H], F32, name="raw")
             w = w3 if piece in (W3_LO, W3_HI) else w1
             o = piece % PASSES
@@ -129,14 +151,26 @@ def tile_moe_two_glu_relu_kernel(
             nc.sync.dma_start(out=tile[:], in_=rows.rearrange("(p k) c -> p (k c)", k=PACK))
             return tile[:]
 
+        def copy_on(engine, into, src):
+            if engine == SCALAR:
+                nc.scalar.copy(out=into, in_=src)
+            else:
+                nc.vector.tensor_copy(out=into, in_=src)
+
         def round_octets(raw, values, piece, first, end, engine):
             src = raw.rearrange("p (k g j d) -> p g j k d", k=PACK, j=PACK, d=PAIR)
             layout = "p (g j d k) -> p g j k d" if piece == W2 else "p (j g d k) -> p g j k d"
             into = values.rearrange(layout, j=PACK, d=PAIR, k=PACK)
-            if engine == SCALAR:
-                nc.scalar.copy(out=into[:, first:end], in_=src[:, first:end])
-            else:
-                nc.vector.tensor_copy(out=into[:, first:end], in_=src[:, first:end])
+            copy_on(engine, into[:, first:end], src[:, first:end])
+
+        def round_groups(raw, values, first, end, engine):
+            src = raw.rearrange("p (k g j d) -> p g j k d", k=PACK, j=PACK, d=PAIR)
+            into = values.rearrange("p (j g d k) -> p g j k d", j=PACK, d=PAIR, k=PACK)
+            copy_on(engine, into[:, :, first:end], src[:, :, first:end])
+
+        def round_columns(raw, values, engine):
+            src = raw.rearrange("p k (c d) -> p c k d", d=PAIR)
+            copy_on(engine, values.rearrange("p (c d k) -> p c k d", d=PAIR, k=PACK), src)
 
         def round_on_gpsimd(raw, into, first, end):
             src = raw.rearrange("p (k c) -> p c k", k=PACK)[:, OCTET * first : OCTET * end]
@@ -152,10 +186,10 @@ def tile_moe_two_glu_relu_kernel(
             nc.vector.quantize_mx(out=codes[:, first:end].bitcast(FP8X4), scales=scales[:, first:end], in_=values)
 
         def first_layer_pass(e, o, banks, matrix, groups):
-            values, codes, scales = matrix
-            for half, j in product(reversed(range(HALVES)), groups):
+            codes, scales, base = matrix
+            for half, j in product(halves_of(e), groups):
                 slots = slice(e * C + half * HALF, e * C + (half + 1) * HALF)
-                cols = slice(o * H + j * P, o * H + (j + 1) * P)
+                cols = slice(base + j * P, base + (j + 1) * P)
                 nc.tensor.matmul_mx(
                     out=banks[half][:, j, :],
                     lhsT=codes[:, cols].bitcast(FP8X4),
@@ -169,32 +203,34 @@ def tile_moe_two_glu_relu_kernel(
         def quantize_first_layer(e, piece, matrix, banks):
             values, codes, scales = matrix
             o = piece % PASSES
-            if e not in (FIRST, LAST) and piece in (W3_LO, W3_HI):
+            if e != FIRST and piece in (W3_LO, W3_HI):
                 if piece == W3_HI:
                     quantize(values[:], codes, scales, 0, PASSES * H)
                     for both in range(PASSES):
-                        first_layer_pass(e, both, banks, matrix, range(PACK))
+                        first_layer_pass(e, both, banks, (codes, scales, both * H), range(PACK))
                 return
-            calls = 2 if (e, piece) == (LAST, W1_HI) else 1
+            calls = 2 if piece == W1_HI and e in [2] else 1
             for call in range(calls):
-                first, end = o * H + call * H // calls, o * H + (call + 1) * H // calls
-                quantize(values[:, PACK * first : PACK * end], codes, scales, first, end)
-                first_layer_pass(e, o, banks, matrix, range(call * PACK // calls, (call + 1) * PACK // calls))
+                first, end = call * PACK // calls, (call + 1) * PACK // calls
+                words = o * H + first * P, o * H + end * P
+                quantize(values[:, PACK * words[0] : PACK * words[1]], codes, scales, *words)
+                first_layer_pass(e, o, banks, (codes, scales, o * H), range(first, end))
 
         def copy_b(e, banks, raw):
             b = {}
-            for half in reversed(range(HALVES)):
+            for half in halves_of(e):
                 if e == FIRST and half == HALVES - 1:
                     room = rows_of(raw)[:, :, :HALF]
+                elif e == LAST - 1:
+                    room = rows_of(bench[:, half * BLOCK : (half + 1) * BLOCK])
                 else:
-                    tile = once.tile([P, PACK * HALF], F32, name=f"b{half}")
-                    room = rows_of(tile[:])
+                    room = rows_of(last_b[:, half * BLOCK : (half + 1) * BLOCK])
                 b[half] = room.rearrange("p a (s j) -> p a s j", j=PACK)
                 nc.scalar.copy(out=b[half], in_=banks[half][:].rearrange("p j (a s) -> p a s j", a=PACK))
             return b
 
-        def make_h(banks_a, b, h):
-            for half in reversed(range(HALVES)):
+        def make_h(e, banks_a, b, h):
+            for half in halves_of(e):
                 nc.vector.scalar_tensor_tensor(
                     out=h[:, half * H : (half + 1) * H].rearrange("p (a s j) -> p a s j", a=PACK, j=PACK),
                     in0=banks_a[half][:].rearrange("p j (a s) -> p a s j", a=PACK),
@@ -212,22 +248,19 @@ def tile_moe_two_glu_relu_kernel(
                 quantize(h[:, PACK * first : PACK * end], codes, scales, first, end)
             return codes, scales
 
-        def second_layer(matrix, h_codes, h_scales, seats):
-            values, codes, scales = matrix
-            banks = [psum_y.tile([P, 2, C], F32, name="bank_y") for blocks in seats]
-            y = {r: bank[:, blocks.index(r), :] for bank, blocks in zip(banks, seats) for r in blocks}
-            for r in range(BLOCKS):
-                cols = slice(r * P, (r + 1) * P)
+        def second_layer(blocks, h_codes, h_scales):
+            bank = psum_y.tile([P, 2, C], F32, name="bank_y")
+            for n, (codes, scales, first) in enumerate(blocks):
                 nc.tensor.matmul_mx(
-                    out=y[r],
-                    lhsT=codes[:, cols].bitcast(FP8X4),
-                    lhsT_scale=scales[:, cols],
-                    rhs=h_codes[:].bitcast(FP8X4),
-                    rhs_scale=h_scales[:],
+                    out=bank[:, n, :],
+                    lhsT=codes[:, first : first + P].bitcast(FP8X4),
+                    lhsT_scale=scales[:, first : first + P],
+                    rhs=h_codes.bitcast(FP8X4),
+                    rhs_scale=h_scales,
                     start=True,
                     stop=True,
                 )
-            return y
+            return bank[:, : len(blocks), :]
 
         def gates_of(e):
             return gates[:, e * C : (e + 1) * C]
@@ -252,6 +285,12 @@ def tile_moe_two_glu_relu_kernel(
                     )
         raw = {}
         for e, piece in product(range(E), range(PIECES)):
+            if (e, piece) == (LAST, W2):
+                early_tile = load_blocks(LAST, 0, 2, P)
+                late = rows_of(load_blocks(LAST - 1, BLOCKS - 1, BLOCKS, 0)[:])
+                rest = rows_of(load_blocks(LAST, 2, BLOCKS, 0)[:])
+                early = rows_of(early_tile[:, : 2 * BLOCK])
+                continue
             raw[e, piece] = load_piece(e, piece)
             if (e, piece) == (FIRST, W3_LO):
                 nc.sync.dma_start(out=gate_cols[:], in_=gate[0, :].rearrange("(p c) -> p c", c=GATE_COLS))
@@ -273,71 +312,115 @@ def tile_moe_two_glu_relu_kernel(
                 in_=spread[:].rearrange("p c s -> p s c"),
             )
 
-        y = {}
-        for e in range(E):
-            middle = e not in (FIRST, LAST)
+        def gate_and_scatter(e, y, blocks, room):
+            spread_gates = gates_of(e).unsqueeze(1).to_broadcast([P, len(blocks), C])
+            nc.vector.tensor_tensor(room, y, spread_gates, ALU.mult)
+            for n, r in enumerate(blocks):
+                nc.scalar.activation(places(e, r), room[:, n, :], COPY)
+
+        y = []
+        for e in range(LAST):
             matrices = [new_matrix("w3", PASSES), new_matrix("w1", PASSES), new_matrix("w2", 1)]
             banks_b = [psum_b.tile([P, PACK, HALF], F32, name="bank") for half in range(HALVES)]
             banks_a = [psum_a.tile([P, PACK, HALF], F32, name="bank") for half in range(HALVES)]
-            if middle:
-                h = w2_tiles[e][:, : C * PACK // 2].bitcast(BF16)
-            else:
-                own = hidden.tile([P, C * PACK], BF16, name="h", align_bytes=64)
+            if leads[e] == 0:
+                own = once.tile([P, C * PACK], BF16, name="h", align_bytes=64)
                 h = own[:]
+            else:
+                h = w2_tiles[e][:, : C * PACK // 2].bitcast(BF16)
 
             for piece in range(W2):
                 matrix = matrices[piece // PASSES]
                 o = piece % PASSES
                 values = matrix[0][:, o * PACK * H : (o + 1) * PACK * H]
-                rooms = rows_of(raw[e, piece])[:, :, :C]
                 for first, end, engine in rounding(e, piece):
                     round_octets(raw[e, piece], values, piece, first, end, engine)
-                for r in leaving(e, piece):
-                    nc.vector.tensor_tensor(rooms[:, 0, :], y[r], gates_of(e - 1), ALU.mult)
-                    nc.scalar.activation(places(e - 1, r), rooms[:, 0, :], COPY)
+                if e > FIRST:
+                    gate_and_scatter(e - 1, y[piece], [piece], rows_of(raw[e, piece])[:, 0:1, :C])
                 if piece == W1_HI:
                     b = copy_b(e, banks_b, raw[e, piece])
                 quantize_first_layer(e, piece, matrix, banks_b if piece < W1_LO else banks_a)
 
-            if e == LAST:
-                kept = rows_of(raw[e, W1_HI])[:, 1, :C]
-                nc.vector.tensor_tensor(kept, y[KEPT_BLOCK], gates_of(e - 1), ALU.mult)
-            if not middle:
-                make_h(banks_a, b, h)
-                h_codes, h_scales = quantize_h(h, HALVES)
-
             values, codes, scales = matrices[W2 // PASSES]
-            if middle:
-                aside = raw[e, W2][:, H_OCTETS * OCTET : H_OCTETS * OCTET + P * PACK // 2].bitcast(BF16)
-            else:
-                aside = matrices[W1_HI // PASSES][0][:, PASSES * PACK * H - P * PACK :]
             parts = rounding(e, W2)
-            for first, end, engine in parts:
-                if engine == GPSIMD:
-                    if middle:
-                        make_h(banks_a, b, h)
-                    round_on_gpsimd(raw[e, W2], aside, first, end)
-                else:
+            shift = P if e == LAST - 1 else 0
+            if e == FIRST:
+                make_h(e, banks_a, b, h)
+                h_codes, h_scales = quantize_h(h, HALVES)
+                for first, end, engine in parts:
                     round_octets(raw[e, W2], values[:], W2, first, end, engine)
-            if middle:
-                parts = [(0, parts[1][1], VECTOR), parts[2]]
-            for first, end, engine in parts:
-                first, end = OCTET * first, OCTET * end
-                source = aside if engine == GPSIMD else values[:, PACK * first : PACK * end]
-                quantize(source, codes, scales, first, end)
-                if middle and first == 0:
-                    h_codes, h_scales = quantize_h(h, 1)
-
-            seats = [[r] for r in range(BLOCKS)] if e == LAST else SEATS
-            y = second_layer(matrices[W2 // PASSES], h_codes, h_scales, seats)
-
-        for r in range(BLOCKS):
-            if r % 2 == 0:
-                nc.scalar.copy(last_y[:, r, :], y[r])
-                nc.vector.tensor_tensor(places(LAST, r), last_y[:, r, :], gates_of(LAST), ALU.mult)
+                for first, end, engine in parts:
+                    first, end = OCTET * first, OCTET * end
+                    quantize(values[:, PACK * first : PACK * end], codes, scales, first, end)
             else:
-                nc.vector.tensor_tensor(last_y[:, r, :], y[r], gates_of(LAST), ALU.mult)
-                nc.scalar.activation(places(LAST, r), last_y[:, r, :], COPY)
-        nc.scalar.activation(places(LAST - 1, KEPT_BLOCK), kept, COPY)
+                start = widths[e]
+                aside = raw[e, W2][:, start : start + P * PACK // 2].bitcast(BF16)
+                for first, end, engine in parts[:-1]:
+                    round_octets(raw[e, W2], values[:, : PACK * widths[e]], W2, first, end, engine)
+                make_h(e, banks_a, b, h)
+                round_on_gpsimd(raw[e, W2], aside, parts[-1][0], parts[-1][1])
+                cut = widths[e] - P
+                quantize(values[:, : PACK * cut], codes, scales, shift, shift + cut)
+                h_codes, h_scales = quantize_h(h, 1)
+                quantize(aside, codes, scales, shift + cut, shift + cut + P)
+            blocks = [(codes, scales, shift + r * P) for r in range(blocks_ahead(e))]
+            if e < LAST - 1:
+                y = [second_layer(blocks[r : r + 1], h_codes[:], h_scales[:]) for r in range(2)]
+                both = second_layer(blocks[2:], h_codes[:], h_scales[:])
+                y = y + [both[:, n : n + 1, :] for n in range(2)]
+
+        y = [second_layer(blocks[r : r + 1], h_codes[:], h_scales[:]) for r in range(BLOCKS - 1)]
+        third = y[2]
+        room = once.tile([P, 2, C], F32, name="room")
+        for r in range(2):
+            gate_and_scatter(LAST - 1, y[r], [r], room[:, r : r + 1, :])
+        old_h = (h_codes[:], h_scales[:])
+
+        banks_b = [psum_b.tile([P, PACK, HALF], F32, name="bank") for half in range(HALVES)]
+        banks_a = [psum_a.tile([P, PACK, HALF], F32, name="bank") for half in range(HALVES)]
+        spent = bench[:].bitcast(BF16)
+        h = early.rearrange("p k c -> p (k c)")[:, :BLOCK].bitcast(BF16)
+        back = coded.tile([P, H], U32, name="codes_w2", align_bytes=64)
+        back_scales = coded.tile([P, H], U8, name="scales_w2", align_bytes=64)
+        front = coded.tile([P, PASSES * H], U32, name="codes_w3", align_bytes=64)
+        front_scales = coded.tile([P, PASSES * H], U8, name="scales_w3", align_bytes=64)
+        w1_codes = coded.tile([P, PASSES * H], U32, name="codes_w1", align_bytes=64)
+        w1_scales = coded.tile([P, PASSES * H], U8, name="scales_w1", align_bytes=64)
+        homes = [(codes, scales, 0), (front, front_scales, 0), (w1_codes, w1_scales, 0), (w1_codes, w1_scales, H)]
+        for piece in range(W2):
+            into, into_scales, base = homes[piece]
+            for first, end, engine in last_rounding(piece):
+                round_groups(raw[LAST, piece], spent, first, end, engine)
+            for first in (0, 2):
+                end = first + 2
+                quantize(spent[:, first * BLOCK : end * BLOCK], into, into_scales, base + first * P, base + end * P)
+                banks = banks_b if piece < W1_LO else banks_a
+                first_layer_pass(LAST, piece % PASSES, banks, homes[piece], range(first, end))
+            if piece == W3_HI:
+                b = copy_b(LAST, banks_b, None)
+
+        round_columns(early[:, :, :P], spent[:, :BLOCK], SCALAR)
+        round_columns(early[:, :, P:], spent[:, BLOCK : 2 * BLOCK], VECTOR)
+        gate_and_scatter(LAST - 1, third, [2], early_tile[:, 2 * BLOCK - P :].unsqueeze(1))
+        quantize(spent[:, : 2 * BLOCK], front, front_scales, H, H + 2 * P)
+        make_h(LAST, banks_a, b, h)
+        rest_values, late_values = last_b[:, :BLOCK].bitcast(BF16), h[:, :BLOCK]
+        round_columns(rest, rest_values, SCALAR)
+        for half in range(HALVES):
+            quantize(h[:, half * BLOCK : (half + 1) * BLOCK], back, back_scales, half * P, (half + 1) * P)
+        hidden_now = (back[:, : 2 * P], back_scales[:, : 2 * P])
+        y = [second_layer([(front, front_scales, H + r * P)], *hidden_now) for r in range(2)]
+        round_columns(late, late_values, VECTOR)
+        quantize(late_values, back, back_scales, 2 * P, 3 * P)
+        y_late = second_layer([(back, back_scales, 2 * P)], *old_h)
+        copy_on(VECTOR, last_y[:, 0:1, :], y[0])
+        gate_and_scatter(LAST, y[1], [1], last_y[:, 1:2, :])
+        nc.vector.tensor_tensor(places(LAST, 0), last_y[:, 0, :], gates_of(LAST), ALU.mult)
+        quantize(rest_values, front, front_scales, H, H + 2 * P)
+        gate_and_scatter(LAST - 1, y_late, [3], last_y[:, 4:5, :])
+        y = [second_layer([(front, front_scales, H + n * P)], *hidden_now) for n in range(2)]
+        nc.vector.tensor_copy(last_y[:, 2:3, :], y[0])
+        gate_and_scatter(LAST, y[1], [3], last_y[:, 3:4, :])
+        nc.vector.tensor_tensor(places(LAST, 2), last_y[:, 2, :], gates_of(LAST), ALU.mult)
         for r in range(BLOCKS):
             nc.sync.dma_start(out=out[r * P : (r + 1) * P, :], in_=windows[r][:])

@@ -72,9 +72,6 @@ def rounding(e, piece):
         return [(0, OCTETS, VECTOR if piece == W1_LO else SCALAR)]
     if piece == W3_LO:
         return [(0, ROOM_OCTETS, SCALAR), (ROOM_OCTETS, OCTETS, VECTOR)]
-    if piece == W1_LO:
-        cut = OCTETS - BLOCK_OCTETS
-        return [(0, ROOM_OCTETS, VECTOR), (ROOM_OCTETS, cut, VECTOR), (cut, OCTETS, SCALAR)]
     return [(0, ROOM_OCTETS, VECTOR), (ROOM_OCTETS, OCTETS, VECTOR)]
 
 

@@ -110,7 +110,7 @@ def tile_moe_two_glu_relu_kernel(
         identity = keep.tile([P, P], F32, name="identity")
         last_y = keep.tile([P, BLOCKS + 1, C], F32, name="last_y")
         last_b = keep.tile([P, 2 * BLOCK], F32, name="last_b", align_bytes=64)
-        bench = keep.tile([P, 2 * BLOCK], F32, name="bench", align_bytes=64)
+        bench = keep.tile([P, 4 * BLOCK], F32, name="bench", align_bytes=64)
         windows = [keep.tile([P, T], F32, name=f"window{r}") for r in range(BLOCKS)]
         leads = [0 if e == FIRST else LEAD for e in range(LAST)]
         widths = [blocks_ahead(e) * P for e in range(LAST)]
@@ -141,7 +141,7 @@ def tile_moe_two_glu_relu_kernel(
         def load_piece(e, piece):
             if piece == W2:
                 return load_w2(w2_tiles[e][:, leads[e] :], e, 0, widths[e])
-            tile = raws.tile([P, PACK * H], F32, name="raw")
+            tile = raws.tile([P, PACK * H], F32, name="raw", align_bytes=64)
             w = w3 if piece in (W3_LO, W3_HI) else w1
             o = piece % PASSES
             rows = w[e, o * K_PASS : (o + 1) * K_PASS, :]
@@ -218,6 +218,8 @@ def tile_moe_two_glu_relu_kernel(
             for half in halves_of(e):
                 if e == FIRST and half == HALVES - 1:
                     room = rows_of(raw)[:, :, :HALF]
+                elif e == LAST:
+                    room = rows_of(raw[:, half * BLOCK : (half + 1) * BLOCK])
                 elif e == LAST - 1:
                     room = rows_of(bench[:, half * BLOCK : (half + 1) * BLOCK])
                 else:
@@ -340,7 +342,7 @@ def tile_moe_two_glu_relu_kernel(
 
             values, codes, scales = matrices[W2 // PASSES]
             parts = rounding(e, W2)
-            shift = P if e == LAST - 1 else 0
+            shift = 0
             if e == FIRST:
                 make_h(e, banks_a, b, h)
                 h_codes, h_scales = quantize_h(h, HALVES)
@@ -368,14 +370,14 @@ def tile_moe_two_glu_relu_kernel(
 
         y = [second_layer(blocks[r : r + 1], h_codes[:], h_scales[:]) for r in range(BLOCKS - 1)]
         third = y[2]
-        room = once.tile([P, 2, C], F32, name="room")
-        for r in range(2):
-            gate_and_scatter(LAST - 1, y[r], [r], room[:, r : r + 1, :])
+        gate_and_scatter(LAST - 1, y[0], [0], last_y[:, 0:1, :])
         old_h = (h_codes[:], h_scales[:])
 
         banks_b = [psum_b.tile([P, PACK, HALF], F32, name="bank") for half in range(HALVES)]
         banks_a = [psum_a.tile([P, PACK, HALF], F32, name="bank") for half in range(HALVES)]
-        spent = bench[:].bitcast(BF16)
+        w3_values = bench[:].bitcast(BF16)
+        w1_values = rounded.tile([P, PASSES * PACK * H], BF16, name="values_w1", align_bytes=64)
+        spent = w1_values[:, PACK * H :]
         h = early.rearrange("p k c -> p (k c)")[:, :BLOCK].bitcast(BF16)
         back = coded.tile([P, H], U32, name="codes_w2", align_bytes=64)
         back_scales = coded.tile([P, H], U8, name="scales_w2", align_bytes=64)
@@ -383,39 +385,44 @@ def tile_moe_two_glu_relu_kernel(
         front_scales = coded.tile([P, PASSES * H], U8, name="scales_w3", align_bytes=64)
         w1_codes = coded.tile([P, PASSES * H], U32, name="codes_w1", align_bytes=64)
         w1_scales = coded.tile([P, PASSES * H], U8, name="scales_w1", align_bytes=64)
-        homes = [(codes, scales, 0), (front, front_scales, 0), (w1_codes, w1_scales, 0), (w1_codes, w1_scales, H)]
-        for piece in range(W2):
-            into, into_scales, base = homes[piece]
+        for first, end, engine in last_rounding(W3_LO):
+            round_groups(raw[LAST, W3_LO], w3_values[:, : PACK * H], first, end, engine)
+        for first, end, engine in rounding(LAST, W3_HI):
+            round_octets(raw[LAST, W3_HI], w3_values[:, PACK * H :], W3_HI, first, end, engine)
+        gate_and_scatter(LAST - 1, y[1], [1], rows_of(raw[LAST, W3_HI])[:, 0:1, :C])
+        quantize(w3_values, front, front_scales, 0, PASSES * H)
+        for o in range(PASSES):
+            first_layer_pass(LAST, o, banks_b, (front, front_scales, o * H), range(PACK))
+        for o, piece in enumerate((W1_LO, W1_HI)):
+            values = w1_values[:, o * PACK * H : (o + 1) * PACK * H]
             for first, end, engine in last_rounding(piece):
-                round_groups(raw[LAST, piece], spent, first, end, engine)
+                round_groups(raw[LAST, piece], values, first, end, engine)
             for first in (0, 2):
-                end = first + 2
-                quantize(spent[:, first * BLOCK : end * BLOCK], into, into_scales, base + first * P, base + end * P)
-                banks = banks_b if piece < W1_LO else banks_a
-                first_layer_pass(LAST, piece % PASSES, banks, homes[piece], range(first, end))
-            if piece == W3_HI:
-                b = copy_b(LAST, banks_b, None)
+                words = o * H + first * P, o * H + (first + 2) * P
+                quantize(values[:, first * BLOCK : (first + 2) * BLOCK], w1_codes, w1_scales, *words)
+                first_layer_pass(LAST, o, banks_a, (w1_codes, w1_scales, o * H), range(first, first + 2))
 
-        round_columns(early[:, :, :P], spent[:, :BLOCK], SCALAR)
+        b = copy_b(LAST, banks_b, raw[LAST, W1_HI])
         round_columns(early[:, :, P:], spent[:, BLOCK : 2 * BLOCK], VECTOR)
+        round_columns(early[:, :, :P], spent[:, :BLOCK], VECTOR)
         gate_and_scatter(LAST - 1, third, [2], early_tile[:, 2 * BLOCK - P :].unsqueeze(1))
-        quantize(spent[:, : 2 * BLOCK], front, front_scales, H, H + 2 * P)
+        quantize(spent[:, : 2 * BLOCK], codes, scales, 0, 2 * P)
         make_h(LAST, banks_a, b, h)
-        rest_values, late_values = last_b[:, :BLOCK].bitcast(BF16), h[:, :BLOCK]
+        rest_values, late_values = raw[LAST, W1_HI][:, :BLOCK].bitcast(BF16), h[:, :BLOCK]
         round_columns(rest, rest_values, SCALAR)
         for half in range(HALVES):
             quantize(h[:, half * BLOCK : (half + 1) * BLOCK], back, back_scales, half * P, (half + 1) * P)
         hidden_now = (back[:, : 2 * P], back_scales[:, : 2 * P])
-        y = [second_layer([(front, front_scales, H + r * P)], *hidden_now) for r in range(2)]
+        y = [second_layer([(codes, scales, r * P)], *hidden_now) for r in range(2)]
         round_columns(late, late_values, VECTOR)
         quantize(late_values, back, back_scales, 2 * P, 3 * P)
         y_late = second_layer([(back, back_scales, 2 * P)], *old_h)
         copy_on(VECTOR, last_y[:, 0:1, :], y[0])
         gate_and_scatter(LAST, y[1], [1], last_y[:, 1:2, :])
         nc.vector.tensor_tensor(places(LAST, 0), last_y[:, 0, :], gates_of(LAST), ALU.mult)
-        quantize(rest_values, front, front_scales, H, H + 2 * P)
+        quantize(rest_values, codes, scales, 0, 2 * P)
         gate_and_scatter(LAST - 1, y_late, [3], last_y[:, 4:5, :])
-        y = [second_layer([(front, front_scales, H + n * P)], *hidden_now) for n in range(2)]
+        y = [second_layer([(codes, scales, n * P)], *hidden_now) for n in range(2)]
         nc.vector.tensor_copy(last_y[:, 2:3, :], y[0])
         gate_and_scatter(LAST, y[1], [3], last_y[:, 3:4, :])
         nc.vector.tensor_tensor(places(LAST, 2), last_y[:, 2, :], gates_of(LAST), ALU.mult)

@@ -155,19 +155,22 @@ def tile_moe_two_glu_relu_kernel(
                 nc.vector.tensor_copy(out=into, in_=src)
 
         def round_octets(raw, values, piece, first, end, engine):
-            src = raw.rearrange("p (k g j d) -> p g j k d", k=PACK, j=PACK, d=PAIR)
-            layout = "p (g j d k) -> p g j k d" if piece == W2 else "p (j g d k) -> p g j k d"
-            into = values.rearrange(layout, j=PACK, d=PAIR, k=PACK)
-            copy_on(engine, into[:, first:end], src[:, first:end])
+            if piece == W2:
+                cols = slice(OCTET * first, OCTET * end)
+                round_columns(rows_of(raw)[:, :, cols], values[:, PACK * cols.start : PACK * cols.stop], engine)
+            else:
+                src = raw.rearrange("p (k g j d) -> p g j k d", k=PACK, j=PACK, d=PAIR)
+                into = values.rearrange("p (j g d k) -> p g j k d", j=PACK, d=PAIR, k=PACK)
+                copy_on(engine, into[:, first:end], src[:, first:end])
 
         def round_groups(raw, values, first, end, engine):
-            src = raw.rearrange("p (k g j d) -> p g j k d", k=PACK, j=PACK, d=PAIR)
-            into = values.rearrange("p (j g d k) -> p g j k d", j=PACK, d=PAIR, k=PACK)
-            copy_on(engine, into[:, :, first:end], src[:, :, first:end])
+            src = raw.rearrange("p (k g j d) -> p g k j d", k=PACK, j=PACK, d=PAIR)
+            into = values.rearrange("p (j g d k) -> p g k j d", j=PACK, d=PAIR, k=PACK)
+            copy_on(engine, into[:, :, :, first:end], src[:, :, :, first:end])
 
         def round_columns(raw, values, engine):
-            src = raw.rearrange("p k (c d) -> p c k d", d=PAIR)
-            copy_on(engine, values.rearrange("p (c d k) -> p c k d", d=PAIR, k=PACK), src)
+            src = raw.rearrange("p k (c d) -> p c k d", d=PACK)
+            copy_on(engine, values.rearrange("p (c d k) -> p c k d", d=PACK, k=PACK), src)
 
         def round_on_gpsimd(raw, into, first, end):
             src = raw.rearrange("p (k c) -> p c k", k=PACK)[:, OCTET * first : OCTET * end]

@@ -185,36 +185,46 @@ def tile_moe_two_glu_relu_kernel(
         def quantize(values, codes, scales, first, end):
             nc.vector.quantize_mx(out=codes[:, first:end].bitcast(FP8X4), scales=scales[:, first:end], in_=values)
 
-        def first_layer_pass(e, o, banks, matrix, groups):
-            codes, scales, base = matrix
-            for half, j in product(halves_of(e), groups):
+        def first_layer(e, banks, codes, scales, parts):
+            for half, (o, j, first) in product(halves_of(e), parts):
                 slots = slice(e * C + half * HALF, e * C + (half + 1) * HALF)
-                cols = slice(base + j * P, base + (j + 1) * P)
                 nc.tensor.matmul_mx(
                     out=banks[half][:, j, :],
-                    lhsT=codes[:, cols].bitcast(FP8X4),
-                    lhsT_scale=scales[:, cols],
+                    lhsT=codes[:, first : first + P].bitcast(FP8X4),
+                    lhsT_scale=scales[:, first : first + P],
                     rhs=slot_words[o][:, slots].bitcast(FP8X4),
                     rhs_scale=slot_scales[SCALE_ROWS * o :, slots],
                     start=(o == 0 and j == 0),
                     stop=(o == PASSES - 1 and j == PACK - 1),
                 )
 
-        def quantize_first_layer(e, piece, matrix, banks):
-            values, codes, scales = matrix
-            o = piece % PASSES
-            if e != FIRST and piece in (W3_LO, W3_HI):
-                if piece == W3_HI:
-                    quantize(values[:], codes, scales, 0, PASSES * H)
-                    for both in range(PASSES):
-                        first_layer_pass(e, both, banks, (codes, scales, both * H), range(PACK))
-                return
-            calls = 2 if piece == W1_HI and e in [2] else 1
-            for call in range(calls):
-                first, end = call * PACK // calls, (call + 1) * PACK // calls
-                words = o * H + first * P, o * H + end * P
+        def round_pair(raw, into, pair, engine):
+            src = raw.rearrange("p (k g j d) -> p g k j d", k=PACK, j=PACK, d=PAIR)[:, :, :, 2 * pair : 2 * pair + 2]
+            copy_on(engine, into.rearrange("p (j g d k) -> p g k j d", j=2, d=PAIR, k=PACK), src)
+
+        def w3_high(e, values, codes, scales, banks, between):
+            for pair in range(2):
+                round_pair(raw[e, W3_HI], values[:, 6 * pair * BLOCK : (6 * pair + 2) * BLOCK], pair, SCALAR if e == FIRST else VECTOR)
+            for pair in range(2):
+                low = [(0, j, (2 + j) * P) for j in (2 * pair, 2 * pair + 1)]
+                high = [(1, j, (j + 4 * pair) * P) for j in (2 * pair, 2 * pair + 1)]
+                if e == FIRST:
+                    first = 6 * pair * P
+                    quantize(values[:, PACK * first : PACK * first + 2 * BLOCK], codes, scales, first, first + 2 * P)
+                    first_layer(e, banks, codes, scales, high)
+                else:
+                    quantize(values[:, pair * PACK * H : (pair + 1) * PACK * H], codes, scales, pair * H, (pair + 1) * H)
+                    first_layer(e, banks, codes, scales, low + high)
+                    if pair == 0:
+                        between()
+
+        def w1_pass(e, o, values, codes, scales, banks, between):
+            for pair in range(2):
+                words = o * H + 2 * pair * P, o * H + 2 * (pair + 1) * P
                 quantize(values[:, PACK * words[0] : PACK * words[1]], codes, scales, *words)
-                first_layer_pass(e, o, banks, (codes, scales, o * H), range(first, end))
+                first_layer(e, banks, codes, scales, [(o, j, o * H + j * P) for j in (2 * pair, 2 * pair + 1)])
+                if pair == 0:
+                    between()
 
         def copy_b(e, banks, raw):
             b = {}
@@ -224,7 +234,7 @@ def tile_moe_two_glu_relu_kernel(
                 elif e == LAST:
                     room = rows_of(raw[:, half * BLOCK : (half + 1) * BLOCK])
                 elif e == LAST - 1:
-                    room = rows_of(bench[:, half * BLOCK : (half + 1) * BLOCK])
+                    room = rows_of(bench[:, (half + 1) * BLOCK : (half + 2) * BLOCK])
                 else:
                     room = rows_of(last_b[:, half * BLOCK : (half + 1) * BLOCK])
                 b[half] = room.rearrange("p a (s j) -> p a s j", j=PACK)
@@ -331,17 +341,34 @@ def tile_moe_two_glu_relu_kernel(
             else:
                 h = w2_tiles[e][:, : C * PACK // 2].bitcast(BF16)
 
-            for piece in range(W2):
-                matrix = matrices[piece // PASSES]
-                o = piece % PASSES
-                values = matrix[0][:, o * PACK * H : (o + 1) * PACK * H]
-                for first, end, engine in rounding(e, piece):
-                    round_octets(raw[e, piece], values, piece, first, end, engine)
+            def leave(piece):
                 if e > FIRST:
                     gate_and_scatter(e - 1, y[piece], [piece], rows_of(raw[e, piece])[:, 0:1, :C])
+
+            values, codes, scales = matrices[0]
+            low = values[:, 2 * BLOCK : 6 * BLOCK]
+            if e == FIRST:
+                for pair in range(2):
+                    round_pair(raw[e, W3_LO], low[:, 2 * pair * BLOCK : 2 * (pair + 1) * BLOCK], pair, SCALAR)
+                quantize(low, codes, scales, 2 * P, 6 * P)
+                first_layer(e, banks_b, codes, scales, [(0, j, (2 + j) * P) for j in range(PACK)])
+            else:
+                for first, end, engine in rounding(e, W3_LO):
+                    round_octets(raw[e, W3_LO], low, W3_LO, first, end, engine)
+            leave(W3_LO)
+            w3_high(e, values, codes, scales, banks_b, lambda: leave(W3_HI))
+            values, codes, scales = matrices[1]
+            for o, piece in enumerate((W1_LO, W1_HI)):
+                part = values[:, o * PACK * H : (o + 1) * PACK * H]
+                if (e, piece) == (FIRST, W1_HI):
+                    for first, end, engine in rounding(e, piece):
+                        round_octets(raw[e, piece], part, piece, first, end, engine)
+                else:
+                    for pair in range(2):
+                        round_pair(raw[e, piece], part[:, 2 * pair * BLOCK : 2 * (pair + 1) * BLOCK], pair, VECTOR)
                 if piece == W1_HI:
                     b = copy_b(e, banks_b, raw[e, piece])
-                quantize_first_layer(e, piece, matrix, banks_b if piece < W1_LO else banks_a)
+                w1_pass(e, o, values, codes, scales, banks_a, lambda: leave(piece))
 
             values, codes, scales = matrices[W2 // PASSES]
             parts = rounding(e, W2)
@@ -389,21 +416,14 @@ def tile_moe_two_glu_relu_kernel(
         w1_codes = coded.tile([P, PASSES * H], U32, name="codes_w1", align_bytes=64)
         w1_scales = coded.tile([P, PASSES * H], U8, name="scales_w1", align_bytes=64)
         for first, end, engine in last_rounding(W3_LO):
-            round_groups(raw[LAST, W3_LO], w3_values[:, : PACK * H], first, end, engine)
-        for first, end, engine in rounding(LAST, W3_HI):
-            round_octets(raw[LAST, W3_HI], w3_values[:, PACK * H :], W3_HI, first, end, engine)
-        gate_and_scatter(LAST - 1, y[1], [1], rows_of(raw[LAST, W3_HI])[:, 0:1, :C])
-        quantize(w3_values, front, front_scales, 0, PASSES * H)
-        for o in range(PASSES):
-            first_layer_pass(LAST, o, banks_b, (front, front_scales, o * H), range(PACK))
+            round_groups(raw[LAST, W3_LO], w3_values[:, 2 * BLOCK : 6 * BLOCK], first, end, engine)
+        second_room = rows_of(raw[LAST, W3_HI])[:, 0:1, :C]
+        w3_high(LAST, w3_values, front, front_scales, banks_b, lambda: gate_and_scatter(LAST - 1, y[1], [1], second_room))
         for o, piece in enumerate((W1_LO, W1_HI)):
             values = w1_values[:, o * PACK * H : (o + 1) * PACK * H]
             for first, end, engine in last_rounding(piece):
                 round_groups(raw[LAST, piece], values, first, end, engine)
-            for first in (0, 2):
-                words = o * H + first * P, o * H + (first + 2) * P
-                quantize(values[:, first * BLOCK : (first + 2) * BLOCK], w1_codes, w1_scales, *words)
-                first_layer_pass(LAST, o, banks_a, (w1_codes, w1_scales, o * H), range(first, first + 2))
+            w1_pass(LAST, o, w1_values, w1_codes, w1_scales, banks_a, lambda: None)
 
         b = copy_b(LAST, banks_b, raw[LAST, W1_HI])
         round_columns(early[:, :, P:], spent[:, BLOCK : 2 * BLOCK], VECTOR)

@@ -52,6 +52,9 @@ RAW_BUFS = 8
 BLOCK = P * PACK
 
 
+WHOLE = (FIRST, FIRST + 1)
+
+
 def halves_of(e):
     return range(HALVES) if e == LAST else range(HALVES - 1, -1, -1)
 
@@ -122,10 +125,10 @@ def tile_moe_two_glu_relu_kernel(
             return flat.rearrange("p (k c) -> p k c", k=PACK)
 
         def load_w2(raw, e, first, end):
-            if (e, first) in []:
-                rows = w2[e].rearrange("(g j d) c -> j g d c", j=PACK, d=PAIR)
-                for j in range(PACK):
-                    nc.sync.dma_start(out=rows_of(raw)[:, j, :], in_=rows[j][:, :, first:end])
+            if e in WHOLE:
+                rows = w2[e].rearrange("(g a d b) c -> d g a (b c)", a=2, d=PAIR, b=2)
+                for d in range(PAIR):
+                    nc.sync.dma_start(out=raw.rearrange("p (a r) -> p a r", a=2)[d:P:PAIR], in_=rows[d])
                 return raw
             rows = w2[e].rearrange("(g j d) c -> d g j c", j=PACK, d=PAIR)
             for d in range(PAIR):
@@ -198,13 +201,18 @@ def tile_moe_two_glu_relu_kernel(
                     stop=(o == PASSES - 1 and j == PACK - 1),
                 )
 
-        def round_pair(raw, into, pair, engine):
-            src = raw.rearrange("p (k g j d) -> p g k j d", k=PACK, j=PACK, d=PAIR)[:, :, :, 2 * pair : 2 * pair + 2]
-            copy_on(engine, into.rearrange("p (j g d k) -> p g k j d", j=2, d=PAIR, k=PACK), src)
+        def round_pair(e, raw, into, pair, engine, first=0, end=OCTETS):
+            if e in WHOLE:
+                src = raw.rearrange("p (k g a d b) -> p a g k d b", k=PACK, a=2, d=PAIR, b=2)[:, pair]
+                into = into.rearrange("p (b g d k) -> p g k d b", b=2, d=PAIR, k=PACK)
+            else:
+                src = raw.rearrange("p (k g a b d) -> p a g k b d", k=PACK, a=2, d=PAIR, b=2)[:, pair]
+                into = into.rearrange("p (b g d k) -> p g k b d", b=2, d=PAIR, k=PACK)
+            copy_on(engine, into[:, first:end], src[:, first:end])
 
         def w3_high(e, values, codes, scales, banks, between):
             for pair in range(2):
-                round_pair(raw[e, W3_HI], values[:, 6 * pair * BLOCK : (6 * pair + 2) * BLOCK], pair, SCALAR if e == FIRST else VECTOR)
+                round_pair(e, raw[e, W3_HI], values[:, 6 * pair * BLOCK : (6 * pair + 2) * BLOCK], pair, SCALAR if e == FIRST else VECTOR)
             for pair in range(2):
                 low = [(0, j, (2 + j) * P) for j in (2 * pair, 2 * pair + 1)]
                 high = [(1, j, (j + 4 * pair) * P) for j in (2 * pair, 2 * pair + 1)]
@@ -349,23 +357,24 @@ def tile_moe_two_glu_relu_kernel(
             low = values[:, 2 * BLOCK : 6 * BLOCK]
             if e == FIRST:
                 for pair in range(2):
-                    round_pair(raw[e, W3_LO], low[:, 2 * pair * BLOCK : 2 * (pair + 1) * BLOCK], pair, SCALAR)
+                    round_pair(e, raw[e, W3_LO], low[:, 2 * pair * BLOCK : 2 * (pair + 1) * BLOCK], pair, SCALAR)
                 quantize(low, codes, scales, 2 * P, 6 * P)
                 first_layer(e, banks_b, codes, scales, [(0, j, (2 + j) * P) for j in range(PACK)])
             else:
-                for first, end, engine in rounding(e, W3_LO):
-                    round_octets(raw[e, W3_LO], low, W3_LO, first, end, engine)
+                for pair, engine in enumerate((SCALAR, VECTOR)):
+                    round_pair(e, raw[e, W3_LO], low[:, 2 * pair * BLOCK : 2 * (pair + 1) * BLOCK], pair, engine)
             leave(W3_LO)
             w3_high(e, values, codes, scales, banks_b, lambda: leave(W3_HI))
             values, codes, scales = matrices[1]
             for o, piece in enumerate((W1_LO, W1_HI)):
                 part = values[:, o * PACK * H : (o + 1) * PACK * H]
                 if (e, piece) == (FIRST, W1_HI):
-                    for first, end, engine in rounding(e, piece):
-                        round_octets(raw[e, piece], part, piece, first, end, engine)
+                    round_pair(e, raw[e, piece], part[:, : 2 * BLOCK], 0, VECTOR)
+                    round_pair(e, raw[e, piece], part[:, 2 * BLOCK :], 1, SCALAR, 0, 2 * W1_SHARE)
+                    round_pair(e, raw[e, piece], part[:, 2 * BLOCK :], 1, VECTOR, 2 * W1_SHARE, OCTETS)
                 else:
                     for pair in range(2):
-                        round_pair(raw[e, piece], part[:, 2 * pair * BLOCK : 2 * (pair + 1) * BLOCK], pair, VECTOR)
+                        round_pair(e, raw[e, piece], part[:, 2 * pair * BLOCK : 2 * (pair + 1) * BLOCK], pair, VECTOR)
                 if piece == W1_HI:
                     b = copy_b(e, banks_b, raw[e, piece])
                 w1_pass(e, o, values, codes, scales, banks_a, lambda: leave(piece))

@@ -67,7 +67,7 @@ def rounding(e, piece):
     if piece == W2:
         end = blocks_ahead(e) * BLOCK_OCTETS
         if e == FIRST:
-            return [(0, OCTETS // 2, SCALAR), (OCTETS // 2, OCTETS, SCALAR)]
+            return [(0, OCTETS // 2, SCALAR), (OCTETS // 2, end - BLOCK_OCTETS, SCALAR), (end - BLOCK_OCTETS, end, GPSIMD)]
         return [(0, H_OCTETS, VECTOR), (H_OCTETS, end - BLOCK_OCTETS, VECTOR), (end - BLOCK_OCTETS, end, GPSIMD)]
     if e == FIRST:
         if piece == W1_HI:
@@ -385,11 +385,14 @@ def tile_moe_two_glu_relu_kernel(
             if e == FIRST:
                 make_h(e, banks_a, b, h)
                 h_codes, h_scales = quantize_h(h, HALVES)
-                for first, end, engine in parts:
+                aside = matrices[1][0][:, 7 * BLOCK :]
+                round_on_gpsimd(raw[e, W2], aside, parts[-1][0], parts[-1][1])
+                for first, end, engine in parts[:-1]:
                     round_octets(raw[e, W2], values[:], W2, first, end, engine)
-                for first, end, engine in parts:
+                for first, end, engine in parts[:-1]:
                     first, end = OCTET * first, OCTET * end
                     quantize(values[:, PACK * first : PACK * end], codes, scales, first, end)
+                quantize(aside, codes, scales, N - P, N)
             else:
                 start = widths[e]
                 aside = raw[e, W2][:, start : start + P * PACK // 2].bitcast(BF16)
@@ -430,8 +433,12 @@ def tile_moe_two_glu_relu_kernel(
         w3_high(LAST, w3_values, front, front_scales, banks_b, lambda: gate_and_scatter(LAST - 1, y[1], [1], second_room))
         for o, piece in enumerate((W1_LO, W1_HI)):
             values = w1_values[:, o * PACK * H : (o + 1) * PACK * H]
-            for first, end, engine in last_rounding(piece):
-                round_groups(raw[LAST, piece], values, first, end, engine)
+            round_pair(LAST, raw[LAST, piece], values[:, : 2 * BLOCK], 0, VECTOR)
+            if piece == W1_LO:
+                round_pair(LAST, raw[LAST, piece], values[:, 2 * BLOCK :], 1, VECTOR)
+            else:
+                round_pair(LAST, raw[LAST, piece], values[:, 2 * BLOCK :], 1, VECTOR, 0, ROOM_OCTETS)
+                round_pair(LAST, raw[LAST, piece], values[:, 2 * BLOCK :], 1, SCALAR, ROOM_OCTETS, OCTETS)
             w1_pass(LAST, o, w1_values, w1_codes, w1_scales, banks_a, lambda: None)
 
         b = copy_b(LAST, banks_b, raw[LAST, W1_HI])

@@ -216,15 +216,15 @@ def tile_moe_two_glu_relu_kernel(
             for pair in range(2):
                 low = [(0, j, (2 + j) * P) for j in (2 * pair, 2 * pair + 1)]
                 high = [(1, j, (j + 4 * pair) * P) for j in (2 * pair, 2 * pair + 1)]
-                if e == FIRST:
+                if e in WHOLE:
                     first = 6 * pair * P
                     quantize(values[:, PACK * first : PACK * first + 2 * BLOCK], codes, scales, first, first + 2 * P)
                     first_layer(e, banks, codes, scales, high)
                 else:
                     quantize(values[:, pair * PACK * H : (pair + 1) * PACK * H], codes, scales, pair * H, (pair + 1) * H)
                     first_layer(e, banks, codes, scales, low + high)
-                    if pair == 0:
-                        between()
+                if pair == (1 if e >= LAST - 1 else 0):
+                    between()
 
         def w1_pass(e, o, values, codes, scales, banks, between):
             for pair in range(2):
@@ -361,9 +361,13 @@ def tile_moe_two_glu_relu_kernel(
                 quantize(low, codes, scales, 2 * P, 6 * P)
                 first_layer(e, banks_b, codes, scales, [(0, j, (2 + j) * P) for j in range(PACK)])
             else:
-                for pair, engine in enumerate((SCALAR, VECTOR)):
-                    round_pair(e, raw[e, W3_LO], low[:, 2 * pair * BLOCK : 2 * (pair + 1) * BLOCK], pair, engine)
+                for (engine, first), pair in product(((SCALAR, 0), (VECTOR, ROOM_OCTETS)), range(2)):
+                    into = low[:, 2 * pair * BLOCK : 2 * (pair + 1) * BLOCK]
+                    round_pair(e, raw[e, W3_LO], into, pair, engine, first, first + ROOM_OCTETS)
             leave(W3_LO)
+            if e > FIRST and e in WHOLE:
+                quantize(low, codes, scales, 2 * P, 6 * P)
+                first_layer(e, banks_b, codes, scales, [(0, j, (2 + j) * P) for j in range(PACK)])
             w3_high(e, values, codes, scales, banks_b, lambda: leave(W3_HI))
             values, codes, scales = matrices[1]
             for o, piece in enumerate((W1_LO, W1_HI)):
@@ -373,8 +377,12 @@ def tile_moe_two_glu_relu_kernel(
                     round_pair(e, raw[e, piece], part[:, 2 * BLOCK :], 1, SCALAR, 0, 2 * W1_SHARE)
                     round_pair(e, raw[e, piece], part[:, 2 * BLOCK :], 1, VECTOR, 2 * W1_SHARE, OCTETS)
                 else:
-                    for pair in range(2):
-                        round_pair(e, raw[e, piece], part[:, 2 * pair * BLOCK : 2 * (pair + 1) * BLOCK], pair, VECTOR)
+                    round_pair(e, raw[e, piece], part[:, : 2 * BLOCK], 0, VECTOR)
+                    if piece == W1_LO and e in (LAST - 1,):
+                        round_pair(e, raw[e, piece], part[:, 2 * BLOCK :], 1, VECTOR, 0, ROOM_OCTETS)
+                        round_pair(e, raw[e, piece], part[:, 2 * BLOCK :], 1, SCALAR, ROOM_OCTETS, OCTETS)
+                    else:
+                        round_pair(e, raw[e, piece], part[:, 2 * BLOCK :], 1, VECTOR)
                 if piece == W1_HI:
                     b = copy_b(e, banks_b, raw[e, piece])
                 w1_pass(e, o, values, codes, scales, banks_a, lambda: leave(piece))
@@ -434,11 +442,8 @@ def tile_moe_two_glu_relu_kernel(
         for o, piece in enumerate((W1_LO, W1_HI)):
             values = w1_values[:, o * PACK * H : (o + 1) * PACK * H]
             round_pair(LAST, raw[LAST, piece], values[:, : 2 * BLOCK], 0, VECTOR)
-            if piece == W1_LO:
-                round_pair(LAST, raw[LAST, piece], values[:, 2 * BLOCK :], 1, VECTOR)
-            else:
-                round_pair(LAST, raw[LAST, piece], values[:, 2 * BLOCK :], 1, VECTOR, 0, ROOM_OCTETS)
-                round_pair(LAST, raw[LAST, piece], values[:, 2 * BLOCK :], 1, SCALAR, ROOM_OCTETS, OCTETS)
+            round_pair(LAST, raw[LAST, piece], values[:, 2 * BLOCK :], 1, VECTOR, 0, ROOM_OCTETS)
+            round_pair(LAST, raw[LAST, piece], values[:, 2 * BLOCK :], 1, SCALAR, ROOM_OCTETS, OCTETS)
             w1_pass(LAST, o, w1_values, w1_codes, w1_scales, banks_a, lambda: None)
 
         b = copy_b(LAST, banks_b, raw[LAST, W1_HI])

@@ -306,9 +306,11 @@ def tile_moe_two_glu_relu_kernel(
         raw = {}
         for e, piece in product(range(E), range(PIECES)):
             if (e, piece) == (LAST, W2):
-                early_tile = load_blocks(LAST, 0, 2, P)
-                late = rows_of(load_blocks(LAST - 1, BLOCKS - 1, BLOCKS, 0)[:])
-                rest = rows_of(load_blocks(LAST, 2, BLOCKS, 0)[:])
+                early_tile = load_blocks(LAST, 0, 2, 0)
+                late_tile = load_blocks(LAST - 1, BLOCKS - 1, BLOCKS, 0)
+                rest_tile = load_blocks(LAST, 2, BLOCKS, P)
+                late = rows_of(late_tile[:])
+                rest = rows_of(rest_tile[:, : 2 * BLOCK])
                 early = rows_of(early_tile[:, : 2 * BLOCK])
                 continue
             raw[e, piece] = load_piece(e, piece)
@@ -427,8 +429,8 @@ def tile_moe_two_glu_relu_kernel(
         banks_a = [psum_a.tile([P, PACK, HALF], F32, name="bank") for half in range(HALVES)]
         w3_values = bench[:].bitcast(BF16)
         w1_values = rounded.tile([P, PASSES * PACK * H], BF16, name="values_w1", align_bytes=64)
-        spent = w1_values[:, PACK * H :]
-        h = early.rearrange("p k c -> p (k c)")[:, :BLOCK].bitcast(BF16)
+        spent = w1_values[:, : PACK * H]
+        h = own[:]
         back = coded.tile([P, H], U32, name="codes_w2", align_bytes=64)
         back_scales = coded.tile([P, H], U8, name="scales_w2", align_bytes=64)
         front = coded.tile([P, PASSES * H], U32, name="codes_w3", align_bytes=64)
@@ -440,35 +442,56 @@ def tile_moe_two_glu_relu_kernel(
         second_room = rows_of(raw[LAST, W3_HI])[:, 0:1, :C]
         w3_high(LAST, w3_values, front, front_scales, banks_b, lambda: gate_and_scatter(LAST - 1, y[1], [1], second_room))
         for o, piece in enumerate((W1_LO, W1_HI)):
-            values = w1_values[:, o * PACK * H : (o + 1) * PACK * H]
+            values = w1_values[:, (1 - o) * PACK * H : (2 - o) * PACK * H]
             round_pair(LAST, raw[LAST, piece], values[:, : 2 * BLOCK], 0, VECTOR)
-            round_pair(LAST, raw[LAST, piece], values[:, 2 * BLOCK :], 1, VECTOR, 0, ROOM_OCTETS)
-            round_pair(LAST, raw[LAST, piece], values[:, 2 * BLOCK :], 1, SCALAR, ROOM_OCTETS, OCTETS)
-            w1_pass(LAST, o, w1_values, w1_codes, w1_scales, banks_a, lambda: None)
+            cut = ROOM_OCTETS
+            round_pair(LAST, raw[LAST, piece], values[:, 2 * BLOCK :], 1, VECTOR, 0, cut)
+            round_pair(LAST, raw[LAST, piece], values[:, 2 * BLOCK :], 1, SCALAR, cut, OCTETS)
+            for first, end in ((0, 2), (2, 4)) if o == 0 else ((0, 2), (2, 3), (3, 4)):
+                quantize(values[:, first * BLOCK : end * BLOCK], w1_codes, w1_scales, o * H + first * P, o * H + end * P)
+                first_layer(LAST, banks_a, w1_codes, w1_scales, [(o, j, o * H + j * P) for j in range(first, end)])
 
         b = copy_b(LAST, banks_b, raw[LAST, W1_HI])
-        round_columns(early[:, :, P:], spent[:, BLOCK : 2 * BLOCK], VECTOR)
-        round_columns(early[:, :, :P], spent[:, :BLOCK], VECTOR)
-        gate_and_scatter(LAST - 1, third, [2], early_tile[:, 2 * BLOCK - P :].unsqueeze(1))
-        quantize(spent[:, : 2 * BLOCK], codes, scales, 0, 2 * P)
+        gate_and_scatter(LAST - 1, third, [2], spent[:, :BLOCK].bitcast(F32).unsqueeze(1))
+        early_values = spent[:, 2 * BLOCK :]
+        nc.gpsimd.tensor_scalar(
+            early_values.rearrange("p (c k) -> p c k", k=PACK), early.rearrange("p k c -> p c k"), 1.0, 0.0, ALU.mult, ALU.add
+        )
         make_h(LAST, banks_a, b, h)
-        rest_values, late_values = raw[LAST, W1_HI][:, :BLOCK].bitcast(BF16), h[:, :BLOCK]
-        round_columns(rest, rest_values, SCALAR)
+        quantize(early_values[:, :BLOCK], codes, scales, 0, P)
         for half in range(HALVES):
             quantize(h[:, half * BLOCK : (half + 1) * BLOCK], back, back_scales, half * P, (half + 1) * P)
         hidden_now = (back[:, : 2 * P], back_scales[:, : 2 * P])
-        y = [second_layer([(codes, scales, r * P)], *hidden_now) for r in range(2)]
-        round_columns(late, late_values, VECTOR)
-        quantize(late_values, back, back_scales, 2 * P, 3 * P)
-        y_late = second_layer([(back, back_scales, 2 * P)], *old_h)
-        copy_on(VECTOR, last_y[:, 0:1, :], y[0])
-        gate_and_scatter(LAST, y[1], [1], last_y[:, 1:2, :])
-        nc.vector.tensor_tensor(places(LAST, 0), last_y[:, 0, :], gates_of(LAST), ALU.mult)
-        quantize(rest_values, codes, scales, 0, 2 * P)
-        gate_and_scatter(LAST - 1, y_late, [3], last_y[:, 4:5, :])
-        y = [second_layer([(codes, scales, n * P)], *hidden_now) for n in range(2)]
-        nc.vector.tensor_copy(last_y[:, 2:3, :], y[0])
-        gate_and_scatter(LAST, y[1], [3], last_y[:, 3:4, :])
-        nc.vector.tensor_tensor(places(LAST, 2), last_y[:, 2, :], gates_of(LAST), ALU.mult)
+        y = second_layer([(codes, scales, 0)], *hidden_now)
+        tail_values = w1_values[:, 3 * BLOCK : 7 * BLOCK]
+        round_columns(late, tail_values[:, 3 * BLOCK :], SCALAR)
+        round_columns(rest[:, :, P:], tail_values[:, 2 * BLOCK : 3 * BLOCK], VECTOR)
+        round_columns(rest[:, :, :P], tail_values[:, BLOCK : 2 * BLOCK], VECTOR)
+        gate_and_scatter(LAST, y, [0], rest_tile[:, 2 * BLOCK - P :].unsqueeze(1))
+        quantize(tail_values, front, front_scales, 0, 4 * P)
+        y_second = second_layer([(front, front_scales, 0)], *hidden_now)
+        y = second_layer([(front, front_scales, P)], *hidden_now)
+        second = rest_tile[:, :C]
+        copy_on(VECTOR, second.unsqueeze(1), y_second)
+        both = psum_y.tile([P, 2, C], F32, name="bank_y")
+        for n, (h_words, h_bytes) in enumerate((old_h, hidden_now)):
+            nc.tensor.matmul_mx(
+                out=both[:, n, :],
+                lhsT=front[:, (3 - n) * P : (4 - n) * P].bitcast(FP8X4),
+                lhsT_scale=front_scales[:, (3 - n) * P : (4 - n) * P],
+                rhs=h_words.bitcast(FP8X4),
+                rhs_scale=h_bytes,
+                start=True,
+                stop=True,
+            )
+        copy_on(SCALAR, last_y[:, 3:5, :], both[:])
+        gate_and_scatter(LAST, y, [2], last_y[:, 2:3, :])
+        nc.vector.tensor_tensor(places(LAST, 1), second, gates_of(LAST), ALU.mult)
+        nc.vector.tensor_tensor(
+            windows[BLOCKS - 1][:].indirect(dst_sb[:, (LAST - 1) * LIST_COLS :]),
+            last_y[:, 3:5, :].rearrange("p a c -> p (a c)"),
+            gates[:, (LAST - 1) * C :],
+            ALU.mult,
+        )
         for r in range(BLOCKS):
             nc.sync.dma_start(out=out[r * P : (r + 1) * P, :], in_=windows[r][:])

@@ -303,19 +303,17 @@ def tile_moe_two_glu_relu_kernel(
                         out=token_scales[QUADRANT * q : QUADRANT * q + SCALE_ROWS * PASSES, :].bitcast(I32),
                         in_=x_scales[:, SCALE_ROWS * q : SCALE_ROWS * (q + 1), :].bitcast(I32),
                     )
+                nc.sync.dma_start(out=gate_cols[:], in_=gate[0, :].rearrange("(p c) -> p c", c=GATE_COLS))
         raw = {}
         for e, piece in product(range(E), range(PIECES)):
             if (e, piece) == (LAST, W2):
-                early_tile = load_blocks(LAST, 0, 2, 0)
+                early = rows_of(load_blocks(LAST, 0, 1, 0)[:])
+                rest_tile = load_blocks(LAST, 1, BLOCKS, P)
                 late_tile = load_blocks(LAST - 1, BLOCKS - 1, BLOCKS, 0)
-                rest_tile = load_blocks(LAST, 2, BLOCKS, P)
                 late = rows_of(late_tile[:])
-                rest = rows_of(rest_tile[:, : 2 * BLOCK])
-                early = rows_of(early_tile[:, : 2 * BLOCK])
+                rest = rows_of(rest_tile[:, : 3 * BLOCK])
                 continue
             raw[e, piece] = load_piece(e, piece)
-            if (e, piece) == (FIRST, W3_LO):
-                nc.sync.dma_start(out=gate_cols[:], in_=gate[0, :].rearrange("(p c) -> p c", c=GATE_COLS))
             if (e, piece) == (FIRST, W1_HI):
                 nc.sync.dma_start(dst_sb[:], dst)
 
@@ -329,7 +327,7 @@ def tile_moe_two_glu_relu_kernel(
             for n in range(SPREAD):
                 col = SPREAD * group + n
                 nc.tensor.transpose(spread[:, n, :], gate_cols[:, col : col + 1].to_broadcast([P, P]), identity[:])
-            nc.vector.tensor_copy(
+            nc.scalar.copy(
                 out=gates[:].rearrange("p (s c) -> p s c", c=GATE_COLS)[:, :, SPREAD * group : SPREAD * (group + 1)],
                 in_=spread[:].rearrange("p c s -> p s c"),
             )
@@ -453,25 +451,27 @@ def tile_moe_two_glu_relu_kernel(
 
         b = copy_b(LAST, banks_b, raw[LAST, W1_HI])
         gate_and_scatter(LAST - 1, third, [2], spent[:, :BLOCK].bitcast(F32).unsqueeze(1))
-        early_values = spent[:, 2 * BLOCK :]
+        early_values = spent[:, 3 * BLOCK :]
         nc.gpsimd.tensor_scalar(
             early_values.rearrange("p (c k) -> p c k", k=PACK), early.rearrange("p k c -> p c k"), 1.0, 0.0, ALU.mult, ALU.add
         )
         make_h(LAST, banks_a, b, h)
-        quantize(early_values[:, :BLOCK], codes, scales, 0, P)
+        quantize(early_values, codes, scales, 0, P)
         for half in range(HALVES):
             quantize(h[:, half * BLOCK : (half + 1) * BLOCK], back, back_scales, half * P, (half + 1) * P)
         hidden_now = (back[:, : 2 * P], back_scales[:, : 2 * P])
         y = second_layer([(codes, scales, 0)], *hidden_now)
-        tail_values = w1_values[:, 3 * BLOCK : 7 * BLOCK]
-        round_columns(late, tail_values[:, 3 * BLOCK :], SCALAR)
-        round_columns(rest[:, :, P:], tail_values[:, 2 * BLOCK : 3 * BLOCK], VECTOR)
-        round_columns(rest[:, :, :P], tail_values[:, BLOCK : 2 * BLOCK], VECTOR)
-        gate_and_scatter(LAST, y, [0], rest_tile[:, 2 * BLOCK - P :].unsqueeze(1))
-        quantize(tail_values, front, front_scales, 0, 4 * P)
+        tail_values = w1_values[:, 4 * BLOCK :]
+        round_columns(rest[:, :, 2 * P :], tail_values[:, 2 * BLOCK : 3 * BLOCK], VECTOR)
+        round_columns(rest[:, :, :P], tail_values[:, :BLOCK], VECTOR)
+        round_columns(rest[:, :, P : 2 * P], tail_values[:, BLOCK : 2 * BLOCK], SCALAR)
+        gate_and_scatter(LAST, y, [0], rest_tile[:, 3 * BLOCK - P :].unsqueeze(1))
+        quantize(tail_values[:, : 3 * BLOCK], front, front_scales, 0, 3 * P)
         y_second = second_layer([(front, front_scales, 0)], *hidden_now)
         y = second_layer([(front, front_scales, P)], *hidden_now)
-        second = rest_tile[:, :C]
+        round_columns(late, tail_values[:, 3 * BLOCK :], VECTOR)
+        quantize(tail_values[:, 3 * BLOCK :], front, front_scales, 3 * P, 4 * P)
+        second = late_tile[:, :C]
         copy_on(VECTOR, second.unsqueeze(1), y_second)
         both = psum_y.tile([P, 2, C], F32, name="bank_y")
         for n, (h_words, h_bytes) in enumerate((old_h, hidden_now)):
@@ -485,7 +485,7 @@ def tile_moe_two_glu_relu_kernel(
                 stop=True,
             )
         copy_on(SCALAR, last_y[:, 3:5, :], both[:])
-        gate_and_scatter(LAST, y, [2], last_y[:, 2:3, :])
+        gate_and_scatter(LAST, y, [2], late_tile[:, C:].unsqueeze(1))
         nc.vector.tensor_tensor(places(LAST, 1), second, gates_of(LAST), ALU.mult)
         nc.vector.tensor_tensor(
             windows[BLOCKS - 1][:].indirect(dst_sb[:, (LAST - 1) * LIST_COLS :]),

@@ -27,63 +27,21 @@ SCALE_ROWS = 4
 HALF = 128
 HALVES = C // HALF
 BLOCKS = N // P
+BLOCK = P * PACK
+PIECE = PACK * H
 LIST_COLS = C // 16
-PAIR = 2
-OCTET = PACK * PAIR
-OCTETS = H // OCTET
-BLOCK_OCTETS = P // OCTET
 GATE_COLS = SLOTS // P
 SPREAD = 4
 FIRST, LAST = 0, E - 1
-
-W3_LO, W3_HI, W1_LO, W1_HI, W2 = range(5)
-PIECES = 5
-SCALAR, VECTOR, GPSIMD = range(3)
-
-ROOM_OCTETS = C // OCTET
-W1_SHARE = 24
-H_OCTETS = 8
-LEAD = C * PACK // 2 - H_OCTETS * OCTET
-SEATS = [[0], [1], [2, 3]]
-KEPT_BLOCK = BLOCKS - 1
+W3_LO, W3_HI, W1_LO, W1_HI = range(4)
+SCALAR, VECTOR = range(2)
+PAIR = 2
+OCTETS = H // 8
+H_COLUMNS = 64
+LEAD = C * PACK // 2 - H_COLUMNS
+FIRST_SHARE = 192
+LOW_SHARE = 288
 RAW_BUFS = 8
-
-
-BLOCK = P * PACK
-
-
-WHOLE = (FIRST, FIRST + 1)
-
-
-def halves_of(e):
-    return range(HALVES) if e == LAST else range(HALVES - 1, -1, -1)
-
-
-def blocks_ahead(e):
-    return BLOCKS - 1 if e == LAST - 1 else BLOCKS
-
-
-def rounding(e, piece):
-    if piece == W2:
-        end = blocks_ahead(e) * BLOCK_OCTETS
-        if e == FIRST:
-            return [(0, OCTETS // 2, SCALAR), (OCTETS // 2, end - BLOCK_OCTETS, SCALAR), (end - BLOCK_OCTETS, end, GPSIMD)]
-        return [(0, H_OCTETS, VECTOR), (H_OCTETS, end - BLOCK_OCTETS, VECTOR), (end - BLOCK_OCTETS, end, GPSIMD)]
-    if e == FIRST:
-        if piece == W1_HI:
-            return [(0, W1_SHARE, SCALAR), (W1_SHARE, OCTETS, VECTOR)]
-        return [(0, OCTETS, VECTOR if piece == W1_LO else SCALAR)]
-    if piece == W3_LO:
-        return [(0, ROOM_OCTETS, SCALAR), (ROOM_OCTETS, OCTETS, VECTOR)]
-    return [(0, ROOM_OCTETS, VECTOR), (ROOM_OCTETS, OCTETS, VECTOR)]
-
-
-def last_rounding(piece):
-    if piece == W3_LO:
-        return [(0, 2, SCALAR), (2, 4, VECTOR)]
-    if piece == W1_HI:
-        return [(0, 2, VECTOR), (2, 3, VECTOR), (3, 4, SCALAR)]
-    return [(0, 2, VECTOR), (2, 4, VECTOR)]
 
 
 def tile_moe_two_glu_relu_kernel(
@@ -94,10 +52,7 @@ def tile_moe_two_glu_relu_kernel(
     with ExitStack() as ctx:
         keep = ctx.enter_context(tc.tile_pool(name="keep", bufs=1))
         raws = ctx.enter_context(tc.tile_pool(name="raws", bufs=RAW_BUFS))
-        rounded = ctx.enter_context(tc.tile_pool(name="rounded", bufs=2))
-        coded = ctx.enter_context(tc.tile_pool(name="coded", bufs=2))
-        hidden = ctx.enter_context(tc.tile_pool(name="hidden", bufs=2))
-        once = ctx.enter_context(tc.tile_pool(name="once", bufs=1))
+        twice = ctx.enter_context(tc.tile_pool(name="twice", bufs=2))
         psum_a = ctx.enter_context(tc.psum_pool(name="psum_a", bufs=HALVES))
         psum_b = ctx.enter_context(tc.psum_pool(name="psum_b", bufs=HALVES))
         psum_y = ctx.enter_context(tc.psum_pool(name="psum_y", bufs=BLOCKS))
@@ -111,45 +66,13 @@ def tile_moe_two_glu_relu_kernel(
         gate_cols = keep.tile([P, GATE_COLS], F32, name="gate_cols")
         gates = keep.tile([P, SLOTS], F32, name="gates")
         identity = keep.tile([P, P], F32, name="identity")
-        last_y = keep.tile([P, BLOCKS + 1, C], F32, name="last_y")
-        last_b = keep.tile([P, 2 * BLOCK], F32, name="last_b", align_bytes=64)
-        bench = keep.tile([P, 4 * BLOCK], F32, name="bench", align_bytes=64)
         windows = [keep.tile([P, T], F32, name=f"window{r}") for r in range(BLOCKS)]
-        leads = [0 if e == FIRST else LEAD for e in range(LAST)]
-        widths = [blocks_ahead(e) * P for e in range(LAST)]
-        w2_tiles = [
-            keep.tile([P, leads[e] + PACK * widths[e]], F32, name=f"raw_w2_{e}", align_bytes=64) for e in range(LAST)
-        ]
+        b_room = keep.tile([P, HALVES * BLOCK], F32, name="b_room")
+        h_room = keep.tile([P, C * PACK], BF16, name="h_room", align_bytes=64)
+        kept_y = keep.tile([P, 2, C], F32, name="kept_y")
 
         def rows_of(flat):
             return flat.rearrange("p (k c) -> p k c", k=PACK)
-
-        def load_w2(raw, e, first, end):
-            if e in WHOLE:
-                rows = w2[e].rearrange("(g a d b) c -> d g a (b c)", a=2, d=PAIR, b=2)
-                for d in range(PAIR):
-                    nc.sync.dma_start(out=raw.rearrange("p (a r) -> p a r", a=2)[d:P:PAIR], in_=rows[d])
-                return raw
-            rows = w2[e].rearrange("(g j d) c -> d g j c", j=PACK, d=PAIR)
-            for d in range(PAIR):
-                nc.sync.dma_start(out=rows_of(raw)[d:P:PAIR], in_=rows[d][:, :, first:end])
-            return raw
-
-        def load_blocks(e, first, end, spare):
-            words = PACK * (end - first) * P
-            tile = keep.tile([P, words + spare], F32, name=f"raw_w2_{e}_{first}", align_bytes=64)
-            load_w2(tile[:, :words], e, first * P, end * P)
-            return tile
-
-        def load_piece(e, piece):
-            if piece == W2:
-                return load_w2(w2_tiles[e][:, leads[e] :], e, 0, widths[e])
-            tile = raws.tile([P, PACK * H], F32, name="raw", align_bytes=64)
-            w = w3 if piece in (W3_LO, W3_HI) else w1
-            o = piece % PASSES
-            rows = w[e, o * K_PASS : (o + 1) * K_PASS, :]
-            nc.sync.dma_start(out=tile[:], in_=rows.rearrange("(p k) c -> p (k c)", k=PACK))
-            return tile[:]
 
         def copy_on(engine, into, src):
             if engine == SCALAR:
@@ -157,100 +80,91 @@ def tile_moe_two_glu_relu_kernel(
             else:
                 nc.vector.tensor_copy(out=into, in_=src)
 
-        def round_octets(raw, values, piece, first, end, engine):
-            if piece == W2:
-                cols = slice(OCTET * first, OCTET * end)
-                round_columns(rows_of(raw)[:, :, cols], values[:, PACK * cols.start : PACK * cols.stop], engine)
+        def load_piece(e, piece):
+            tile = raws.tile([P, PIECE], F32, name="raw", align_bytes=64)
+            w = w3 if piece in (W3_LO, W3_HI) else w1
+            o = piece % PASSES
+            rows = w[e, o * K_PASS : (o + 1) * K_PASS, :]
+            nc.sync.dma_start(out=tile[:], in_=rows.rearrange("(p k) c -> p (k c)", k=PACK))
+            return tile[:]
+
+        def load_w2(e, first, end, lead, spare, by_rows):
+            words = PACK * (end - first) * P
+            tile = keep.tile([P, lead + words + spare], F32, name=f"raw_w2_{e}_{first}", align_bytes=64)
+            rows = rows_of(tile[:, lead : lead + words])
+            cols = slice(first * P, end * P)
+            if e < LAST:
+                nc.sync.dma_start(out=rows, in_=w2[e].rearrange("(p k) c -> p k c", k=PACK)[:, :, cols])
+            elif by_rows:
+                for j in range(PACK):
+                    nc.sync.dma_start(out=rows[:, j, :], in_=w2[e].rearrange("(g j d) c -> j g d c", j=PACK, d=PAIR)[j][:, :, cols])
             else:
-                src = raw.rearrange("p (k g j d) -> p g j k d", k=PACK, j=PACK, d=PAIR)
-                into = values.rearrange("p (j g d k) -> p g j k d", j=PACK, d=PAIR, k=PACK)
-                copy_on(engine, into[:, first:end], src[:, first:end])
+                for d in range(PAIR):
+                    nc.sync.dma_start(out=rows[d:P:PAIR], in_=w2[e].rearrange("(g j d) c -> d g j c", j=PACK, d=PAIR)[d][:, :, cols])
+            return tile, rows
 
-        def round_groups(raw, values, first, end, engine):
-            src = raw.rearrange("p (k g j d) -> p g k j d", k=PACK, j=PACK, d=PAIR)
-            into = values.rearrange("p (j g d k) -> p g k j d", j=PACK, d=PAIR, k=PACK)
-            copy_on(engine, into[:, :, :, first:end], src[:, :, :, first:end])
+        def round_range(raw, values, first, end, engine):
+            src = raw.rearrange("p (k m j) -> p m k j", k=PACK, j=PACK)
+            into = values.rearrange("p (j m k) -> p m k j", j=PACK, k=PACK)
+            copy_on(engine, into[:, first // PACK : end // PACK], src[:, first // PACK : end // PACK])
 
-        def round_columns(raw, values, engine):
-            src = raw.rearrange("p k (c d) -> p c k d", d=PACK)
-            copy_on(engine, values.rearrange("p (c d k) -> p c k d", d=PACK, k=PACK), src)
-
-        def round_on_gpsimd(raw, into, first, end):
-            src = raw.rearrange("p (k c) -> p c k", k=PACK)[:, OCTET * first : OCTET * end]
-            nc.gpsimd.tensor_scalar(into.rearrange("p (c k) -> p c k", k=PACK), src, 1.0, 0.0, ALU.mult, ALU.add)
-
-        def new_matrix(name, passes):
-            values = rounded.tile([P, passes * PACK * H], BF16, name=f"values_{name}", align_bytes=64)
-            codes = coded.tile([P, passes * H], U32, name=f"codes_{name}", align_bytes=64)
-            scales = coded.tile([P, passes * H], U8, name=f"scales_{name}", align_bytes=64)
-            return values, codes, scales
-
-        def quantize(values, codes, scales, first, end):
-            nc.vector.quantize_mx(out=codes[:, first:end].bitcast(FP8X4), scales=scales[:, first:end], in_=values)
-
-        def first_layer(e, banks, codes, scales, parts):
-            for half, (o, j, first) in product(halves_of(e), parts):
-                slots = slice(e * C + half * HALF, e * C + (half + 1) * HALF)
-                nc.tensor.matmul_mx(
-                    out=banks[half][:, j, :],
-                    lhsT=codes[:, first : first + P].bitcast(FP8X4),
-                    lhsT_scale=scales[:, first : first + P],
-                    rhs=slot_words[o][:, slots].bitcast(FP8X4),
-                    rhs_scale=slot_scales[SCALE_ROWS * o :, slots],
-                    start=(o == 0 and j == 0),
-                    stop=(o == PASSES - 1 and j == PACK - 1),
-                )
-
-        def round_pair(e, raw, into, pair, engine, first=0, end=OCTETS):
-            if e in WHOLE:
-                src = raw.rearrange("p (k g a d b) -> p a g k d b", k=PACK, a=2, d=PAIR, b=2)[:, pair]
-                into = into.rearrange("p (b g d k) -> p g k d b", b=2, d=PAIR, k=PACK)
-            else:
-                src = raw.rearrange("p (k g a b d) -> p a g k b d", k=PACK, a=2, d=PAIR, b=2)[:, pair]
-                into = into.rearrange("p (b g d k) -> p g k b d", b=2, d=PAIR, k=PACK)
+        def round_pair(raw, values, pair, engine, first=0, end=OCTETS):
+            src = raw.rearrange("p (k g a b d) -> p a g k b d", k=PACK, a=2, d=PAIR, b=2)[:, pair]
+            into = values[:, 2 * pair * BLOCK : 2 * (pair + 1) * BLOCK].rearrange("p (b g d k) -> p g k b d", b=2, d=PAIR, k=PACK)
             copy_on(engine, into[:, first:end], src[:, first:end])
 
-        def w3_high(e, values, codes, scales, banks, between):
-            for pair in range(2):
-                round_pair(e, raw[e, W3_HI], values[:, 6 * pair * BLOCK : (6 * pair + 2) * BLOCK], pair, SCALAR if e == FIRST else VECTOR)
-            for pair in range(2):
-                low = [(0, j, (2 + j) * P) for j in (2 * pair, 2 * pair + 1)]
-                high = [(1, j, (j + 4 * pair) * P) for j in (2 * pair, 2 * pair + 1)]
-                if e in WHOLE:
-                    first = 6 * pair * P
-                    quantize(values[:, PACK * first : PACK * first + 2 * BLOCK], codes, scales, first, first + 2 * P)
-                    first_layer(e, banks, codes, scales, high)
-                else:
-                    quantize(values[:, pair * PACK * H : (pair + 1) * PACK * H], codes, scales, pair * H, (pair + 1) * H)
-                    first_layer(e, banks, codes, scales, low + high)
-                if pair == (1 if e >= LAST - 1 else 0):
-                    between()
+        def round_columns(rows, values, engine):
+            src = rows.rearrange("p k (c d) -> p c k d", d=PACK)
+            copy_on(engine, values.rearrange("p (c d k) -> p c k d", d=PACK, k=PACK), src)
 
-        def w1_pass(e, o, values, codes, scales, banks, between):
-            for pair in range(2):
-                words = o * H + 2 * pair * P, o * H + 2 * (pair + 1) * P
-                quantize(values[:, PACK * words[0] : PACK * words[1]], codes, scales, *words)
-                first_layer(e, banks, codes, scales, [(o, j, o * H + j * P) for j in (2 * pair, 2 * pair + 1)])
-                if pair == 0:
-                    between()
+        def round_on_gpsimd(rows, values):
+            nc.gpsimd.tensor_scalar(
+                values.rearrange("p (c k) -> p c k", k=PACK), rows.rearrange("p k c -> p c k"), 1.0, 0.0, ALU.mult, ALU.add
+            )
 
-        def copy_b(e, banks, raw):
-            b = {}
-            for half in halves_of(e):
-                if e == FIRST and half == HALVES - 1:
-                    room = rows_of(raw)[:, :, :HALF]
-                elif e == LAST:
-                    room = rows_of(raw[:, half * BLOCK : (half + 1) * BLOCK])
-                elif e == LAST - 1:
-                    room = rows_of(bench[:, (half + 1) * BLOCK : (half + 2) * BLOCK])
-                else:
-                    room = rows_of(last_b[:, half * BLOCK : (half + 1) * BLOCK])
-                b[half] = room.rearrange("p a (s j) -> p a s j", j=PACK)
-                nc.scalar.copy(out=b[half], in_=banks[half][:].rearrange("p j (a s) -> p a s j", a=PACK))
+        def new_codes(name, words):
+            codes = twice.tile([P, words], U32, name=f"codes_{name}", align_bytes=64)
+            scales = twice.tile([P, words], U8, name=f"scales_{name}", align_bytes=64)
+            return codes, scales
+
+        def quantize(values, coded, first):
+            codes, scales = coded
+            end = first + values.shape[1] // PACK
+            nc.vector.quantize_mx(out=codes[:, first:end].bitcast(FP8X4), scales=scales[:, first:end], in_=values)
+
+        def matmul(into, left, first, right_words, right_scales, start, stop):
+            codes, scales = left
+            nc.tensor.matmul_mx(
+                out=into,
+                lhsT=codes[:, first : first + P].bitcast(FP8X4),
+                lhsT_scale=scales[:, first : first + P],
+                rhs=right_words.bitcast(FP8X4),
+                rhs_scale=right_scales,
+                start=start,
+                stop=stop,
+            )
+
+        def multiply_groups(e, o, values, coded, banks, first, end):
+            quantize(values[:, first * BLOCK : end * BLOCK], coded, o * H + first * P)
+            for half, j in product(range(HALVES), range(first, end)):
+                slots = slice(e * C + half * HALF, e * C + (half + 1) * HALF)
+                matmul(
+                    banks[half][:, j, :],
+                    coded,
+                    o * H + j * P,
+                    slot_words[o][:, slots],
+                    slot_scales[SCALE_ROWS * o :, slots],
+                    o == 0 and j == 0,
+                    o == PASSES - 1 and j == PACK - 1,
+                )
+
+        def copy_b(bank, room):
+            b = room.rearrange("p a (s j) -> p a s j", j=PACK)
+            nc.scalar.copy(out=b, in_=bank[:].rearrange("p j (a s) -> p a s j", a=PACK))
             return b
 
-        def make_h(e, banks_a, b, h):
-            for half in halves_of(e):
+        def make_h(banks_a, b, h, halves):
+            for half in halves:
                 nc.vector.scalar_tensor_tensor(
                     out=h[:, half * H : (half + 1) * H].rearrange("p (a s j) -> p a s j", a=PACK, j=PACK),
                     in0=banks_a[half][:].rearrange("p j (a s) -> p a s j", a=PACK),
@@ -260,33 +174,15 @@ def tile_moe_two_glu_relu_kernel(
                     op1=ALU.mult,
                 )
 
-        def quantize_h(h, calls):
-            codes = hidden.tile([P, C], U32, name="h_codes", align_bytes=64)
-            scales = hidden.tile([P, C], U8, name="h_scales", align_bytes=64)
-            for call in reversed(range(calls)):
-                first, end = call * C // calls, (call + 1) * C // calls
-                quantize(h[:, PACK * first : PACK * end], codes, scales, first, end)
-            return codes, scales
-
-        def second_layer(blocks, h_codes, h_scales):
+        def second_layer(parts):
             bank = psum_y.tile([P, 2, C], F32, name="bank_y")
-            for n, (codes, scales, first) in enumerate(blocks):
-                nc.tensor.matmul_mx(
-                    out=bank[:, n, :],
-                    lhsT=codes[:, first : first + P].bitcast(FP8X4),
-                    lhsT_scale=scales[:, first : first + P],
-                    rhs=h_codes.bitcast(FP8X4),
-                    rhs_scale=h_scales,
-                    start=True,
-                    stop=True,
-                )
-            return bank[:, : len(blocks), :]
+            for n, (coded, first, hidden) in enumerate(parts):
+                matmul(bank[:, n, :], coded, first, hidden[0][:, :C], hidden[1][:, :C], True, True)
+            return [bank[:, n, :] for n in range(len(parts))], bank
 
-        def gates_of(e):
-            return gates[:, e * C : (e + 1) * C]
-
-        def places(e, r):
-            return windows[r][:].indirect(dst_sb[:, e * LIST_COLS : (e + 1) * LIST_COLS])
+        def gate_and_scatter(e, r, y, room):
+            nc.vector.tensor_tensor(room, y, gates[:, e * C : (e + 1) * C], ALU.mult)
+            nc.scalar.activation(windows[r][:].indirect(dst_sb[:, e * LIST_COLS : (e + 1) * LIST_COLS]), room, COPY)
 
         nc.vector.memset(token_scales[:].bitcast(I32), 0)
         nc.vector.memset(windows[0][:], 0.0)
@@ -304,18 +200,17 @@ def tile_moe_two_glu_relu_kernel(
                         in_=x_scales[:, SCALE_ROWS * q : SCALE_ROWS * (q + 1), :].bitcast(I32),
                     )
                 nc.sync.dma_start(out=gate_cols[:], in_=gate[0, :].rearrange("(p c) -> p c", c=GATE_COLS))
-        raw = {}
-        for e, piece in product(range(E), range(PIECES)):
-            if (e, piece) == (LAST, W2):
-                early = rows_of(load_blocks(LAST, 0, 1, 0)[:])
-                rest_tile = load_blocks(LAST, 1, BLOCKS, P)
-                late_tile = load_blocks(LAST - 1, BLOCKS - 1, BLOCKS, 0)
-                late = rows_of(late_tile[:])
-                rest = rows_of(rest_tile[:, : 3 * BLOCK])
-                continue
-            raw[e, piece] = load_piece(e, piece)
-            if (e, piece) == (FIRST, W1_HI):
+        raw, raw_w2 = {}, {}
+        for e in range(E):
+            for piece in range(4):
+                raw[e, piece] = load_piece(e, piece)
+            if e == FIRST:
                 nc.sync.dma_start(dst_sb[:], dst)
+            if e < LAST:
+                raw_w2[e] = load_w2(e, 0, BLOCKS - (e == LAST - 1), LEAD * (e > FIRST), 0, False)
+        early_tile, early = load_w2(LAST, 0, 1, 0, 0, False)
+        rest_tile, rest = load_w2(LAST, 1, BLOCKS, 0, P, True)
+        late_tile, late = load_w2(LAST - 1, BLOCKS - 1, BLOCKS, 0, 0, False)
 
         for o in range(PASSES):
             nc.vector.tensor_copy(slot_words[o][:], token_words[o][:].bitcast(U32).indirect(offs_sb[:]))
@@ -332,164 +227,122 @@ def tile_moe_two_glu_relu_kernel(
                 in_=spread[:].rearrange("p c s -> p s c"),
             )
 
-        def gate_and_scatter(e, y, blocks, room):
-            spread_gates = gates_of(e).unsqueeze(1).to_broadcast([P, len(blocks), C])
-            nc.vector.tensor_tensor(room, y, spread_gates, ALU.mult)
-            for n, r in enumerate(blocks):
-                nc.scalar.activation(places(e, r), room[:, n, :], COPY)
-
         y = []
         for e in range(LAST):
-            matrices = [new_matrix("w3", PASSES), new_matrix("w1", PASSES), new_matrix("w2", 1)]
             banks_b = [psum_b.tile([P, PACK, HALF], F32, name="bank") for half in range(HALVES)]
             banks_a = [psum_a.tile([P, PACK, HALF], F32, name="bank") for half in range(HALVES)]
-            if leads[e] == 0:
-                own = once.tile([P, C * PACK], BF16, name="h", align_bytes=64)
-                h = own[:]
-            else:
-                h = w2_tiles[e][:, : C * PACK // 2].bitcast(BF16)
-
-            def leave(piece):
-                if e > FIRST:
-                    gate_and_scatter(e - 1, y[piece], [piece], rows_of(raw[e, piece])[:, 0:1, :C])
-
-            values, codes, scales = matrices[0]
-            low = values[:, 2 * BLOCK : 6 * BLOCK]
-            if e == FIRST:
-                for pair in range(2):
-                    round_pair(e, raw[e, W3_LO], low[:, 2 * pair * BLOCK : 2 * (pair + 1) * BLOCK], pair, SCALAR)
-                quantize(low, codes, scales, 2 * P, 6 * P)
-                first_layer(e, banks_b, codes, scales, [(0, j, (2 + j) * P) for j in range(PACK)])
-            else:
-                for (engine, first), pair in product(((SCALAR, 0), (VECTOR, ROOM_OCTETS)), range(2)):
-                    into = low[:, 2 * pair * BLOCK : 2 * (pair + 1) * BLOCK]
-                    round_pair(e, raw[e, W3_LO], into, pair, engine, first, first + ROOM_OCTETS)
-            leave(W3_LO)
-            if e > FIRST and e in WHOLE:
-                quantize(low, codes, scales, 2 * P, 6 * P)
-                first_layer(e, banks_b, codes, scales, [(0, j, (2 + j) * P) for j in range(PACK)])
-            w3_high(e, values, codes, scales, banks_b, lambda: leave(W3_HI))
-            values, codes, scales = matrices[1]
-            for o, piece in enumerate((W1_LO, W1_HI)):
-                part = values[:, o * PACK * H : (o + 1) * PACK * H]
-                if (e, piece) == (FIRST, W1_HI):
-                    round_pair(e, raw[e, piece], part[:, : 2 * BLOCK], 0, VECTOR)
-                    round_pair(e, raw[e, piece], part[:, 2 * BLOCK :], 1, SCALAR, 0, 2 * W1_SHARE)
-                    round_pair(e, raw[e, piece], part[:, 2 * BLOCK :], 1, VECTOR, 2 * W1_SHARE, OCTETS)
+            for piece in range(4):
+                o = piece % PASSES
+                if o == 0:
+                    matrix = twice.tile([P, PASSES * PIECE], BF16, name=f"values{piece}", align_bytes=64)
+                    coded = new_codes(piece, PASSES * H)
+                values = matrix[:, o * PIECE : (o + 1) * PIECE]
+                if e == FIRST:
+                    cut = {W3_LO: H, W3_HI: H, W1_LO: 0, W1_HI: FIRST_SHARE}[piece]
+                    parts = [(0, cut, SCALAR), (cut, H, VECTOR)]
+                elif piece == W3_LO:
+                    parts = [(0, LOW_SHARE, SCALAR), (LOW_SHARE, H, VECTOR)]
                 else:
-                    round_pair(e, raw[e, piece], part[:, : 2 * BLOCK], 0, VECTOR)
-                    if piece == W1_LO and e in (LAST - 1,):
-                        round_pair(e, raw[e, piece], part[:, 2 * BLOCK :], 1, VECTOR, 0, ROOM_OCTETS)
-                        round_pair(e, raw[e, piece], part[:, 2 * BLOCK :], 1, SCALAR, ROOM_OCTETS, OCTETS)
-                    else:
-                        round_pair(e, raw[e, piece], part[:, 2 * BLOCK :], 1, VECTOR)
-                if piece == W1_HI:
-                    b = copy_b(e, banks_b, raw[e, piece])
-                w1_pass(e, o, values, codes, scales, banks_a, lambda: leave(piece))
+                    parts = [(0, C, VECTOR), (C, H, VECTOR)]
+                for first, end, engine in parts:
+                    if first < end:
+                        round_range(raw[e, piece], values, first, end, engine)
+                if e > FIRST:
+                    gate_and_scatter(e - 1, piece, y[piece], raw[e, piece][:, :C])
+                for first, end in ((0, 2), (2, 4)) if piece == W1_HI else ((0, 4),):
+                    multiply_groups(e, o, values, coded, banks_b if piece < W1_LO else banks_a, first, end)
+                if piece == (W1_HI if e == FIRST else W3_HI):
+                    rooms = [rows_of(b_room[:, half * BLOCK : (half + 1) * BLOCK]) for half in range(HALVES)]
+                    if e == FIRST:
+                        rooms[1] = rows_of(raw[e, piece])[:, :, :HALF]
+                    b = [copy_b(banks_b[half], rooms[half]) for half in range(HALVES)]
 
-            values, codes, scales = matrices[W2 // PASSES]
-            parts = rounding(e, W2)
-            shift = 0
+            tile, rows = raw_w2[e]
+            width = rows.shape[2]
+            cut = width - P
+            values = twice.tile([P, PIECE], BF16, name="values_w2", align_bytes=64)
+            coded = new_codes("w2", N)
+            hidden = new_codes("h", C)
             if e == FIRST:
-                make_h(e, banks_a, b, h)
-                h_codes, h_scales = quantize_h(h, HALVES)
-                aside = matrices[1][0][:, 7 * BLOCK :]
-                round_on_gpsimd(raw[e, W2], aside, parts[-1][0], parts[-1][1])
-                for first, end, engine in parts[:-1]:
-                    round_octets(raw[e, W2], values[:], W2, first, end, engine)
-                for first, end, engine in parts[:-1]:
-                    first, end = OCTET * first, OCTET * end
-                    quantize(values[:, PACK * first : PACK * end], codes, scales, first, end)
-                quantize(aside, codes, scales, N - P, N)
+                make_h(banks_a, b, h_room[:], (1, 0))
+                for half in (1, 0):
+                    quantize(h_room[:, half * BLOCK : (half + 1) * BLOCK], hidden, half * P)
+                aside = matrix[:, 7 * BLOCK :]
+                round_on_gpsimd(rows[:, :, cut:], aside)
+                for first, end in ((0, C), (C, cut)):
+                    round_columns(rows[:, :, first:end], values[:, PACK * first : PACK * end], SCALAR)
+                for first, end in ((0, C), (C, cut)):
+                    quantize(values[:, PACK * first : PACK * end], coded, first)
             else:
-                start = widths[e]
-                aside = raw[e, W2][:, start : start + P * PACK // 2].bitcast(BF16)
-                for first, end, engine in parts[:-1]:
-                    round_octets(raw[e, W2], values[:, : PACK * widths[e]], W2, first, end, engine)
-                make_h(e, banks_a, b, h)
-                round_on_gpsimd(raw[e, W2], aside, parts[-1][0], parts[-1][1])
-                cut = widths[e] - P
-                quantize(values[:, : PACK * cut], codes, scales, shift, shift + cut)
-                h_codes, h_scales = quantize_h(h, 1)
-                quantize(aside, codes, scales, shift + cut, shift + cut + P)
-            blocks = [(codes, scales, shift + r * P) for r in range(blocks_ahead(e))]
-            if e < LAST - 1:
-                y = [second_layer(blocks[r : r + 1], h_codes[:], h_scales[:]) for r in range(2)]
-                both = second_layer(blocks[2:], h_codes[:], h_scales[:])
-                y = y + [both[:, n : n + 1, :] for n in range(2)]
+                h = tile[:, : C * PACK // 2].bitcast(BF16)
+                aside = tile[:, LEAD + width : LEAD + width + BLOCK // 2].bitcast(BF16)
+                for first, end, engine in ((0, H_COLUMNS, VECTOR), (H_COLUMNS, C, VECTOR), (C, cut, SCALAR)):
+                    if first < end:
+                        round_columns(rows[:, :, first:end], values[:, PACK * first : PACK * end], engine)
+                make_h(banks_a, b, h, (1, 0))
+                round_on_gpsimd(rows[:, :, cut:], aside)
+                quantize(values[:, : PACK * cut], coded, 0)
+                quantize(h, hidden, 0)
+            quantize(aside, coded, cut)
+            y = [second_layer([(coded, r * P, hidden)])[0][0] for r in range(2)]
+            y = y + second_layer([(coded, r * P, hidden) for r in range(2, width // P)])[0]
 
-        y = [second_layer(blocks[r : r + 1], h_codes[:], h_scales[:]) for r in range(BLOCKS - 1)]
-        third = y[2]
-        gate_and_scatter(LAST - 1, y[0], [0], last_y[:, 0:1, :])
-        old_h = (h_codes[:], h_scales[:])
-
+        third_hidden, w2_coded = hidden, coded
         banks_b = [psum_b.tile([P, PACK, HALF], F32, name="bank") for half in range(HALVES)]
         banks_a = [psum_a.tile([P, PACK, HALF], F32, name="bank") for half in range(HALVES)]
-        w3_values = bench[:].bitcast(BF16)
-        w1_values = rounded.tile([P, PASSES * PACK * H], BF16, name="values_w1", align_bytes=64)
-        spent = w1_values[:, : PACK * H]
-        h = own[:]
-        back = coded.tile([P, H], U32, name="codes_w2", align_bytes=64)
-        back_scales = coded.tile([P, H], U8, name="scales_w2", align_bytes=64)
-        front = coded.tile([P, PASSES * H], U32, name="codes_w3", align_bytes=64)
-        front_scales = coded.tile([P, PASSES * H], U8, name="scales_w3", align_bytes=64)
-        w1_codes = coded.tile([P, PASSES * H], U32, name="codes_w1", align_bytes=64)
-        w1_scales = coded.tile([P, PASSES * H], U8, name="scales_w1", align_bytes=64)
-        for first, end, engine in last_rounding(W3_LO):
-            round_groups(raw[LAST, W3_LO], w3_values[:, 2 * BLOCK : 6 * BLOCK], first, end, engine)
-        second_room = rows_of(raw[LAST, W3_HI])[:, 0:1, :C]
-        w3_high(LAST, w3_values, front, front_scales, banks_b, lambda: gate_and_scatter(LAST - 1, y[1], [1], second_room))
-        for o, piece in enumerate((W1_LO, W1_HI)):
-            values = w1_values[:, (1 - o) * PACK * H : (2 - o) * PACK * H]
-            round_pair(LAST, raw[LAST, piece], values[:, : 2 * BLOCK], 0, VECTOR)
-            cut = ROOM_OCTETS
-            round_pair(LAST, raw[LAST, piece], values[:, 2 * BLOCK :], 1, VECTOR, 0, cut)
-            round_pair(LAST, raw[LAST, piece], values[:, 2 * BLOCK :], 1, SCALAR, cut, OCTETS)
-            for first, end in ((0, 2), (2, 4)) if o == 0 else ((0, 2), (2, 3), (3, 4)):
-                quantize(values[:, first * BLOCK : end * BLOCK], w1_codes, w1_scales, o * H + first * P, o * H + end * P)
-                first_layer(LAST, banks_a, w1_codes, w1_scales, [(o, j, o * H + j * P) for j in range(first, end)])
+        w3_values = twice.tile([P, PASSES * PIECE], BF16, name=f"values{W3_LO}", align_bytes=64)
+        w3_coded = new_codes(W3_LO, PASSES * H)
+        for (engine, first), pair in product(((SCALAR, 0), (VECTOR, OCTETS // 2)), range(2)):
+            round_pair(raw[LAST, W3_LO], w3_values[:, :PIECE], pair, engine, first, first + OCTETS // 2)
+        gate_and_scatter(LAST - 1, 0, y[0], raw[LAST, W3_LO][:, :C])
+        multiply_groups(LAST, 0, w3_values[:, :PIECE], w3_coded, banks_b, 0, 4)
+        for pair in range(2):
+            round_pair(raw[LAST, W3_HI], w3_values[:, PIECE:], pair, VECTOR)
+        multiply_groups(LAST, 1, w3_values[:, PIECE:], w3_coded, banks_b, 0, 2)
+        gate_and_scatter(LAST - 1, 1, y[1], raw[LAST, W3_HI][:, :C])
+        multiply_groups(LAST, 1, w3_values[:, PIECE:], w3_coded, banks_b, 2, 4)
 
-        b = copy_b(LAST, banks_b, raw[LAST, W1_HI])
-        gate_and_scatter(LAST - 1, third, [2], spent[:, :BLOCK].bitcast(F32).unsqueeze(1))
-        early_values = spent[:, 3 * BLOCK :]
-        nc.gpsimd.tensor_scalar(
-            early_values.rearrange("p (c k) -> p c k", k=PACK), early.rearrange("p k c -> p c k"), 1.0, 0.0, ALU.mult, ALU.add
-        )
-        make_h(LAST, banks_a, b, h)
-        quantize(early_values, codes, scales, 0, P)
+        w1_values = twice.tile([P, PASSES * PIECE], BF16, name=f"values{W1_LO}", align_bytes=64)
+        w1_coded = new_codes(W1_LO, PASSES * H)
+        low, high = w1_values[:, PIECE:], w1_values[:, :PIECE]
+        for pair in range(2):
+            round_pair(raw[LAST, W1_LO], low, pair, VECTOR)
+        for pair in range(2):
+            multiply_groups(LAST, 0, low, w1_coded, banks_a, 2 * pair, 2 * pair + 2)
+        round_pair(raw[LAST, W1_HI], high, 0, VECTOR)
+        round_pair(raw[LAST, W1_HI], high, 1, VECTOR, 0, OCTETS // 2)
+        round_pair(raw[LAST, W1_HI], high, 1, SCALAR, OCTETS // 2, OCTETS)
+        for first, end in ((0, 2), (2, 3), (3, 4)):
+            multiply_groups(LAST, 1, high, w1_coded, banks_a, first, end)
+        rooms = [b_room[:, :BLOCK], raw[LAST, W1_HI][:, BLOCK : 2 * BLOCK]]
+        b = [copy_b(banks_b[half], rows_of(rooms[half])) for half in range(HALVES)]
+
+        gate_and_scatter(LAST - 1, 2, y[2], high[:, :BLOCK].bitcast(F32))
+        round_on_gpsimd(early, high[:, 3 * BLOCK :])
+        make_h(banks_a, b, h_room[:], (0, 1))
+        quantize(high[:, 3 * BLOCK :], w2_coded, 0)
+        hidden = new_codes("h", C)
+        first_bank = psum_y.tile([P, 2, C], F32, name="bank_y")
         for half in range(HALVES):
-            quantize(h[:, half * BLOCK : (half + 1) * BLOCK], back, back_scales, half * P, (half + 1) * P)
-        hidden_now = (back[:, : 2 * P], back_scales[:, : 2 * P])
-        y = second_layer([(codes, scales, 0)], *hidden_now)
-        tail_values = w1_values[:, 4 * BLOCK :]
-        round_columns(rest[:, :, 2 * P :], tail_values[:, 2 * BLOCK : 3 * BLOCK], VECTOR)
-        round_columns(rest[:, :, :P], tail_values[:, :BLOCK], VECTOR)
-        round_columns(rest[:, :, P : 2 * P], tail_values[:, BLOCK : 2 * BLOCK], SCALAR)
-        gate_and_scatter(LAST, y, [0], rest_tile[:, 3 * BLOCK - P :].unsqueeze(1))
-        quantize(tail_values[:, : 3 * BLOCK], front, front_scales, 0, 3 * P)
-        y_second = second_layer([(front, front_scales, 0)], *hidden_now)
-        y = second_layer([(front, front_scales, P)], *hidden_now)
-        round_columns(late, tail_values[:, 3 * BLOCK :], VECTOR)
-        quantize(tail_values[:, 3 * BLOCK :], front, front_scales, 3 * P, 4 * P)
-        second = late_tile[:, :C]
-        copy_on(VECTOR, second.unsqueeze(1), y_second)
-        both = psum_y.tile([P, 2, C], F32, name="bank_y")
-        for n, (h_words, h_bytes) in enumerate((old_h, hidden_now)):
-            nc.tensor.matmul_mx(
-                out=both[:, n, :],
-                lhsT=front[:, (3 - n) * P : (4 - n) * P].bitcast(FP8X4),
-                lhsT_scale=front_scales[:, (3 - n) * P : (4 - n) * P],
-                rhs=h_words.bitcast(FP8X4),
-                rhs_scale=h_bytes,
-                start=True,
-                stop=True,
-            )
-        copy_on(SCALAR, last_y[:, 3:5, :], both[:])
-        gate_and_scatter(LAST, y, [2], late_tile[:, C:].unsqueeze(1))
-        nc.vector.tensor_tensor(places(LAST, 1), second, gates_of(LAST), ALU.mult)
+            quantize(h_room[:, half * BLOCK : (half + 1) * BLOCK], hidden, half * P)
+        for half in range(HALVES):
+            slots = slice(half * HALF, (half + 1) * HALF)
+            matmul(first_bank[:, 0, slots], w2_coded, 0, hidden[0][:, slots], hidden[1][:, slots], True, True)
+        round_columns(rest[:, :, 2 * P :], low[:, 2 * BLOCK : 3 * BLOCK], VECTOR)
+        round_columns(rest[:, :, :P], low[:, :BLOCK], VECTOR)
+        round_columns(rest[:, :, P : 2 * P], low[:, BLOCK : 2 * BLOCK], SCALAR)
+        gate_and_scatter(LAST, 0, first_bank[:, 0, :], rest_tile[:, 3 * BLOCK - P :])
+        quantize(low[:, : 3 * BLOCK], w3_coded, 0)
+        y = [second_layer([(w3_coded, n * P, hidden)])[0][0] for n in range(2)]
+        round_columns(late, low[:, 3 * BLOCK :], VECTOR)
+        quantize(low[:, 3 * BLOCK :], w3_coded, 3 * P)
+        gate_and_scatter(LAST, 1, y[0], late_tile[:, :C])
+        both = second_layer([(w3_coded, 3 * P, third_hidden), (w3_coded, 2 * P, hidden)])[1]
+        gate_and_scatter(LAST, 2, y[1], late_tile[:, C:])
+        nc.vector.tensor_copy(kept_y[:], both[:])
         nc.vector.tensor_tensor(
             windows[BLOCKS - 1][:].indirect(dst_sb[:, (LAST - 1) * LIST_COLS :]),
-            last_y[:, 3:5, :].rearrange("p a c -> p (a c)"),
+            kept_y[:].rearrange("p a c -> p (a c)"),
             gates[:, (LAST - 1) * C :],
             ALU.mult,
         )

@@ -37,10 +37,9 @@ W3_LO, W3_HI, W1_LO, W1_HI = range(4)
 SCALAR, VECTOR = range(2)
 PAIR = 2
 OCTETS = H // 8
-H_COLUMNS = 64
-LEAD = C * PACK // 2 - H_COLUMNS
-FIRST_SHARE = 192
-LOW_SHARE = 288
+WHOLE = (FIRST, FIRST + 1)
+FIRST_SHARE = 48
+LOW_SHARE = 36
 RAW_BUFS = 8
 
 
@@ -93,24 +92,28 @@ def tile_moe_two_glu_relu_kernel(
             tile = keep.tile([P, lead + words + spare], F32, name=f"raw_w2_{e}_{first}", align_bytes=64)
             rows = rows_of(tile[:, lead : lead + words])
             cols = slice(first * P, end * P)
-            if e < LAST:
-                nc.sync.dma_start(out=rows, in_=w2[e].rearrange("(p k) c -> p k c", k=PACK)[:, :, cols])
-            elif by_rows:
-                for j in range(PACK):
-                    nc.sync.dma_start(out=rows[:, j, :], in_=w2[e].rearrange("(g j d) c -> j g d c", j=PACK, d=PAIR)[j][:, :, cols])
-            else:
+            if e in WHOLE:
+                src = w2[e].rearrange("(g a d b) c -> d g a (b c)", a=2, d=PAIR, b=2)
                 for d in range(PAIR):
-                    nc.sync.dma_start(out=rows[d:P:PAIR], in_=w2[e].rearrange("(g j d) c -> d g j c", j=PACK, d=PAIR)[d][:, :, cols])
+                    nc.sync.dma_start(out=rows.rearrange("p (a b) c -> p a (b c)", a=2)[d:P:PAIR], in_=src[d])
+            elif by_rows:
+                src = w2[e].rearrange("(g j d) c -> j g d c", j=PACK, d=PAIR)
+                for j in range(PACK):
+                    nc.sync.dma_start(out=rows[:, j, :], in_=src[j][:, :, cols])
+            else:
+                src = w2[e].rearrange("(g j d) c -> d g j c", j=PACK, d=PAIR)
+                for d in range(PAIR):
+                    nc.sync.dma_start(out=rows[d:P:PAIR], in_=src[d][:, :, cols])
             return tile, rows
 
-        def round_range(raw, values, first, end, engine):
-            src = raw.rearrange("p (k m j) -> p m k j", k=PACK, j=PACK)
-            into = values.rearrange("p (j m k) -> p m k j", j=PACK, k=PACK)
-            copy_on(engine, into[:, first // PACK : end // PACK], src[:, first // PACK : end // PACK])
-
-        def round_pair(raw, values, pair, engine, first=0, end=OCTETS):
-            src = raw.rearrange("p (k g a b d) -> p a g k b d", k=PACK, a=2, d=PAIR, b=2)[:, pair]
-            into = values[:, 2 * pair * BLOCK : 2 * (pair + 1) * BLOCK].rearrange("p (b g d k) -> p g k b d", b=2, d=PAIR, k=PACK)
+        def round_pair(e, piece, values, pair, engine, first=0, end=OCTETS):
+            into = values[:, 2 * pair * BLOCK : 2 * (pair + 1) * BLOCK]
+            if e in WHOLE:
+                src = raw[e, piece].rearrange("p (k g a d b) -> p a g k d b", k=PACK, a=2, d=PAIR, b=2)[:, pair]
+                into = into.rearrange("p (b g d k) -> p g k d b", b=2, d=PAIR, k=PACK)
+            else:
+                src = raw[e, piece].rearrange("p (k g a b d) -> p a g k b d", k=PACK, a=2, d=PAIR, b=2)[:, pair]
+                into = into.rearrange("p (b g d k) -> p g k b d", b=2, d=PAIR, k=PACK)
             copy_on(engine, into[:, first:end], src[:, first:end])
 
         def round_columns(rows, values, engine):
@@ -163,16 +166,15 @@ def tile_moe_two_glu_relu_kernel(
             nc.scalar.copy(out=b, in_=bank[:].rearrange("p j (a s) -> p a s j", a=PACK))
             return b
 
-        def make_h(banks_a, b, h, halves):
-            for half in halves:
-                nc.vector.scalar_tensor_tensor(
-                    out=h[:, half * H : (half + 1) * H].rearrange("p (a s j) -> p a s j", a=PACK, j=PACK),
-                    in0=banks_a[half][:].rearrange("p j (a s) -> p a s j", a=PACK),
-                    scalar=0.0,
-                    in1=b[half],
-                    op0=ALU.max,
-                    op1=ALU.mult,
-                )
+        def make_h(banks_a, b, h, half):
+            nc.vector.scalar_tensor_tensor(
+                out=h.rearrange("p (a s j) -> p a s j", a=PACK, j=PACK),
+                in0=banks_a[half][:].rearrange("p j (a s) -> p a s j", a=PACK),
+                scalar=0.0,
+                in1=b[half],
+                op0=ALU.max,
+                op1=ALU.mult,
+            )
 
         def second_layer(parts):
             bank = psum_y.tile([P, 2, C], F32, name="bank_y")
@@ -207,10 +209,12 @@ def tile_moe_two_glu_relu_kernel(
             if e == FIRST:
                 nc.sync.dma_start(dst_sb[:], dst)
             if e < LAST:
-                raw_w2[e] = load_w2(e, 0, BLOCKS - (e == LAST - 1), LEAD * (e > FIRST), 0, False)
-        early_tile, early = load_w2(LAST, 0, 1, 0, 0, False)
+                blocks = BLOCKS - (e == LAST - 1)
+                lead = (BLOCK // 2 - (blocks - 2) * P // 2) * (e > FIRST)
+                raw_w2[e] = load_w2(e, 0, blocks, lead, lead, False)
+        early_tile, early = load_w2(LAST, 0, 1, 0, 0, True)
         rest_tile, rest = load_w2(LAST, 1, BLOCKS, 0, P, True)
-        late_tile, late = load_w2(LAST - 1, BLOCKS - 1, BLOCKS, 0, 0, False)
+        late_tile, late = load_w2(LAST - 1, BLOCKS - 1, BLOCKS, 0, 0, True)
 
         for o in range(PASSES):
             nc.vector.tensor_copy(slot_words[o][:], token_words[o][:].bitcast(U32).indirect(offs_sb[:]))
@@ -237,24 +241,25 @@ def tile_moe_two_glu_relu_kernel(
                     matrix = twice.tile([P, PASSES * PIECE], BF16, name=f"values{piece}", align_bytes=64)
                     coded = new_codes(piece, PASSES * H)
                 values = matrix[:, o * PIECE : (o + 1) * PIECE]
-                if e == FIRST:
-                    cut = {W3_LO: H, W3_HI: H, W1_LO: 0, W1_HI: FIRST_SHARE}[piece]
-                    parts = [(0, cut, SCALAR), (cut, H, VECTOR)]
-                elif piece == W3_LO:
-                    parts = [(0, LOW_SHARE, SCALAR), (LOW_SHARE, H, VECTOR)]
+                banks = banks_b if piece < W1_LO else banks_a
+                if (e, piece) == (FIRST, W1_HI):
+                    parts = [(0, VECTOR, 0, OCTETS), (1, SCALAR, 0, FIRST_SHARE), (1, VECTOR, FIRST_SHARE, OCTETS)]
+                elif e > FIRST and piece == W3_LO:
+                    parts = [(pair, SCALAR, 0, LOW_SHARE) for pair in range(2)]
+                    parts = parts + [(pair, VECTOR, LOW_SHARE, OCTETS) for pair in range(2)]
                 else:
-                    parts = [(0, C, VECTOR), (C, H, VECTOR)]
-                for first, end, engine in parts:
-                    if first < end:
-                        round_range(raw[e, piece], values, first, end, engine)
+                    parts = [(pair, SCALAR if e == FIRST and piece < W1_LO else VECTOR, 0, OCTETS) for pair in range(2)]
+                for part in parts:
+                    round_pair(e, piece, values, *part)
+                if piece != W3_LO:
+                    multiply_groups(e, o, values, coded, banks, 0, 2)
                 if e > FIRST:
                     gate_and_scatter(e - 1, piece, y[piece], raw[e, piece][:, :C])
-                for first, end in ((0, 2), (2, 4)) if piece == W1_HI else ((0, 4),):
-                    multiply_groups(e, o, values, coded, banks_b if piece < W1_LO else banks_a, first, end)
+                multiply_groups(e, o, values, coded, banks, 2 * (piece != W3_LO), 4)
                 if piece == (W1_HI if e == FIRST else W3_HI):
                     rooms = [rows_of(b_room[:, half * BLOCK : (half + 1) * BLOCK]) for half in range(HALVES)]
                     if e == FIRST:
-                        rooms[1] = rows_of(raw[e, piece])[:, :, :HALF]
+                        rooms[0] = rows_of(raw[e, piece])[:, :, :HALF]
                     b = [copy_b(banks_b[half], rooms[half]) for half in range(HALVES)]
 
             tile, rows = raw_w2[e]
@@ -264,8 +269,9 @@ def tile_moe_two_glu_relu_kernel(
             coded = new_codes("w2", N)
             hidden = new_codes("h", C)
             if e == FIRST:
-                make_h(banks_a, b, h_room[:], (1, 0))
-                for half in (1, 0):
+                for half in range(HALVES):
+                    make_h(banks_a, b, h_room[:, half * BLOCK : (half + 1) * BLOCK], half)
+                for half in range(HALVES):
                     quantize(h_room[:, half * BLOCK : (half + 1) * BLOCK], hidden, half * P)
                 aside = matrix[:, 7 * BLOCK :]
                 round_on_gpsimd(rows[:, :, cut:], aside)
@@ -274,18 +280,29 @@ def tile_moe_two_glu_relu_kernel(
                 for first, end in ((0, C), (C, cut)):
                     quantize(values[:, PACK * first : PACK * end], coded, first)
             else:
-                h = tile[:, : C * PACK // 2].bitcast(BF16)
-                aside = tile[:, LEAD + width : LEAD + width + BLOCK // 2].bitcast(BF16)
-                for first, end, engine in ((0, H_COLUMNS, VECTOR), (H_COLUMNS, C, VECTOR), (C, cut, SCALAR)):
-                    if first < end:
-                        round_columns(rows[:, :, first:end], values[:, PACK * first : PACK * end], engine)
-                make_h(banks_a, b, h, (1, 0))
-                round_on_gpsimd(rows[:, :, cut:], aside)
+                words = tile.shape[1]
+                h = [tile[:, words - BLOCK // 2 :].bitcast(BF16), tile[:, : BLOCK // 2].bitcast(BF16)]
+                edge = (width - 2 * P) // 2
+                start = BLOCK // 2 - edge + (width if e in WHOLE else cut)
+                aside = tile[:, start : start + BLOCK // 2].bitcast(BF16)
+                src = rows.rearrange("p k (r c d) -> p r c k d", c=edge // PACK, d=PACK)
+                into = values[:, : PACK * cut].rearrange("p (r c d k) -> p r c k d", c=edge // PACK, d=PACK, k=PACK)
+                runs, skipped = cut // edge, P // edge
+                nc.vector.tensor_copy(out=into[:, :: runs - 1], in_=src[:, :: runs - 1 + skipped])
+                if e in WHOLE:
+                    nc.vector.tensor_copy(out=into[:, 1], in_=src[:, 1])
+                else:
+                    nc.vector.tensor_copy(out=into[:, 1:3], in_=src[:, 1 : 2 + skipped + 1 : 1 + skipped])
+                for half in range(HALVES):
+                    make_h(banks_a, b, h[half], half)
+                round_on_gpsimd(rows[:, :, cut - P : cut], aside)
                 quantize(values[:, : PACK * cut], coded, 0)
-                quantize(h, hidden, 0)
+                for half in range(HALVES):
+                    quantize(h[half], hidden, half * P)
             quantize(aside, coded, cut)
-            y = [second_layer([(coded, r * P, hidden)])[0][0] for r in range(2)]
-            y = y + second_layer([(coded, r * P, hidden) for r in range(2, width // P)])[0]
+            seats = list(range(width // P)) if e == FIRST else list(range(width // P - 2)) + [width // P - 1, width // P - 2]
+            y = [second_layer([(coded, n * P, hidden)])[0][0] for n in seats[:2]]
+            y = y + second_layer([(coded, n * P, hidden) for n in seats[2:]])[0]
 
         third_hidden, w2_coded = hidden, coded
         banks_b = [psum_b.tile([P, PACK, HALF], F32, name="bank") for half in range(HALVES)]
@@ -293,11 +310,11 @@ def tile_moe_two_glu_relu_kernel(
         w3_values = twice.tile([P, PASSES * PIECE], BF16, name=f"values{W3_LO}", align_bytes=64)
         w3_coded = new_codes(W3_LO, PASSES * H)
         for (engine, first), pair in product(((SCALAR, 0), (VECTOR, OCTETS // 2)), range(2)):
-            round_pair(raw[LAST, W3_LO], w3_values[:, :PIECE], pair, engine, first, first + OCTETS // 2)
+            round_pair(LAST, W3_LO, w3_values[:, :PIECE], pair, engine, first, first + OCTETS // 2)
         gate_and_scatter(LAST - 1, 0, y[0], raw[LAST, W3_LO][:, :C])
         multiply_groups(LAST, 0, w3_values[:, :PIECE], w3_coded, banks_b, 0, 4)
         for pair in range(2):
-            round_pair(raw[LAST, W3_HI], w3_values[:, PIECE:], pair, VECTOR)
+            round_pair(LAST, W3_HI, w3_values[:, PIECE:], pair, VECTOR)
         multiply_groups(LAST, 1, w3_values[:, PIECE:], w3_coded, banks_b, 0, 2)
         gate_and_scatter(LAST - 1, 1, y[1], raw[LAST, W3_HI][:, :C])
         multiply_groups(LAST, 1, w3_values[:, PIECE:], w3_coded, banks_b, 2, 4)
@@ -306,12 +323,12 @@ def tile_moe_two_glu_relu_kernel(
         w1_coded = new_codes(W1_LO, PASSES * H)
         low, high = w1_values[:, PIECE:], w1_values[:, :PIECE]
         for pair in range(2):
-            round_pair(raw[LAST, W1_LO], low, pair, VECTOR)
+            round_pair(LAST, W1_LO, low, pair, VECTOR)
         for pair in range(2):
             multiply_groups(LAST, 0, low, w1_coded, banks_a, 2 * pair, 2 * pair + 2)
-        round_pair(raw[LAST, W1_HI], high, 0, VECTOR)
-        round_pair(raw[LAST, W1_HI], high, 1, VECTOR, 0, OCTETS // 2)
-        round_pair(raw[LAST, W1_HI], high, 1, SCALAR, OCTETS // 2, OCTETS)
+        round_pair(LAST, W1_HI, high, 0, VECTOR)
+        round_pair(LAST, W1_HI, high, 1, VECTOR, 0, OCTETS // 2)
+        round_pair(LAST, W1_HI, high, 1, SCALAR, OCTETS // 2, OCTETS)
         for first, end in ((0, 2), (2, 3), (3, 4)):
             multiply_groups(LAST, 1, high, w1_coded, banks_a, first, end)
         rooms = [b_room[:, :BLOCK], raw[LAST, W1_HI][:, BLOCK : 2 * BLOCK]]
@@ -319,7 +336,8 @@ def tile_moe_two_glu_relu_kernel(
 
         gate_and_scatter(LAST - 1, 2, y[2], high[:, :BLOCK].bitcast(F32))
         round_on_gpsimd(early, high[:, 3 * BLOCK :])
-        make_h(banks_a, b, h_room[:], (0, 1))
+        for half in range(HALVES):
+            make_h(banks_a, b, h_room[:, half * BLOCK : (half + 1) * BLOCK], half)
         quantize(high[:, 3 * BLOCK :], w2_coded, 0)
         hidden = new_codes("h", C)
         first_bank = psum_y.tile([P, 2, C], F32, name="bank_y")

from contextlib import ExitStack
from itertools import product

import concourse.mybir as mybir
from concourse.masks import make_identity

K, T, E, C, H, N = 1024, 1536, 4, 256, 512, 512
SLOTS = E * C
FLOPS = 2 * SLOTS * (2 * K * H + H * N)

F32 = mybir.dt.float32
BF16 = mybir.dt.bfloat16
I32 = mybir.dt.int32
U32 = mybir.dt.uint32
U16 = mybir.dt.uint16
U8 = mybir.dt.uint8
FP8X4 = mybir.dt.float8_e4m3fn_x4
ALU = mybir.AluOpType
COPY = mybir.ActivationFunctionType.Copy

P = 128
PACK = 4
K_PASS = P * PACK
PASSES = K // K_PASS
QUADRANT = 32
SCALE_ROWS = 4
HALF = 128
HALVES = C // HALF
BLOCKS = N // P
BLOCK = P * PACK
PIECE = PACK * H
LIST_COLS = C // 16
GATE_COLS = SLOTS // P
SPREAD = 4
FIRST, LAST = 0, E - 1
W3_LO, W3_HI, W1_LO, W1_HI = range(4)
SCALAR, VECTOR = range(2)
PAIR = 2
OCTETS = H // 8
WHOLE = (FIRST, FIRST + 1)
FIRST_SHARE = 48
LOW_SHARE = 36
RAW_BUFS = 8


def tile_moe_two_glu_relu_kernel(
    tc, x_words, x_scales, w1, w3, w2, gate, offs, dst, out
):
    nc = tc.nc

    with ExitStack() as ctx:
        keep = ctx.enter_context(tc.tile_pool(name="keep", bufs=1))
        raws = ctx.enter_context(tc.tile_pool(name="raws", bufs=RAW_BUFS))
        twice = ctx.enter_context(tc.tile_pool(name="twice", bufs=2))
        psum_a = ctx.enter_context(tc.psum_pool(name="psum_a", bufs=HALVES))
        psum_b = ctx.enter_context(tc.psum_pool(name="psum_b", bufs=HALVES))
        psum_y = ctx.enter_context(tc.psum_pool(name="psum_y", bufs=BLOCKS))

        offs_sb = keep.tile([P, SLOTS // 16], U16, name="offs_sb")
        dst_sb = keep.tile([P, SLOTS // 16], U16, name="dst_sb")
        token_words = [keep.tile([P, T], I32, name=f"token_words{o}") for o in range(PASSES)]
        token_scales = keep.tile([P, T], U8, name="token_scales")
        slot_words = [keep.tile([P, SLOTS], U32, name=f"slot_words{o}", align_bytes=64) for o in range(PASSES)]
        slot_scales = keep.tile([P, SLOTS], U8, name="slot_scales", align_bytes=64)
        gate_cols = keep.tile([P, GATE_COLS], F32, name="gate_cols")
        gates = keep.tile([P, SLOTS], F32, name="gates")
        identity = keep.tile([P, P], F32, name="identity")
        windows = [keep.tile([P, T], F32, name=f"window{r}") for r in range(BLOCKS)]
        b_room = keep.tile([P, HALVES * BLOCK], F32, name="b_room")
        h_room = keep.tile([P, C * PACK], BF16, name="h_room", align_bytes=64)
        kept_y = keep.tile([P, 2, C], F32, name="kept_y")

        def rows_of(flat):
            return flat.rearrange("p (k c) -> p k c", k=PACK)

        def copy_on(engine, into, src):
            if engine == SCALAR:
                nc.scalar.copy(out=into, in_=src)
            else:
                nc.vector.tensor_copy(out=into, in_=src)

        def load_piece(e, piece):
            tile = raws.tile([P, PIECE], F32, name="raw", align_bytes=64)
            w = w3 if piece in (W3_LO, W3_HI) else w1
            o = piece % PASSES
            rows = w[e, o * K_PASS : (o + 1) * K_PASS, :]
            nc.sync.dma_start(out=tile[:], in_=rows.rearrange("(p k) c -> p (k c)", k=PACK))
            return tile[:]

        def load_w2(e, first, end, lead, spare, by_rows):
            words = PACK * (end - first) * P
            tile = keep.tile([P, lead + words + spare], F32, name=f"raw_w2_{e}_{first}", align_bytes=64)
            rows = rows_of(tile[:, lead : lead + words])
            cols = slice(first * P, end * P)
            if e in WHOLE:
                src = w2[e].rearrange("(g a d b) c -> d g a (b c)", a=2, d=PAIR, b=2)
                for d in range(PAIR):
                    nc.sync.dma_start(out=rows.rearrange("p (a b) c -> p a (b c)", a=2)[d:P:PAIR], in_=src[d])
            elif by_rows:
                src = w2[e].rearrange("(g j d) c -> j g d c", j=PACK, d=PAIR)
                for j in range(PACK):
                    nc.sync.dma_start(out=rows[:, j, :], in_=src[j][:, :, cols])
            else:
                src = w2[e].rearrange("(g j d) c -> d g j c", j=PACK, d=PAIR)
                for d in range(PAIR):
                    nc.sync.dma_start(out=rows[d:P:PAIR], in_=src[d][:, :, cols])
            return tile, rows

        def round_pair(e, piece, values, pair, engine, first=0, end=OCTETS):
            into = values[:, 2 * pair * BLOCK : 2 * (pair + 1) * BLOCK]
            if e in WHOLE:
                src = raw[e, piece].rearrange("p (k g a d b) -> p a g k d b", k=PACK, a=2, d=PAIR, b=2)[:, pair]
                into = into.rearrange("p (b g d k) -> p g k d b", b=2, d=PAIR, k=PACK)
            else:
                src = raw[e, piece].rearrange("p (k g a b d) -> p a g k b d", k=PACK, a=2, d=PAIR, b=2)[:, pair]
                into = into.rearrange("p (b g d k) -> p g k b d", b=2, d=PAIR, k=PACK)
            copy_on(engine, into[:, first:end], src[:, first:end])

        def round_columns(rows, values, engine):
            src = rows.rearrange("p k (c d) -> p c k d", d=PACK)
            copy_on(engine, values.rearrange("p (c d k) -> p c k d", d=PACK, k=PACK), src)

        def round_on_gpsimd(rows, values):
            nc.gpsimd.tensor_scalar(
                values.rearrange("p (c k) -> p c k", k=PACK), rows.rearrange("p k c -> p c k"), 1.0, 0.0, ALU.mult, ALU.add
            )

        def new_codes(name, words):
            codes = twice.tile([P, words], U32, name=f"codes_{name}", align_bytes=64)
            scales = twice.tile([P, words], U8, name=f"scales_{name}", align_bytes=64)
            return codes, scales

        def quantize(values, coded, first):
            codes, scales = coded
            end = first + values.shape[1] // PACK
            nc.vector.quantize_mx(out=codes[:, first:end].bitcast(FP8X4), scales=scales[:, first:end], in_=values)

        def matmul(into, left, first, right_words, right_scales, start, stop):
            codes, scales = left
            nc.tensor.matmul_mx(
                out=into,
                lhsT=codes[:, first : first + P].bitcast(FP8X4),
                lhsT_scale=scales[:, first : first + P],
                rhs=right_words.bitcast(FP8X4),
                rhs_scale=right_scales,
                start=start,
                stop=stop,
            )

        def multiply_groups(e, o, values, coded, banks, first, end):
            quantize(values[:, first * BLOCK : end * BLOCK], coded, o * H + first * P)
            for half, j in product(range(HALVES), range(first, end)):
                slots = slice(e * C + half * HALF, e * C + (half + 1) * HALF)
                matmul(
                    banks[half][:, j, :],
                    coded,
                    o * H + j * P,
                    slot_words[o][:, slots],
                    slot_scales[SCALE_ROWS * o :, slots],
                    o == 0 and j == 0,
                    o == PASSES - 1 and j == PACK - 1,
                )

        def copy_b(bank, room):
            b = room.rearrange("p a (s j) -> p a s j", j=PACK)
            nc.scalar.copy(out=b, in_=bank[:].rearrange("p j (a s) -> p a s j", a=PACK))
            return b

        def make_h(banks_a, b, h, half):
            nc.vector.scalar_tensor_tensor(
                out=h.rearrange("p (a s j) -> p a s j", a=PACK, j=PACK),
                in0=banks_a[half][:].rearrange("p j (a s) -> p a s j", a=PACK),
                scalar=0.0,
                in1=b[half],
                op0=ALU.max,
                op1=ALU.mult,
            )

        def second_layer(parts):
            bank = psum_y.tile([P, 2, C], F32, name="bank_y")
            for n, (coded, first, hidden) in enumerate(parts):
                matmul(bank[:, n, :], coded, first, hidden[0][:, :C], hidden[1][:, :C], True, True)
            return [bank[:, n, :] for n in range(len(parts))], bank

        def gate_and_scatter(e, r, y, room):
            nc.vector.tensor_tensor(room, y, gates[:, e * C : (e + 1) * C], ALU.mult)
            nc.scalar.activation(windows[r][:].indirect(dst_sb[:, e * LIST_COLS : (e + 1) * LIST_COLS]), room, COPY)

        nc.vector.memset(token_scales[:].bitcast(I32), 0)
        nc.vector.memset(windows[0][:], 0.0)
        for r in range(1, BLOCKS):
            nc.scalar.copy(out=windows[r][:], in_=windows[0][:])
        make_identity(nc, identity[:])

        for o in range(PASSES):
            nc.sync.dma_start(out=token_words[o][:], in_=x_words[o].rearrange("p t r -> p (t r)").bitcast(I32))
            if o == 0:
                nc.sync.dma_start(offs_sb[:], offs)
                for q in range(P // QUADRANT):
                    nc.sync.dma_start(
                        out=token_scales[QUADRANT * q : QUADRANT * q + SCALE_ROWS * PASSES, :].bitcast(I32),
                        in_=x_scales[:, SCALE_ROWS * q : SCALE_ROWS * (q + 1), :].bitcast(I32),
                    )
                nc.sync.dma_start(out=gate_cols[:], in_=gate[0, :].rearrange("(p c) -> p c", c=GATE_COLS))
        raw, raw_w2 = {}, {}
        for e in range(E):
            for piece in range(4):
                raw[e, piece] = load_piece(e, piece)
            if e == FIRST:
                nc.sync.dma_start(dst_sb[:], dst)
            if e < LAST:
                blocks = BLOCKS - (e == LAST - 1)
                lead = (BLOCK // 2 - (blocks - 2) * P // 2) * (e > FIRST)
                raw_w2[e] = load_w2(e, 0, blocks, lead, lead, False)
        early_tile, early = load_w2(LAST, 0, 1, 0, 0, True)
        rest_tile, rest = load_w2(LAST, 1, BLOCKS, 0, P, True)
        late_tile, late = load_w2(LAST - 1, BLOCKS - 1, BLOCKS, 0, 0, True)

        for o in range(PASSES):
            nc.vector.tensor_copy(slot_words[o][:], token_words[o][:].bitcast(U32).indirect(offs_sb[:]))
            if o == 0:
                nc.vector.tensor_copy(slot_scales[:], token_scales[:].indirect(offs_sb[:]))

        for group in range(GATE_COLS // SPREAD):
            spread = psum_y.tile([P, SPREAD, P], F32, name="bank_y")
            for n in range(SPREAD):
                col = SPREAD * group + n
                nc.tensor.transpose(spread[:, n, :], gate_cols[:, col : col + 1].to_broadcast([P, P]), identity[:])
            nc.scalar.copy(
                out=gates[:].rearrange("p (s c) -> p s c", c=GATE_COLS)[:, :, SPREAD * group : SPREAD * (group + 1)],
                in_=spread[:].rearrange("p c s -> p s c"),
            )

        y = []
        for e in range(LAST):
            banks_b = [psum_b.tile([P, PACK, HALF], F32, name="bank") for half in range(HALVES)]
            banks_a = [psum_a.tile([P, PACK, HALF], F32, name="bank") for half in range(HALVES)]
            for piece in range(4):
                o = piece % PASSES
                if o == 0:
                    matrix = twice.tile([P, PASSES * PIECE], BF16, name=f"values{piece}", align_bytes=64)
                    coded = new_codes(piece, PASSES * H)
                values = matrix[:, o * PIECE : (o + 1) * PIECE]
                banks = banks_b if piece < W1_LO else banks_a
                if (e, piece) == (FIRST, W1_HI):
                    parts = [(0, VECTOR, 0, OCTETS), (1, SCALAR, 0, FIRST_SHARE), (1, VECTOR, FIRST_SHARE, OCTETS)]
                elif e > FIRST and piece == W3_LO:
                    parts = [(pair, SCALAR, 0, LOW_SHARE) for pair in range(2)]
                    parts = parts + [(pair, VECTOR, LOW_SHARE, OCTETS) for pair in range(2)]
                else:
                    parts = [(pair, SCALAR if e == FIRST and piece < W1_LO else VECTOR, 0, OCTETS) for pair in range(2)]
                for part in parts:
                    round_pair(e, piece, values, *part)
                if piece != W3_LO:
                    multiply_groups(e, o, values, coded, banks, 0, 2)
                if e > FIRST:
                    gate_and_scatter(e - 1, piece, y[piece], raw[e, piece][:, :C])
                multiply_groups(e, o, values, coded, banks, 2 * (piece != W3_LO), 4)
                if piece == (W1_HI if e == FIRST else W3_HI):
                    rooms = [rows_of(b_room[:, half * BLOCK : (half + 1) * BLOCK]) for half in range(HALVES)]
                    if e == FIRST:
                        rooms[0] = rows_of(raw[e, piece])[:, :, :HALF]
                    b = [copy_b(banks_b[half], rooms[half]) for half in range(HALVES)]

            tile, rows = raw_w2[e]
            width = rows.shape[2]
            cut = width - P
            values = twice.tile([P, PIECE], BF16, name="values_w2", align_bytes=64)
            coded = new_codes("w2", N)
            hidden = new_codes("h", C)
            if e == FIRST:
                for half in range(HALVES):
                    make_h(banks_a, b, h_room[:, half * BLOCK : (half + 1) * BLOCK], half)
                for half in range(HALVES):
                    quantize(h_room[:, half * BLOCK : (half + 1) * BLOCK], hidden, half * P)
                aside = matrix[:, 7 * BLOCK :]
                round_on_gpsimd(rows[:, :, cut:], aside)
                for first, end in ((0, C), (C, cut)):
                    round_columns(rows[:, :, first:end], values[:, PACK * first : PACK * end], SCALAR)
                for first, end in ((0, C), (C, cut)):
                    quantize(values[:, PACK * first : PACK * end], coded, first)
            else:
                words = tile.shape[1]
                h = [tile[:, words - BLOCK // 2 :].bitcast(BF16), tile[:, : BLOCK // 2].bitcast(BF16)]
                edge = (width - 2 * P) // 2
                start = BLOCK // 2 - edge + (width if e in WHOLE else cut)
                aside = tile[:, start : start + BLOCK // 2].bitcast(BF16)
                src = rows.rearrange("p k (r c d) -> p r c k d", c=edge // PACK, d=PACK)
                into = values[:, : PACK * cut].rearrange("p (r c d k) -> p r c k d", c=edge // PACK, d=PACK, k=PACK)
                runs, skipped = cut // edge, P // edge
                nc.vector.tensor_copy(out=into[:, :: runs - 1], in_=src[:, :: runs - 1 + skipped])
                if e in WHOLE:
                    nc.vector.tensor_copy(out=into[:, 1], in_=src[:, 1])
                else:
                    nc.vector.tensor_copy(out=into[:, 1:3], in_=src[:, 1 : 2 + skipped + 1 : 1 + skipped])
                for half in range(HALVES):
                    make_h(banks_a, b, h[half], half)
                round_on_gpsimd(rows[:, :, cut - P : cut], aside)
                quantize(values[:, : PACK * cut], coded, 0)
                for half in range(HALVES):
                    quantize(h[half], hidden, half * P)
            quantize(aside, coded, cut)
            seats = list(range(width // P)) if e == FIRST else list(range(width // P - 2)) + [width // P - 1, width // P - 2]
            y = [second_layer([(coded, n * P, hidden)])[0][0] for n in seats[:2]]
            y = y + second_layer([(coded, n * P, hidden) for n in seats[2:]])[0]

        third_hidden, w2_coded = hidden, coded
        banks_b = [psum_b.tile([P, PACK, HALF], F32, name="bank") for half in range(HALVES)]
        banks_a = [psum_a.tile([P, PACK, HALF], F32, name="bank") for half in range(HALVES)]
        w3_values = twice.tile([P, PASSES * PIECE], BF16, name=f"values{W3_LO}", align_bytes=64)
        w3_coded = new_codes(W3_LO, PASSES * H)
        for (engine, first), pair in product(((SCALAR, 0), (VECTOR, OCTETS // 2)), range(2)):
            round_pair(LAST, W3_LO, w3_values[:, :PIECE], pair, engine, first, first + OCTETS // 2)
        gate_and_scatter(LAST - 1, 0, y[0], raw[LAST, W3_LO][:, :C])
        multiply_groups(LAST, 0, w3_values[:, :PIECE], w3_coded, banks_b, 0, 4)
        for pair in range(2):
            round_pair(LAST, W3_HI, w3_values[:, PIECE:], pair, VECTOR)
        multiply_groups(LAST, 1, w3_values[:, PIECE:], w3_coded, banks_b, 0, 2)
        gate_and_scatter(LAST - 1, 1, y[1], raw[LAST, W3_HI][:, :C])
        multiply_groups(LAST, 1, w3_values[:, PIECE:], w3_coded, banks_b, 2, 4)

        w1_values = twice.tile([P, PASSES * PIECE], BF16, name=f"values{W1_LO}", align_bytes=64)
        w1_coded = new_codes(W1_LO, PASSES * H)
        low, high = w1_values[:, PIECE:], w1_values[:, :PIECE]
        for pair in range(2):
            round_pair(LAST, W1_LO, low, pair, VECTOR)
        for pair in range(2):
            multiply_groups(LAST, 0, low, w1_coded, banks_a, 2 * pair, 2 * pair + 2)
        round_pair(LAST, W1_HI, high, 0, VECTOR)
        round_pair(LAST, W1_HI, high, 1, VECTOR, 0, OCTETS // 2)
        round_pair(LAST, W1_HI, high, 1, SCALAR, OCTETS // 2, OCTETS)
        for first, end in ((0, 2), (2, 3), (3, 4)):
            multiply_groups(LAST, 1, high, w1_coded, banks_a, first, end)
        rooms = [b_room[:, :BLOCK], raw[LAST, W1_HI][:, BLOCK : 2 * BLOCK]]
        b = [copy_b(banks_b[half], rows_of(rooms[half])) for half in range(HALVES)]

        gate_and_scatter(LAST - 1, 2, y[2], high[:, :BLOCK].bitcast(F32))
        round_on_gpsimd(early, high[:, 3 * BLOCK :])
        for half in range(HALVES):
            make_h(banks_a, b, h_room[:, half * BLOCK : (half + 1) * BLOCK], half)
        quantize(high[:, 3 * BLOCK :], w2_coded, 0)
        hidden = new_codes("h", C)
        first_bank = psum_y.tile([P, 2, C], F32, name="bank_y")
        for half in range(HALVES):
            quantize(h_room[:, half * BLOCK : (half + 1) * BLOCK], hidden, half * P)
        for half in range(HALVES):
            slots = slice(half * HALF, (half + 1) * HALF)
            matmul(first_bank[:, 0, slots], w2_coded, 0, hidden[0][:, slots], hidden[1][:, slots], True, True)
        round_columns(rest[:, :, 2 * P :], low[:, 2 * BLOCK : 3 * BLOCK], VECTOR)
        round_columns(rest[:, :, :P], low[:, :BLOCK], VECTOR)
        round_columns(rest[:, :, P : 2 * P], low[:, BLOCK : 2 * BLOCK], SCALAR)
        gate_and_scatter(LAST, 0, first_bank[:, 0, :], rest_tile[:, 3 * BLOCK - P :])
        quantize(low[:, : 3 * BLOCK], w3_coded, 0)
        y = [second_layer([(w3_coded, n * P, hidden)])[0][0] for n in range(2)]
        round_columns(late, low[:, 3 * BLOCK :], VECTOR)
        quantize(low[:, 3 * BLOCK :], w3_coded, 3 * P)
        gate_and_scatter(LAST, 1, y[0], late_tile[:, :C])
        both = second_layer([(w3_coded, 3 * P, third_hidden), (w3_coded, 2 * P, hidden)])[1]
        gate_and_scatter(LAST, 2, y[1], late_tile[:, C:])
        nc.vector.tensor_copy(kept_y[:], both[:])
        nc.vector.tensor_tensor(
            windows[BLOCKS - 1][:].indirect(dst_sb[:, (LAST - 1) * LIST_COLS :]),
            kept_y[:].rearrange("p a c -> p (a c)"),
            gates[:, (LAST - 1) * C :],
            ALU.mult,
        )
        for r in range(BLOCKS):
            nc.sync.dma_start(out=out[r * P : (r + 1) * P, :], in_=windows[r][:])
